import numpy as np, ml_dtypes
CORES = [13,21,141,149]
N = 4
BF = ml_dtypes.bfloat16
def gentries(a):
    return np.ascontiguousarray(a.reshape(8, 16, -1).transpose(0, 2, 1)).reshape(8, -1)
def gtable(e):
    e = np.asarray(e); return np.ascontiguousarray(e.reshape(8, -1, 16).transpose(0, 2, 1)).reshape(128, -1).astype(np.int32)
B, L, S, T, TH = 1280, 256, 64, 4, 1250
W = B + 2 * S * T
def pack(kb, ch, q, hv):
    return {"kb": np.ascontiguousarray(kb.reshape(N, 128, B)).astype(np.float32).astype(BF), "ch": np.ascontiguousarray(ch.reshape(N, 128, B)).astype(np.int32),
            "qs": np.ascontiguousarray(q.reshape(N, 128, L)).astype(np.float32).astype(BF), "hv": np.stack([gtable(a.reshape(8, -1)) for a in hv])}
def nodes(rng, pop, n):
    often = np.take_along_axis(pop, rng.integers(0, pop.shape[2], (N, 8, n)), 2)
    return np.where(rng.random((N, 8, n)) < 0.5, often, rng.integers(1, B, (N, 8, n)))
def abroad(h):
    return np.stack([np.roll(h[:, :, t], -t, axis=0) for t in range(T)], axis=2)
def setup_inputs(rng):
    pop = rng.integers(1, B, (N, 8, B // 4)); kb = rng.integers(0, 256, (N, 8, 16, B))
    ch = nodes(rng, pop, 16 * B).reshape(N, 8, 16, B)
    none = rng.choice(np.array([0.03, 0.1, 0.2, 0.3]), (N, 8, 1, 1)); none = np.where(rng.random((N, 8, 1, B)) < 0.02, 1.0, none)
    ch = np.where(rng.random(ch.shape) < none, 0, ch)
    q = rng.integers(0, 256, (N, 8, 16, L)); edge = rng.integers(0, 41, q.shape); edge = np.where(rng.random(q.shape) < 0.5, edge, 255 - edge)
    q = np.where(rng.random((N, 8, 1, L)) < 0.125, edge, q)
    return pack(kb, ch, q, abroad(nodes(rng, pop, T * L).reshape(N, 8, T, L)))
def setup_inputs_spread(rng):
    kb = (np.exp2(8 * rng.random((N, 8, 1, B))) * rng.random((N, 8, 16, B))).astype(np.int64)
    q = (np.exp2(8 * rng.random((N, 8, 1, L))) * rng.random((N, 8, 16, L))).astype(np.int64)
    ch = 1 + ((B - 1) * rng.random((N, 8, 16, B)) ** 2).astype(np.int64)
    ch = np.where(rng.random(ch.shape) < rng.random((N, 8, 1, B)) ** 2, 0, ch)
    hv = 1 + ((B - 1) * rng.random((N, 8, T, L)) ** 2).astype(np.int64)
    return pack(np.minimum(kb, 255), np.minimum(ch, B - 1), np.minimum(q, 255), np.minimum(hv, B - 1))
def setup_inputs_ends(rng):
    d = rng.choice(np.array([0.08, 0.15, 0.5, 0.9]), (N, 8, 1, B), p=np.array([0.4, 0.3, 0.1, 0.2])); kb = 255 * (rng.random((N, 8, 16, B)) < d).astype(np.int64)
    d = rng.choice(np.array([0.08, 0.2, 0.5, 0.9]), (N, 8, 1, L), p=np.array([0.4, 0.3, 0.15, 0.15])); q = 255 * (rng.random((N, 8, 16, L)) < d).astype(np.int64)
    u = rng.random((N, 8, 16, B)); ch = np.where(u < 0.42, 0, np.where(u < 0.64, B - 1, rng.integers(2, B - 1, u.shape)))
    end = rng.random((N, 8, T, L)) < np.where(np.arange(L) < S, 0.35, 0.95)
    hv = np.where(end, np.where(rng.random(end.shape) < 0.5, 1, B - 1), rng.integers(2, B - 1, end.shape))
    kb[..., 1] = 255; kb[..., B - 1] = 255; kb[..., 2] = 0; kb[..., B - 2] = 0; row = np.arange(16)
    ch[..., 1] = np.where(row == 0, 0, np.where(row % 2 == 1, B - 1, 1)); ch[..., 2] = np.where(row % 2 == 1, B - 2, 2)
    q[..., 0] = 0; q[..., L - 1] = 255; q[..., L - 2] = 0; q[..., L - 3] = 0; q[..., L - 4] = 255
    hv[:, :, 0, 0] = 1; hv[:, :, 0, L - 2:] = 1; hv[:, :, 0, L - 4:L - 2] = 2
    return pack(kb, ch, q, hv)
def setup_inputs_corners(rng):
    kb = rng.integers(0, 61, (N, 8, 16, B)); q = rng.integers(0, 61, (N, 8, 16, L)); ch = np.zeros((N, 8, 16, B), np.int64)
    hv = rng.integers(1, B, (N, 8, T, L)); hv[..., 0] = 1; hv[..., L - 1] = B - 1; v = np.arange(B)
    for r in range(N):
        for g in range(8):
            k = (g + r) % 8; c = ch[r, g]; some = rng.integers(1, B, (16, B))
            if k == 0: c[:] = v
            elif k == 2: c[15] = some[15]
            elif k == 3: c[14] = some[14]
            elif k == 4: c[0] = some[0]
            elif k == 5: c[:] = np.where(some % 2 == 0, 1, B - 1)
            elif k == 6: c[rng.integers(0, 16, B), v] = np.where(v < B - 1, v + 1, 1)
            elif k == 7:
                c[:] = some; kb[r, g] = rng.integers(0, 256, (16, B)); q[r, g] = rng.integers(0, 256, (16, L))
    return pack(kb, ch, q, hv)
def setup_inputs_crowd(rng):
    kb = rng.integers(200, 256, (N, 8, 16, B)); q = rng.integers(0, 61, (N, 8, 16, L)); hv = rng.integers(1, B, (N, 8, T, L))
    ch = np.where(rng.random((N, 8, 16, B)) < 0.5, 0, rng.integers(1, B, (N, 8, 16, B)))
    plan = np.zeros((N, 8, 4 * S + 3), np.int64); cuts = np.zeros(N, np.int64); i = np.arange(S)
    for r in range(N):
        for g in range(8):
            o = rng.permutation(np.arange(1, B))
            for place, node in ((2 * S - 1, B - 1), (3 * S - 2, 1)):
                w = int(np.argmax(o == node)); o[w] = o[place]; o[place] = node
            ring = o[:4 * S]; z, y, w = [int(a) for a in o[4 * S:4 * S + 3]]; far = o[4 * S + 3:]; plan[r, g] = o[:4 * S + 3]
            kg = kb[r, g]; cg = ch[r, g]
            kg[:, ring] = rng.integers(0, 61, (16, 4 * S)); kg[:, y] = 5
            cg[:, ring] = np.where(rng.random((16, 4 * S)) < 0.5, 0, far[rng.integers(0, far.size, (16, 4 * S))])
            row = rng.integers(0, 15, 4 * S); row[S] = 0; row[S + 1] = 14; row[2 * S] = 14; row[2 * S + 1] = 0
            cg[row, ring] = np.roll(ring, -S)
            cg[:, [z, y, w]] = 0; cg[int(rng.integers(0, 16)), z] = y
            m = 0 if r == 0 else (1 if g == 7 else 0) if r == 1 else (g + r) % 8
            chain = i + 0; stage = 0 * i; n = S
            if m == 1: chain[1] = 0; n = S - 2
            elif m == 2: chain = 0 * i + S - 1; n = 0
            elif m == 3: chain = 0 * i; chain[S - 1] = S - 1; n = 0
            elif m == 4: chain = 0 * i; chain[S - 2] = S - 2; chain[S - 1] = S - 1; n = 2
            elif m == 5: chain = i % 4; n = 4
            elif m == 6: chain = i - i % 2; stage = 2 * (i % 2)
            elif m == 7: chain = i - i % 2; stage = 3 * (i % 2); n = 0
            hv[r, g, 0, :S] = ring[stage * S + chain]; hv[r, g, 0, S:] = ring[rng.integers(0, 4 * S, L - S)]
            cuts[r] += n
    for t in range(1, T):
        near = np.take_along_axis(np.roll(plan, -t, axis=0), rng.integers(0, 4 * S, (N, 8, L)), 2)
        hv[:, :, t] = np.where(rng.random((N, 8, L)) < 0.75, near, hv[:, :, t])
    then = np.roll(plan, -1, axis=0)
    for e in range(3):
        hv[:, :, 0, L - 6 + e] = plan[:, :, 4 * S]; hv[:, :, 0, L - 3 + e] = plan[:, :, 4 * S + 2]; hv[:, :, 1, L - 3 + e] = then[:, :, 4 * S]
        for r in range(N):
            for lane, s in ((L - 6 + e, TH + e - 1), (L - 3 + e, TH + (int(cuts[(r + 1) % N]) & 63) + e - 1)):
                q[r, :, :, lane] = 5 + s // 16 + (np.arange(16) < s % 16).astype(np.int64)
    return pack(kb, ch, q, hv)
def check_inputs(d):
    bad = []
    for k, lo, hi in (("kb", 0, 255), ("ch", 0, B - 1), ("qs", 0, 255), ("hv", 1, B - 1)):
        v = np.asarray(d[k]).astype(np.float32)
        if not np.all((v >= lo) & (v <= hi)): bad.append("range of " + k)
        elif np.any(v != np.floor(v)): bad.append("whole numbers in " + k)
    return bad
def reference(kb, ch, qs, hv):
    c = np.zeros((N, 8, 16, W), np.int64); c[..., :B] = ch.reshape(N, 8, 16, B)
    K = np.zeros((N, 8, 16, W), np.int32); K[..., :B] = kb.astype(np.float32).astype(np.int32).reshape(N, 8, 16, B)
    q = qs.astype(np.float32).astype(np.int32).reshape(N, 8, 16, L); p = np.zeros((N, 8, 16, L), np.int32)
    h = np.stack([gentries(a) for a in hv]).astype(np.int64).reshape(N, 8, T, L)
    A = [0] * N; row = np.arange(16)[None, :]; lower = np.tril(np.ones((S, S), bool), -1); twin = np.arange(S) ^ 1
    for t in range(T):
        for x in range(N):
            o = (x - t) % N; C = c[x]; Kx = K[x]; Q = q[o][:, :, None, :]; P = p[o]; v = h[o, :, t]
            never = np.ones((8, L), bool); at = [v]; by = []
            for step in range(3):
                kids = np.take_along_axis(C, v[:, None, :], 2)
                key = np.take_along_axis(Kx, kids.reshape(8, 1, 16 * L), 2).reshape(8, 16, 16, L)
                y = np.abs(P[:, :, None, :] - key)
                s = np.where(kids == 0, 2 ** 20, np.add.reduce(np.abs(y - Q), axis=1))
                k = np.argmin(s, axis=1)
                go = np.take_along_axis(s, k[:, None, :], 1)[:, 0] <= TH + A[x]
                v = np.where(go, np.take_along_axis(kids, k[:, None, :], 1)[:, 0], v)
                P = np.where(go[:, None, :], np.take_along_axis(y, k[:, None, None, :], 2)[:, :, 0], P)
                never = never & go; at.append(v); by.append(k)
            p[o] = P
            a, b, j, k = at[1][:, :S], at[2][:, :S], by[1][:, :S], by[2][:, :S]
            can = never[:, :S] & (a != b) & (j < 15)
            two = np.stack([a, b], axis=-1)
            meet = np.any(two[:, :, None, :, None] == two[:, None, :, None, :], axis=(3, 4))
            stand = can & ~np.any(meet & lower & can[:, None, :], axis=2)
            g, i = np.nonzero(stand & stand[:, twin])
            a, b, j, k = a[g, i], b[g, i], j[g, i], k[g, i]; every = np.arange(len(g))
            m = B + 2 * S * t + 2 * i; n = m + 1; other = B + 2 * S * t + 2 * (i ^ 1)
            ra = C[g, :, a]; rb = C[g, :, b]
            ua = row > j[:, None]; ub = row > k[:, None]
            rm = np.where(ua, ra, 0); rm[every, j] = n
            na = np.where(ua, 0, ra); na[every, j + 1] = other
            C[g, :, a] = na; C[g, :, b] = np.where(ub, 0, rb); C[g, :, m] = rm; C[g, :, n] = np.where(ub, rb, 0)
            if t < T - 1:
                Kx[g, :, m] = Kx[g, :, a]; Kx[g, :, n] = Kx[g, :, b]
            A[x] = len(g) & 63
    return {"yc": c.reshape(N, 128, W).astype(np.float32), "yp": p.reshape(N, 128, L).astype(np.float32).astype(BF)}

@@ -1,0 +1,794 @@
+import numpy as np
+from concourse.mybir import AluOpType as ALU, AxisListType as AX, ActivationFunctionType as AF
+
+NB, NL, NS, NT, TH = 1280, 256, 64, 4, 1250
+NW = NB + 2 * NS * NT
+MUL = 4096
+
+CFG = {
+    "chunks": [128, 128],
+    "order": [[(0, 0), (1, 0), (0, 1), (1, 1), (0, 2), (1, 2)]] * 3,
+    "piece": {"v": 16, "s": 32}, "fv": [0.28, 0.5], "small": "s", "wage": 1000, "sl_age": 0, "misc": "s0", "gt": "v", "cage": 99,
+    "own": False, "half": 64, "lg": "v", "bias": {}, "polish": 30000, "heat": 300.0, "seed": 1, "look": 150.0, "part": 0.4, "short": 320.0, "fvs": {},
+    "sl_after": 0,
+    "nd": 4,
+    "ns": 2,
+    "G": 1.56, "SC": 3.8, "cyc": 1.04, "pe": 0.52, "ov": 20.0, "os": 30.0, "mn": 50, "oi": 45.0, "kf": "v", "lat": 100.0, "hop": 2500.0,
+}
+
+
+def layout(cfg):
+    ch = cfg["chunks"]
+    sc = {
+        "chi": ("sbuf", [128, NB], "int32"), "Cw": ("sbuf", [128, NW + 256], "float32"), "K": ("sbuf", [128, NW], "bfloat16"),
+        "psend": ("sbuf", [128, NT * NL], "bfloat16"), "pfin": ("sbuf", [128, NL], "bfloat16"),
+        "hU": ("sbuf", [128, 64], "uint16"), "thr": ("sbuf", [128, 64], "float32"),
+        "ci": ("sbuf", [128, 8], "int32"), "cf": ("sbuf", [128, 16], "float32"),
+        "U": ("sbuf", [128, 144], "float32"), "LY": ("sbuf", [128, 144], "bfloat16"),
+        "SY": ("sbuf", [128, 8], "bfloat16"), "SM": ("sbuf", [128, 8], "bfloat16"), "EM": ("sbuf", [128, 128], "float32"),
+        "RP": ("sbuf", [128, 128], "bfloat16"),
+        "I1": ("sbuf", [128, 128], "bfloat16"), "I2": ("sbuf", [128, 128], "bfloat16"),
+        "G8": ("sbuf", [128, 128], "float32"), "BOf": ("sbuf", [128, 128], "float32"), "BOb": ("sbuf", [128, 128], "bfloat16"),
+        "ones": ("sbuf", [128, 128], "bfloat16"), "R16": ("sbuf", [128, 128], "float32"), "D0": ("sbuf", [128, 128], "float32"),
+        "mk": ("sbuf", [128, 112], "float32"), "C32": ("sbuf", [128, 128], "float32"), "Dq": ("sbuf", [128, 128], "float32"),
+        "Dt": ("sbuf", [128, 256], "float32"),
+        "GT": ("sbuf", [128, 17 * ch[0]], "bfloat16"), "CI": ("sbuf", [128, 16], "float32"), "TG0": ("sbuf", [128, 8], "float32"),
+        "TG": ("sbuf", [128, 16], "float32"), "Dm": ("sbuf", [128, 16], "float32"), "qoff": ("sbuf", [128, 2], "uint16"),
+        "NO": ("sbuf", [128, NT * 128], "float32"), "Z": ("sbuf", [128, 224], "float32"), "X": ("sbuf", [128, 704], "bfloat16"),
+        "sm": ("sbuf", [128, 64], "float32"), "nm": ("sbuf", [128, 8], "float32"), "qsc": ("sbuf", [128, 128], "float32"),
+        "sl": ("sbuf", [128, 4], "bfloat16"), "zi": ("sbuf", [128, 2], "int32"), "zf": ("sbuf", [128, 1], "float32"),
+        "Y": ("sbuf", [128, 384], "float32"), "E2": ("sbuf", [128, 64], "float32"), "sU": ("sbuf", [128, 16], "uint16"),
+    }
+    if cfg["misc"] == "misc":
+        sc["misc"] = ("psum", [128, 512], "float32")
+    sc["LT"] = ("sbuf", [128, 16], "float32")
+    sc["R2"] = ("sbuf", [128, 128], "bfloat16")
+    sc["DG"] = ("sbuf", [128, 128], "bfloat16")
+    sc["ND"] = ("sbuf", [128, 32], "bfloat16")
+    sc["LG"] = ("sbuf", [128, 512], "bfloat16")
+    sc["EQ"] = ("sbuf", [128, 16], "float32")
+    sc["K0"] = ("sbuf", [128, 8], "bfloat16")
+    for L in sorted(set(ch)):
+        sc["OH%d" % L] = ("sbuf", [128, 18 * L], "bfloat16")
+        sc["RJ%d" % L] = ("sbuf", [128, L], "bfloat16")
+        sc["RS%d" % L] = ("sbuf", [128, L], "float32")
+        sc["xi%d" % L] = ("sbuf", [128, 8], "int32")
+        sc["xo%d" % L] = ("sbuf", [128, 8], "uint16")
+    for t in range(NT):
+        sc["q%d" % t] = ("sbuf", [128, NL], "bfloat16")
+        sc["hb%d" % t] = ("sbuf", [128, 80], "int32")
+    for c, L in enumerate(ch):
+        n = L // 16
+        sc["W%d" % c] = ("sbuf", [128, 5 * 17 * L], "bfloat16")
+        sc["key%d" % c] = ("sbuf", [128, 16 * L], "bfloat16")
+        sc["M%d" % c] = ("sbuf", [128, 16 * L], "bfloat16")
+        sc["kU%d" % c] = ("sbuf", [128, L], "uint16")
+        sc["kF%d" % c] = ("sbuf", [128, 2 * L], "float32")
+        sc["pr%d" % c] = ("sbuf", [128, L], "float32")
+        sc["sc%d" % c] = ("sbuf", [128, L], "float32")
+        sc["m%d" % c] = ("sbuf", [128, L], "float32")
+        sc["ex%d" % c] = ("sbuf", [128, 128], "float32")
+        if L == 64:
+            sc["w2%d" % c] = ("sbuf", [128, n], "float32")
+        sc["wi%d" % c] = ("sbuf", [128, n], "int32")
+        sc["ni%d" % c] = ("sbuf", [128, 3 * n], "int32")
+        sc["nU%d" % c] = ("sbuf", [128, 3 * n], "uint16")
+        sc["vU%d" % c] = ("sbuf", [128, 2 * n], "uint16")
+    nq = 8 - (cfg["misc"] == "misc") - cfg["nd"] - cfg["ns"]
+    for k in range(cfg["nd"]):
+        sc["d%d" % k] = ("psum", [128, 512], "float32")
+    for k in range(cfg["ns"]):
+        sc["s%d" % k] = ("psum", [128, 512], "float32")
+    for k in range(nq):
+        sc["qp%d" % k] = ("psum", [128, 512], "float32")
+    place, share = {}, len(ch) - nq
+    small = [c for c in range(len(ch)) if ch[c] == 64]
+    b = 0
+    while share > 0:
+        place[small.pop(0)] = (b, 0, 256)
+        place[small.pop(-1)] = (b, 256, 256)
+        b += 1
+        share -= 1
+    for c in range(len(ch)):
+        if c not in place:
+            place[c] = (b, 0, 512)
+            b += 1
+    sems = ["cv", "cs", "ct", "cg", "ls", "rq", "aq1", "aq2", "aq3", "lq", "lh", "lk", "lk0", "lc0", "lc1", "lc2", "lc3", "syc"]
+    for c in range(len(ch)):
+        sems.append("syp%d" % c)
+        for t in range(NT):
+            sems.append("ap%d_%d" % (t, c))
+    return sc, sems, place
+
+
+SCRATCH, SEMAPHORES, _PLACE = layout(CFG)
+
+
+def R(name, a, b, step=1):
+    return (name, a, b, step)
+
+
+def cnt(x):
+    if x[0] == "ind":
+        return 16 * cnt(x[2])
+    return len(range(x[1], x[2], x[3]))
+
+
+def ap(T, x):
+    if not isinstance(x, tuple):
+        return x
+    if x[0] == "ind":
+        return ap(T, x[1]).indirect(ap(T, x[2]))
+    if x[3] == 1:
+        return T[x[0]][:, x[1]:x[2]]
+    return T[x[0]][:, x[1]:x[2]:x[3]]
+
+
+def IND(win, off):
+    return ("ind", win, off)
+
+
+def regions(xs):
+    out = []
+    for x in xs:
+        if isinstance(x, tuple):
+            if x[0] == "ind":
+                out += [x[1], x[2]]
+            else:
+                out.append(x)
+    return out
+
+
+def build(cfg):
+    sc, _, place = layout(cfg)
+    ch = cfg["chunks"]
+    G, cyc = cfg["G"], cfg["cyc"]
+    ops, hist, banks, age = [], {}, {}, [99]
+
+    def add(eng, cost, reads, writes, calls, sem=None, lat=0.0, after=(), tag=""):
+        k = len(ops)
+        deps, order = set(after), set()
+        acc = [(x, False) for x in regions(reads)]
+        for x in writes:
+            if x[0] == "ind":
+                acc += [(x[1], True), (x[2], False)]
+            else:
+                acc.append((x, True))
+        for x, w in acc:
+            name = x[0]
+            if name not in sc:
+                continue
+            ps = sc[name][0] == "psum"
+            h = hist.setdefault(name, [])
+            keep = []
+            for e in h:
+                o, a, b, ow = e
+                if o != k and a < x[2] and x[1] < b and (w or ow):
+                    if ps and ops[o]["eng"] == eng and eng == "t":
+                        order.add(o)
+                    else:
+                        deps.add(o)
+                if not (w and x[3] == 1 and x[1] <= a and b <= x[2]):
+                    keep.append(e)
+            keep.append((k, x[1], x[2], w))
+            hist[name] = keep
+            if ps:
+                st = banks.setdefault(name, [None, [], []])
+                if st[0] != eng:
+                    st[0], st[2], st[1] = eng, st[1], []
+                deps.update(st[2])
+                if eng == "t":
+                    order.update(o for o in st[1] if o != k)
+                if k not in st[1]:
+                    st[1].append(k)
+        deps.discard(k)
+        ops.append({"eng": eng, "cost": cost, "deps": deps, "order": order - deps, "calls": calls, "sem": sem, "lat": lat, "tag": tag,
+                    "alt": None, "swap": None, "age": age[0]})
+        return k
+
+    def two(*xs):
+        return all(sc[(x[1] if x[0] == "ind" else x)[0]][2] in ("bfloat16", "uint16") for x in xs)
+
+    def vcost(n, rate):
+        return cfg["ov"] + max(n * rate, cfg["mn"]) * cyc + (cfg["oi"] if rate in (G, cfg["SC"]) else 0)
+
+    def rate(out, a, plain):
+        if a[0] == "ind":
+            return G
+        if out[0] == "ind":
+            return cfg["SC"]
+        return plain
+
+    def copy(out, a, tag=""):
+        return add("v", vcost(cnt(a), rate(out, a, 0.5 if two(out, a) else 1)), [a], [out],
+                   [lambda q, T: q.tensor_copy(ap(T, out), ap(T, a))], tag=tag)
+
+    def tt(out, a, b, op, tag=""):
+        ps = any(x[0] != "ind" and sc[x[0]][0] == "psum" for x in (a, b))
+        return add("v", vcost(cnt(a), rate(out, a, 1 if ps else 2)), [a, b], [out],
+                   [lambda q, T: q.tensor_tensor(ap(T, out), ap(T, a), ap(T, b), op)], tag=tag)
+
+    def ts(out, a, s1, op0, s2=None, op1=None, tag=""):
+        if op1 is None:
+            f = lambda q, T: q.tensor_scalar(ap(T, out), ap(T, a), ap(T, s1), None, op0)
+        else:
+            f = lambda q, T: q.tensor_scalar(ap(T, out), ap(T, a), ap(T, s1), ap(T, s2), op0, op1)
+        return add("v", vcost(cnt(a), rate(out, a, 0.5 if two(out, a) else 1)), [a, s1, s2], [out], [f], tag=tag)
+
+    def mset(out, val):
+        return add("v", vcost(cnt(out), 0.5 if two(out) else 1), [], [out], [lambda q, T: q.memset(ap(T, out), val)])
+
+    def scan(out, d0, d1, op1, tag=""):
+        return add("v", vcost(cnt(d1), 1), [d0, d1], [out],
+                   [lambda q, T: q.tensor_tensor_scan(ap(T, out), ap(T, d0), ap(T, d1), 0.0, ALU.add, op1)], tag=tag)
+
+    def rmin(out, a):
+        return add("v", vcost(cnt(a), 1), [a], [out], [lambda q, T: q.tensor_reduce(ap(T, out), ap(T, a), AX.X, ALU.min)], tag="red")
+
+    def act(out, a, func, tag="", scale=None, bias=None):
+        if scale is not None:
+            f = lambda q, T: q.activation(ap(T, out), ap(T, a), func, scale=ap(T, scale))
+        elif bias is not None:
+            f = lambda q, T: q.activation(ap(T, out), ap(T, a), func, bias=ap(T, bias))
+        else:
+            f = lambda q, T: q.activation(ap(T, out), ap(T, a), func)
+        return add("s", cfg["os"] + (cnt(a) * cyc * G + cfg["oi"] if a[0] == "ind" else max(cnt(a), cfg["mn"]) * cyc),
+                   [a, scale, bias], [out], [f], tag=tag)
+
+    def gather(eng, out, a, tag=""):
+        eng = cfg["small"] if eng == "x" else eng
+        k = act(out, a, AF.Copy, tag)
+        ops[k]["swap"] = {"s": (ops[k]["cost"], ops[k]["calls"]),
+                          "v": (vcost(cnt(a), G), [lambda q, T: q.tensor_copy(ap(T, out), ap(T, a))])}
+        ops[k]["eng"] = eng
+        ops[k]["cost"], ops[k]["calls"] = ops[k]["swap"][eng]
+        return k
+
+    def mm(lst, tag=""):
+        cost, calls = 0.0, []
+        for (o, l, r, st, sp) in lst:
+            cost += max(64, cnt(r)) * cfg["pe"] * (4 if sc[l[0]][2] == "float32" else 1)
+            calls.append(lambda q, T, o=o, l=l, r=r, st=st, sp=sp: q.matmul(ap(T, o), ap(T, l), ap(T, r), st, sp))
+        return add("t", cost, [x[1] for x in lst] + [x[2] for x in lst], [x[0] for x in lst], calls, lat=60.0, tag=tag)
+
+    def iota(out, pat, base, cm=0):
+        if sc[out[0]][2] == "int32":
+            f = lambda q, T: q.iota(ap(T, out), pat, base, cm)
+        else:
+            f = lambda q, T: q.iota(ap(T, out), pat, base, cm, allow_small_or_imprecise_dtypes=True)
+        return add("g", 160 + 2 * cyc * cnt(out), [], [out], [f])
+
+    def dma(eng, out, a, sem, lat):
+        return add(eng, 60.0, [a], [out], [lambda q, T: q.dma_start(ap(T, out), ap(T, a))], sem=sem, lat=lat, tag="dma")
+
+    def col(k):
+        return R("cf", k, k + 1)
+
+    def whole(n):
+        return R(n, 0, sc[n][1][1])
+
+    dma("y", R("hb0", 0, 64), R("hv", 0, 64), "lh", 2000)
+    for k in range(4):
+        dma("y", R("chi", 320 * k, 320 * k + 320), R("ch", 320 * k, 320 * k + 320), "lc%d" % k, 2300 + 500 * k)
+    dma("s", whole("q0"), R("qs", 0, NL), "lq", 2000)
+    dma("s", whole("K0"), R("kb", 0, 8), "lk0", 2000)
+    dma("s", R("K", 8, NB), R("kb", 8, NB), "lk", 4400)
+
+    iota(R("ci", 0, 1), [[0, 1]], 0, 1)
+    iota(col(3), [[0, 1]], 0, 1)
+    iota(whole("U"), [[1, 144]], 0)
+    ts(R("ci", 1, 2), R("ci", 0, 1), 15, ALU.bitwise_and)
+    ts(R("ci", 2, 3), R("ci", 0, 1), 4, ALU.arith_shift_right)
+    ts(R("ci", 3, 4), R("ci", 0, 1), 14, ALU.bitwise_and)
+    ts(R("ci", 4, 5), R("ci", 0, 1), 3, ALU.bitwise_and)
+    copy(R("cf", 0, 2), R("ci", 1, 3))
+    ts(col(2), R("ci", 2, 3), 16, ALU.mult, 15, ALU.add)
+    ts(col(4), R("ci", 1, 2), -2048, ALU.mult, 15 * 2048, ALU.add)
+    ts(col(5), R("ci", 3, 4), 2, ALU.mult)
+    ts(col(6), R("ci", 3, 4), -2 ** 20, ALU.mult, 28 * 2 ** 19, ALU.add)
+    ts(col(10), R("ci", 3, 4), 2 ** 20, ALU.mult, -28 * 2 ** 19, ALU.add)
+    ts(col(7), R("ci", 3, 4), 2, ALU.mult, 3, ALU.add)
+    ts(col(8), R("ci", 1, 2), 2, ALU.mult)
+    ts(R("qoff", 0, 1), R("ci", 4, 5), 32, ALU.mult, 31, ALU.add)
+    ts(whole("I1"), R("U", 0, 128), col(3), ALU.is_equal)
+    ts(whole("I2"), R("U", 0, 128), col(3), ALU.is_equal, -1.0, ALU.mult)
+    ts(whole("LY"), whole("U"), col(2), ALU.is_equal, float(MUL), ALU.mult)
+    first = [sum(ch[:c]) for c in range(len(ch))]
+    for c, L in enumerate(ch):
+        iota(R("CI", first[c] // 16, (first[c] + L) // 16), [[16, L // 16]], MUL * TH + 16 * L)
+        mset(R("W%d" % c, 16 * L, 17 * L), 0.0)
+    ts(whole("CI"), whole("CI"), col(0), ALU.add)
+    for L in sorted(set(ch)):
+        iota(whole("RJ%d" % L), [[0, 8], [128, L // 8]], 0)
+        mset(whole("RS%d" % L), 0.0)
+        mset(R("RS%d" % L, 0, L, L // 8), float(2 ** 28))
+        iota(whole("xi%d" % L), [[L // 8, 8]], L // 8 - 1)
+        copy(whole("xo%d" % L), whole("xi%d" % L))
+    iota(whole("RP"), [[0, 128]], 0, 1)
+    iota(whole("G8"), [[1, 8], [0, 16]], 0)
+    ts(whole("BOf"), whole("G8"), col(1), ALU.is_equal)
+    ts(whole("BOb"), whole("G8"), col(1), ALU.is_equal, 2048.0, ALU.mult)
+    mset(whole("ones"), 1.0)
+    iota(whole("R16"), [[0, 8], [1, 16]], 0)
+    age[0] = 0
+    ts(whole("EM"), whole("R16"), col(0), ALU.is_equal)
+    ts(whole("LT"), R("U", 0, 16), col(0), ALU.is_lt)
+    ts(whole("EQ"), R("U", 0, 16), col(0), ALU.is_equal)
+    for L in sorted(set(ch)):
+        mset(R("OH%d" % L, 16 * L, 18 * L), 0.0)
+        for u in range(16):
+            act(R("OH%d" % L, u * L, u * L + L), R("ones", 0, L), AF.Copy, tag="tab", scale=R("EQ", u, u + 1))
+    L = ch[0]
+    mset(R("GT", 15 * L, 17 * L), 0.0)
+    for u in range(15):
+        if cfg["gt"] == "s":
+            act(R("GT", u * L, u * L + L), R("ones", 0, L), AF.Copy, tag="tab", scale=R("LT", u, u + 1))
+        else:
+            ts(R("GT", u * L, u * L + L), R("ones", 0, L), R("LT", u, u + 1), ALU.mult)
+    age[0] = cfg["cage"]
+    ts(whole("SY"), R("U", 0, 8), col(1), ALU.is_equal, float(MUL), ALU.mult)
+    ts(whole("SM"), R("U", 0, 8), col(1), ALU.is_equal, -2.0 * MUL, ALU.mult)
+    ts(whole("D0"), whole("EM"), 65536.0 + 2048.0, ALU.mult, -2048.0, ALU.add)
+    ts(col(9), R("ci", 1, 2), -1, ALU.mult)
+    act(whole("mk"), R("R16", 0, 112), AF.Sign, bias=col(9))
+    iota(R("mk", 16, 64), [[0, 48]], 1)
+    iota(whole("C32"), [[0, 4], [1, 32]], 0)
+    iota(whole("R2"), [[0, 4], [1, 16], [0, 2]], 0)
+    ts(whole("DG"), whole("R2"), col(0), ALU.is_equal)
+    ts(whole("ND"), R("R2", 0, 32), col(0), ALU.is_equal, -1.0, ALU.mult)
+    ts(whole("Dq"), whole("C32"), col(5), ALU.is_equal, -float(2 ** 25), ALU.mult)
+    ts(R("Dt", 0, 128), whole("C32"), col(5), ALU.is_lt, float(2 ** 19), ALU.mult)
+    ts(R("Dt", 128, 256), whole("C32"), col(7), ALU.is_gt, float(2 ** 19), ALU.mult)
+    tt(R("Dt", 0, 128), R("Dt", 0, 128), R("Dt", 128, 256), ALU.add)
+    tt(whole("Dq"), whole("Dq"), R("Dt", 0, 128), ALU.add)
+    iota(whole("TG0"), [[1, 2], [32, 4]], NB)
+    iota(whole("Dm"), [[16, 16]], NW)
+    ts(whole("Dm"), whole("Dm"), col(0), ALU.add)
+    for t in range(NT):
+        iota(R("NO", 128 * t, 128 * t + 64), [[-2, 64]], -(NB + 128 * t + 1))
+        iota(R("NO", 128 * t + 64, 128 * t + 128), [[4, 32], [-2, 2]], NB + 128 * t + 2)
+
+    iota(R("Cw", NB, NW + 256), [[0, NW + 256 - NB]], 0)
+    iota(R("Y", 64, 128), [[0, 64]], 0)
+    mset(R("Cw", 0, 1), 0.0)
+    for k in range(4):
+        a = max(1, 320 * k)
+        copy(R("Cw", a, 320 * k + 320), R("chi", a, 320 * k + 320))
+    mset(R("K", 0, 1), 2048.0)
+    copy(R("K", 1, 8), R("K0", 1, 8))
+
+    misc = cfg["misc"]
+    mm([(R(misc, 336, 352), R("LY", 15 - r, 143 - r), R("q0", r, NL, 16), r == 0, r == 15) for r in range(16)])
+    tt(R("hb0", 64, 80), whole("CI"), R(misc, 336, 352), ALU.subtract)
+    k = add("g", 3000.0, [whole("q0"), whole("hb0")], [], [("sendq",)], sem="ls")
+    for t in range(1, NT):
+        add("n", 0.0, [], [whole("q%d" % t), whole("hb%d" % t)], [], sem="aq%d" % t, lat=3 * cfg["hop"], after=[k])
+
+    turn = [0, 0]
+
+    def step(t, c, s):
+        L, f0 = ch[c], first[c]
+        n = L // 16
+        Wn, key, M = "W%d" % c, "key%d" % c, "M%d" % c
+        w = 17 * L * (4 if s == 1 else t)
+        wn = 17 * L * (4 if s == 0 else t)
+        base = NB + 128 * t
+        voff = R("hU", 16 * t + f0 // 16, 16 * t + f0 // 16 + n) if s == 0 else R("vU%d" % c, (s - 1) * n, s * n)
+        kids = IND(whole("chi") if t + s == 0 and cfg["kf"] == "v" else R("Cw", 0, NW), voff)
+        copy(whole("kU%d" % c), kids, "gC")
+        if s == 2 and c == 0:
+            copy(R("Y", 320, 384), R("kU0", 0, 64), "gCf")
+        elif s < 2:
+            if cfg["kf"] == "v":
+                copy(R("kF%d" % c, s * L, s * L + L), whole("kU%d" % c), "gCf")
+            else:
+                gather("s", R("kF%d" % c, s * L, s * L + L), kids, "gCf")
+        cut = cfg["fvs"].get(age[0], 2 * int(round(L * cfg["fv"][s == 0 and c == 0] / 2)))
+        for eng, a0, b0 in (("v", 0, cut), ("s", cut, L)):
+            m = -(-(b0 - a0) // cfg["piece"][eng])
+            for u in range(m):
+                a, b = a0 + 2 * ((b0 - a0) // 2 * u // m), a0 + 2 * ((b0 - a0) // 2 * (u + 1) // m)
+                gather(eng, R(key, 16 * a, 16 * b), IND(R("K", 0, base), R("kU%d" % c, a, b)), "gK")
+        qb, qa, qw = place[c]
+        if s == 0:
+            mm([(R("qp%d" % qb, qa + u, qa + u + L), whole("I1"), R("q%d" % t, f0, f0 + L), True, True) for u in range(0, qw, L)], "q")
+        per, J = 512 // L, L // 8
+        S = "s%d" % ((c if cfg["ns"] >= len(ch) else turn[1]) % cfg["ns"])
+        turn[1] += 1
+        mm([(R(S, 0, L), whole("I1"), whole("RJ%d" % L), True, False), (R(S, 0, L), whole("I1"), R("RP", 0, L), False, False)], "low")
+        p = R(Wn, w + 16 * L, w + 17 * L)
+        for j0 in range(0, 16, per):
+            d = "d%d" % (2 * c + turn[0] % 2 if cfg["own"] else turn[0] % cfg["nd"])
+            turn[0] += 1
+            h = cfg["half"]
+            for i0 in range(0, L, h):
+                lst, i1 = [], min(L, i0 + h)
+                for u in range(per):
+                    o = R(d, u * L + i0, u * L + i1)
+                    alone = t == 0 and s == 0
+                    lst.append((o, whole("I1"), R(key, 16 * i0 + j0 + u, 16 * i1, 16), True, alone))
+                    if not alone:
+                        lst.append((o, whole("I2"), R(Wn, p[1] + i0, p[1] + i1), False, True))
+                mm(lst, "d")
+            act(R(Wn, w + j0 * L, w + j0 * L + 512), whole(d), AF.Abs, "abs")
+            for u in range(0, 512, qw):
+                a = j0 * L + u
+                tt(R(M, a, a + qw), R(Wn, w + a, w + a + qw), R("qp%d" % qb, qa, qa + qw), ALU.min, "min")
+            tiles = range(j0 * L // 128, j0 * L // 128 + 4)
+            mm([(R(S, u, L, J), R(Wn, w + 128 * u, w + 128 * u + 128), whole("SY"), False, False) for u in tiles]
+               + [(R(S, u, L, J), R(M, 128 * u, 128 * u + 128), whole("SM"), False, u == J - 1) for u in tiles], "sum")
+        scan(whole("m%d" % c), whole("RS%d" % L), R(S, 0, L), ALU.min, "amin")
+        tt(whole("ex%d" % c), IND(whole("m%d" % c), whole("xo%d" % L)), whole("EM"), ALU.mult, "ex")
+        mm([(R(S, 256, 264), whole("ex%d" % c), R("BOf", 0, 128, 16), True, True)], "exm")
+        bound = R("thr", 16 * t + f0 // 16, 16 * t + f0 // 16 + n)
+        if L == 64:
+            tt(whole("w2%d" % c), R(S, 260, 264), bound, ALU.min, "A0")
+            bound = whole("w2%d" % c)
+        tt(whole("wi%d" % c), R(S, 256, 256 + n), bound, ALU.min, "A")
+        ni, nU = R("ni%d" % c, s * n, s * n + n), R("nU%d" % c, s * n, s * n + n)
+        ts(ni, whole("wi%d" % c), MUL - 1, ALU.bitwise_and, tag="B")
+        copy(nU, ni, "C")
+        if s < 2:
+            gather("x", R(Wn, wn + 16 * L, wn + 17 * L), IND(R(Wn, w, w + 17 * L), nU), "gp")
+            pr = "pr%d" % c
+            tt(whole(pr), IND(R("OH%d" % L, 0, 17 * L), nU), R("kF%d" % c, s * L, s * L + L), ALU.mult, "oh")
+            lst = [(R(S, 272, 272 + L), whole("BOf"), whole(pr), True, True)]
+            if c == 0:
+                if L > 64:
+                    lst.append((R(S, 272 + L, 272 + L + 64), whole("BOf"), R(pr, 0, 64), True, True))
+                z = 272 if L == 64 else 272 + L
+                lst.append((R(S, z + 64, z + 112), whole("BOf"), R(pr, 16, 64), True, True))
+            mm(lst, "vrep")
+            scan(whole("sc%d" % c), R("D0", 0, L), R(S, 272, 272 + L), ALU.min, "scan")
+            ts(R("vU%d" % c, s * n, s * n + n), R("sc%d" % c, 15, L, 16), col(4), ALU.add, tag="cvt")
+            if c == 0:
+                tt(R("Z", s, 224, 2), R(S, z, z + 112), whole("mk"), ALU.mult)
+                act(R("TG", 8 + 4 * s, 12 + 4 * s), R("sc0", 15, 64, 16), AF.Identity, bias=col(4))
+                if t < NT - 1:
+                    gather("x", R("K", base + s, base + 128, 2), IND(R("K", 0, base), R("vU0", n * s, n * s + 4)))
+        else:
+            src = R("psend", NL * t + f0, NL * t + f0 + L)
+            dst = R(Wn, 17 * L * (t + 1) + 16 * L, 17 * L * (t + 2)) if t < NT - 1 else R("pfin", f0, f0 + L)
+            gather("x", src, IND(R(Wn, w, w + 17 * L), nU), "gp")
+            k = add("g", 300.0, [src], [], [("sendp", src, dst, "ap%d_%d" % (t, c))], sem="ls")
+            add("n", 0.0, [], [dst], [], sem="ap%d_%d" % (t, c), lat=2 * cfg["hop"], after=[k])
+            if t == NT - 1:
+                dma("y", R("yp", f0, f0 + L), dst, "syp%d" % c, 2200)
+
+    def slices(t):
+        ts(R("TG", 0, 8), whole("TG0"), col(8), ALU.add, float(128 * t), ALU.add)
+        tt(R("sm", 0, 4), R("TG", 8, 12), R("TG", 12, 16), ALU.not_equal)
+        L = ch[0]
+        n = L // 16
+        ts(R("sm", 4, 8), R("ni0", n, n + 4), 15 * L, ALU.is_lt, tag="pre")
+        tt(R("sm", 8, 12), R("sm", 0, 4), R("sm", 4, 8), ALU.mult, "pre")
+        for u in range(2):
+            tt(R("nm", 4 * u, 4 * u + 4), R("TG", 8 + 4 * u, 12 + 4 * u), R("sm", 8, 12), ALU.mult, "pre")
+        act(R("sm", 16, 32), whole("TG"), AF.Identity, "pre", bias=col(10))
+        tt(R("sm", 12, 16), R("wi0", 0, 4), R("thr", 16 * t, 16 * t + 4), ALU.is_lt, "go")
+        seg = [(0, 128, [(0, 128, 0)]), (64, 160, [(0, 64, 64), (64, 96, 32)]), (96, 192, [(0, 32, 96), (64, 96, 64)]), (192, 224, [(0, 32, 96)])]
+        lst, x = [(R(misc, 256, 384), whole("BOb"), whole("DG"), True, False)], 0
+        for c, (a, b, parts) in enumerate(seg):
+            lg = R("LG", 128 * c, 128 * c + 128)
+            if cfg["lg"] == "v":
+                ts(lg, whole("BOb"), R("sm", 12 + c, 13 + c), ALU.mult, tag="go")
+            else:
+                act(lg, whole("BOb"), AF.Copy, "go", scale=R("sm", 12 + c, 13 + c))
+            lst.append((R(misc, 256 + 32 * c, 288 + 32 * c), lg, whole("ND"), False, False))
+            for u in range(2):
+                ts(R("X", x, x + b - a), R("Z", a, b), R("nm", 4 * u + c, 4 * u + c + 1), ALU.is_equal, tag="cmp")
+                for (i0, i1, to) in parts:
+                    lst.append((R(misc, 256 + to, 256 + to + i1 - i0), lg, R("X", x + i0, x + i1), False, c == 3 and u == 1))
+                x += b - a
+        mm(lst, "cnt")
+        scan(whole("qsc"), whole("Dq"), R(misc, 256, 384), ALU.max, "post")
+        tt(R("sm", 32, 48), IND(whole("qsc"), R("qoff", 0, 1)), R("sm", 16, 32), ALU.add, "post")
+        tt(R("sm", 48, 64), R("sm", 32, 48), whole("Dm"), ALU.min, "post")
+        copy(whole("sU"), R("sm", 48, 64), "post")
+        ra, rb = R("kF0", L, L + 64), R("Y", 320, 384)
+        for u, old in enumerate((ra, rb)):
+            tt(R("Y", 128 + 64 * u, 192 + 64 * u), IND(whole("GT"), R("nU0", n * (u + 1), n * (u + 1) + 4)), old, ALU.mult, "v4")
+        tt(R("Y", 0, 64), IND(R("OH%d" % L, 0, 17 * L), R("nU0", n, n + 4)), R("NO", 128 * t, 128 * t + 64), ALU.mult, "v4")
+        tt(whole("E2"), IND(R("OH%d" % L, L, 18 * L), R("nU0", n, n + 4)), R("NO", 128 * t + 64, 128 * t + 128), ALU.mult, "v4")
+        tt(R("Y", 256, 320), whole("E2"), ra, ALU.add, "v4")
+        if t < NT - 1:
+            ts(whole("sl"), R("qsc", 31, 128, 32), col(6), ALU.is_equal)
+            mm([(R(misc, 384, 385), whole("ones"), R("sl", u, u + 1), u == 0, u == 3) for u in range(4)])
+            copy(R("zi", 0, 1), R(misc, 384, 385))
+            ts(R("zi", 1, 2), R("zi", 0, 1), 63, ALU.bitwise_and)
+            ts(whole("zf"), R("zi", 1, 2), MUL, ALU.mult)
+
+    for t in range(NT):
+        order = cfg["order"][0 if t == 0 else 2 if t == NT - 1 else 1]
+        age[0] = t * len(order)
+        copy(R("hU", 16 * t, 16 * t + 16), R("hb%d" % t, 16 * t, 16 * t + 16))
+        if t == 0:
+            copy(R("thr", 0, 16), R("hb0", 64, 80))
+        else:
+            ts(R("thr", 16 * t, 16 * t + 16), R("hb%d" % t, 64, 80), whole("zf"), ALU.add)
+        at = min(order.index((0, 2)) + cfg["sl_after"], len(order) - 1)
+        for u, (c, s) in enumerate(order):
+            age[0] = t * len(order) + u
+            step(t, c, s)
+            if u == at:
+                age[0] = t * len(order) + order.index((0, 2)) + cfg["sl_age"]
+                slices(t)
+        age[0] = (t + 1) * len(order) - 1
+        tt(IND(whole("Cw"), whole("sU")), R("Y", 128, 384), R("Y", 0, 256), ALU.subtract, "scat")
+    copy(R("Cw", 0, 1), R("chi", 0, 1))
+    dma("y", R("yc", 0, NW), R("Cw", 0, NW), "syc", 5000)
+    return ops
+
+
+def schedule(ops, cfg):
+    n, lat = len(ops), cfg["lat"]
+    succ = [[] for _ in range(n)]
+    left = [0] * n
+    for k, o in enumerate(ops):
+        for d in o["deps"] | o["order"]:
+            succ[d].append(k)
+            left[k] += 1
+    prio = [0.0] * n
+    for k in range(n - 1, -1, -1):
+        prio[k] = ops[k]["cost"] + ops[k]["lat"] + max([prio[x] + lat for x in succ[k]], default=0.0)
+    age = [o["age"] for o in ops]
+    for k in range(n - 1, -1, -1):
+        age[k] = min([age[k]] + [age[x] for x in succ[k]])
+        if ops[k]["tag"] == "tab":
+            age[k], prio[k] = -1, prio[0]
+        prio[k] += cfg["bias"].get(ops[k]["tag"] + str(age[k]), 0) - cfg["wage"] * age[k]
+    ready = {e: [] for e in "vstgyn"}
+    at = [0.0] * n
+
+    def offer(k):
+        for e in (ops[k]["alt"] or ops[k]["eng"]):
+            ready[e].append(k)
+
+    for k in range(n):
+        if left[k] == 0:
+            offer(k)
+    free = {e: 0.0 for e in ready}
+    seq, start, end = [], [0.0] * n, [0.0] * n
+    while len(seq) < n:
+        best = None
+        for e, lst in ready.items():
+            if lst:
+                t0 = max(free[e], min(at[k] for k in lst))
+                if best is None or t0 < best[0]:
+                    best = (t0, e)
+        t0, e = best
+        k = max((x for x in ready[e] if at[x] <= t0 + 1e-6), key=lambda x: (prio[x], -x))
+        soon = [x for x in ready[e] if t0 + 1e-6 < at[x] <= t0 + min(cfg["look"], cfg["part"] * ops[k]["cost"])
+                and prio[x] > prio[k] and ops[x]["cost"] < cfg["short"]]
+        if soon:
+            k = min(soon, key=lambda x: at[x])
+            t0 = at[k]
+        for e2 in (ops[k]["alt"] or e):
+            ready[e2].remove(k)
+        if ops[k]["alt"]:
+            ops[k]["eng"] = e
+            ops[k]["cost"], ops[k]["calls"] = ops[k]["alt"][e]
+        start[k] = t0
+        free[e] = t0 + ops[k]["cost"]
+        end[k] = free[e] + ops[k]["lat"]
+        seq.append(k)
+        for x in succ[k]:
+            at[x] = max(at[x], end[k] + lat if k in ops[x]["deps"] else free[e])
+            left[x] -= 1
+            if left[x] == 0:
+                offer(x)
+    return seq, start, end
+
+
+def polish(ops, seq, cfg):
+    n, lat = len(ops), cfg["lat"]
+    code = {e: u for u, e in enumerate("vstgyn")}
+    eng = [code[o["eng"]] for o in ops]
+    cost = [o["cost"] for o in ops]
+    tail = [o["lat"] + lat for o in ops]
+    deps = [tuple(o["deps"]) for o in ops]
+    pred = [o["deps"] | o["order"] for o in ops]
+    other = [(o["swap"]["v"][0], o["swap"]["s"][0]) if o["swap"] else None for o in ops]
+
+    def run(sq):
+        free, last = [0.0] * 6, [-1] * 6
+        end, start, why = [0.0] * n, [0.0] * n, [-1] * n
+        for k in sq:
+            e = eng[k]
+            t, w = free[e], last[e]
+            for d in deps[k]:
+                if end[d] > t:
+                    t, w = end[d], n + d
+            start[k], why[k] = t, w
+            t += cost[k]
+            free[e], last[e] = t, k
+            end[k] = t + tail[k]
+        return max(end), start, why, end
+
+    state = [cfg["seed"]]
+
+    def rnd():
+        state[0] = (state[0] * 6364136223846793005 + 1442695040888963407) % 2 ** 64
+        return (state[0] >> 11) / 2.0 ** 53
+
+    now, start, why, end = run(seq)
+    best, keep = now, (list(seq), list(eng))
+    arcs = None
+    for it in range(cfg["polish"]):
+        if arcs is None:
+            seq = [k for _, _, k in sorted((start[k], u, k) for u, k in enumerate(seq))]
+            arcs, k = [], max(range(n), key=lambda x: end[x])
+            while k >= 0:
+                w = why[k]
+                if 0 <= w < n:
+                    arcs.append((w, k))
+                k = w - n if w >= n else w
+        u, v = arcs[int(rnd() * len(arcs))]
+        flip = u if other[u] else v if other[v] else -1
+        if flip >= 0 and rnd() < 0.3:
+            eng[flip] ^= 1
+            cost[flip] = other[flip][eng[flip]]
+            new = seq
+        else:
+            flip = -1
+            if u in pred[v]:
+                continue
+            a, b = seq.index(u), seq.index(v)
+            far = int(rnd() ** 2 * 4)
+            if rnd() < 0.5:
+                while far and b + 1 < n:
+                    b += 1
+                    far -= eng[seq[b]] == eng[u]
+                if any(u in pred[x] for x in seq[a + 1:b + 1]):
+                    continue
+                new = seq[:a] + seq[a + 1:b + 1] + [u] + seq[b + 1:]
+            else:
+                while far and a > 0:
+                    a -= 1
+                    far -= eng[seq[a]] == eng[v]
+                early = [v]
+                for x in seq[b - 1:a - 1 if a else None:-1]:
+                    if any(x in pred[y] for y in early):
+                        early.append(x)
+                if any(eng[x] == eng[v] for x in early[1:]):
+                    continue
+                early.reverse()
+                new = seq[:a] + early + [x for x in seq[a:b] if x not in early] + seq[b + 1:]
+        r = run(new)
+        if r[0] <= now + cfg["heat"] * (1.0 - it / cfg["polish"]) * rnd() ** 3:
+            now, start, why, end = r
+            seq, arcs = new, None
+            if now < best:
+                best, keep = now, (list(seq), list(eng))
+        elif flip >= 0:
+            eng[flip] ^= 1
+            cost[flip] = other[flip][eng[flip]]
+    seq, eng = keep
+    for k, o in enumerate(ops):
+        if o["swap"]:
+            o["eng"] = "vs"[eng[k]]
+            o["cost"], o["calls"] = o["swap"][o["eng"]]
+    return seq, best
+
+
+_PLAN = {}
+
+
+def plan():
+    if not _PLAN:
+        _PLAN["ops"] = build(CFG)
+        _PLAN["seq"] = polish(_PLAN["ops"], schedule(_PLAN["ops"], CFG)[0], CFG)[0]
+    return _PLAN["ops"], _PLAN["seq"]
+
+
+def relay_of(core, T, topo):
+    ok = [c for c in topo.cores_of(core) if T.rank_of(c) is None and all(topo.may_write(c, d) for d in T.cores)]
+    same = [c for c in ok if topo.die(c) == topo.die(core)]
+    return (same or ok)[0]
+
+
+def put(g, T, topo, core, dst_core, out, src, sem):
+    rid, pid = topo.addr(dst_core, core)
+    g.remote_dma(ap(T, out), ap(T, src), T.sem[sem], T.sem.ls, pid, rid, topo.mask(core, dst_core))
+    return len(topo.engines(core, dst_core))
+
+
+def bundle(t):
+    return [R("q%d" % t, 0, NL), R("hb%d" % t, 0, 80)]
+
+
+def last_hop(T, topo, src_rank, dst_rank):
+    a, b = T.cores[src_rank], T.cores[dst_rank]
+    return a if topo.may_write(a, b) else relay_of(a, T, topo)
+
+
+def relay_program(g, core, rank, T, topo):
+    ops, seq = plan()
+    N = len(T.cores)
+    own = T.cores[rank]
+    e = len(topo.engines(own, core))
+    sent = 0
+    for k in seq:
+        for call in ops[k]["calls"]:
+            if isinstance(call, tuple) and call[0] == "sendq":
+                far = [t for t in range(1, NT) if last_hop(T, topo, rank, (rank + t) % N) == core]
+                if far:
+                    g.wait_ge(T.sem.rq, 2 * e)
+                for t in far:
+                    for o, s in zip(bundle(t), bundle(0)):
+                        sent += put(g, T, topo, core, T.cores[(rank + t) % N], o, s, "aq%d" % t)
+            elif isinstance(call, tuple) and last_hop(T, topo, rank, (rank + 1) % N) == core:
+                g.wait_ge(T.sem[call[3]], e)
+                sent += put(g, T, topo, core, T.cores[(rank + 1) % N], call[2], call[1], call[3])
+    if sent:
+        g.wait_ge(T.sem.ls, sent)
+
+
+def rank_program(g, core, T, topo):
+    rank = T.rank_of(core)
+    N = len(T.cores)
+    if rank is None:
+        for r in range(N):
+            if relay_of(T.cores[r], T, topo) == core:
+                relay_program(g, core, r, T, topo)
+        return
+    ops, seq = plan()
+    queue = {"v": g.vector, "s": g.scalar, "t": g.tensor, "g": g, "y": g.sync}
+    own = {"v": "cv", "s": "cs", "t": "ct", "g": "cg"}
+    relay = relay_of(core, T, topo)
+    count = {}
+    known = {e: {} for e in queue}
+    done = {}
+    for k in seq:
+        o = ops[k]
+        e = o["eng"]
+        if e == "n":
+            if o["sem"][1] == "q":
+                frm, times = (rank - int(o["sem"][2])) % N, 2
+            else:
+                frm, times = (rank - 1) % N, 1
+            count[o["sem"]] = times * len(topo.engines(last_hop(T, topo, frm, rank), core))
+            done[k] = (o["sem"], count[o["sem"]], {})
+            continue
+        q, kn = queue[e], known[e]
+        need = {}
+        for d in o["deps"]:
+            if done[d][0] != "ls" and done[d][1] > need.get(done[d][0], (0, None))[0]:
+                need[done[d][0]] = (done[d][1], d)
+        for s, (v, d) in sorted(need.items(), key=lambda x: -x[1][1]):
+            if kn.get(s, 0) < v:
+                q.wait_ge(T.sem[s], v)
+                kn[s] = v
+                for s2, v2 in done[d][2].items():
+                    if kn.get(s2, 0) < v2:
+                        kn[s2] = v2
+        s = o["sem"] or own[e]
+        for call in o["calls"]:
+            if not isinstance(call, tuple):
+                inc = 16 if o["sem"] else 1
+                call(q, T).then_inc(T.sem[s], inc)
+                count[s] = count.get(s, 0) + inc
+            elif call[0] == "sendq":
+                via = False
+                for t in range(1, NT):
+                    to = (rank + t) % N
+                    if last_hop(T, topo, rank, to) != core:
+                        via = True
+                if via:
+                    for x in bundle(0):
+                        count[s] = count.get(s, 0) + put(g, T, topo, core, relay, x, x, "rq")
+                for t in range(1, NT):
+                    to = (rank + t) % N
+                    if last_hop(T, topo, rank, to) == core:
+                        for x, y in zip(bundle(t), bundle(0)):
+                            count[s] = count.get(s, 0) + put(g, T, topo, core, T.cores[to], x, y, "aq%d" % t)
+            else:
+                to = (rank + 1) % N
+                if last_hop(T, topo, rank, to) == core:
+                    count[s] = count.get(s, 0) + put(g, T, topo, core, T.cores[to], call[2], call[1], call[3])
+                else:
+                    count[s] = count.get(s, 0) + put(g, T, topo, core, relay, call[1], call[1], call[3])
+        done[k] = (s, count[s], dict(kn))
+    for s, v in sorted(count.items()):
+        e = "y" if s[0] == "s" else "g"
+        queue[e].wait_ge(T.sem[s], v)

@@ -1,116 +1,76 @@
 import numpy as np
-from concourse.mybir import AluOpType as ALU, AxisListType as AX, ActivationFunctionType as AF
+from concourse.mybir import AluOpType as ALU, ActivationFunctionType as AF
 
 NB, NL, NS, NT, TH = 1280, 256, 64, 4, 1250
 NW = NB + 2 * NS * NT
 MUL = 4096
+RB = 4
+REST = 2048
 
 CFG = {
-    "chunks": [128, 128],
-    "order": [[(0, 0), (1, 0), (0, 1), (1, 1), (0, 2), (1, 2)]] * 3,
-    "piece": {"v": 16, "s": 32}, "fv": [0.28, 0.5], "small": "s", "wage": 1000, "sl_age": 0, "misc": "s0", "gt": "v", "cage": 99,
-    "own": False, "half": 64, "lg": "v", "bias": {}, "polish": 30000, "heat": 300.0, "seed": 1, "look": 150.0, "part": 0.4, "short": 320.0, "fvs": {},
-    "sl_after": 0,
-    "nd": 4,
-    "ns": 2,
-    "G": 1.56, "SC": 3.8, "cyc": 1.04, "pe": 0.52, "ov": 20.0, "os": 30.0, "mn": 50, "oi": 45.0, "kf": "v", "lat": 100.0, "hop": 2500.0,
+    "chunks": [96, 96, 64], "ab": 4, "nd": 4, "piece": 24, "half": 64, "early": True,
+    "wage": (1000, 2000), "steal": (1500, 5000), "look": 60.0, "polish": 14000, "heat": 150.0,
+    "ov": 20.0, "os": 30.0, "mn": 50, "oi": 45.0, "hop": 2500.0,
 }
+COSTS = [{"cyc": 0.88, "pe": 0.44, "lat": 160.0, "G": 1.5, "SC": 3.5, "weight": 0.5},
+         {"cyc": 1.2, "pe": 0.6, "lat": 120.0, "G": 1.9, "SC": 5.0, "weight": 0.385}]
 
 
 def layout(cfg):
-    ch = cfg["chunks"]
-    sc = {
-        "chi": ("sbuf", [128, NB], "int32"), "Cw": ("sbuf", [128, NW + 256], "float32"), "K": ("sbuf", [128, NW], "bfloat16"),
-        "psend": ("sbuf", [128, NT * NL], "bfloat16"), "pfin": ("sbuf", [128, NL], "bfloat16"),
-        "hU": ("sbuf", [128, 64], "uint16"), "thr": ("sbuf", [128, 64], "float32"),
-        "ci": ("sbuf", [128, 8], "int32"), "cf": ("sbuf", [128, 16], "float32"),
-        "U": ("sbuf", [128, 144], "float32"), "LY": ("sbuf", [128, 144], "bfloat16"),
-        "SY": ("sbuf", [128, 8], "bfloat16"), "SM": ("sbuf", [128, 8], "bfloat16"), "EM": ("sbuf", [128, 128], "float32"),
-        "RP": ("sbuf", [128, 128], "bfloat16"),
-        "I1": ("sbuf", [128, 128], "bfloat16"), "I2": ("sbuf", [128, 128], "bfloat16"),
-        "G8": ("sbuf", [128, 128], "float32"), "BOf": ("sbuf", [128, 128], "float32"), "BOb": ("sbuf", [128, 128], "bfloat16"),
-        "ones": ("sbuf", [128, 128], "bfloat16"), "R16": ("sbuf", [128, 128], "float32"), "D0": ("sbuf", [128, 128], "float32"),
-        "mk": ("sbuf", [128, 112], "float32"), "C32": ("sbuf", [128, 128], "float32"), "Dq": ("sbuf", [128, 128], "float32"),
-        "Dt": ("sbuf", [128, 256], "float32"),
-        "GT": ("sbuf", [128, 17 * ch[0]], "bfloat16"), "CI": ("sbuf", [128, 16], "float32"), "TG0": ("sbuf", [128, 8], "float32"),
-        "TG": ("sbuf", [128, 16], "float32"), "Dm": ("sbuf", [128, 16], "float32"), "qoff": ("sbuf", [128, 2], "uint16"),
-        "NO": ("sbuf", [128, NT * 128], "float32"), "Z": ("sbuf", [128, 224], "float32"), "X": ("sbuf", [128, 704], "bfloat16"),
-        "sm": ("sbuf", [128, 64], "float32"), "nm": ("sbuf", [128, 8], "float32"), "qsc": ("sbuf", [128, 128], "float32"),
-        "sl": ("sbuf", [128, 4], "bfloat16"), "zi": ("sbuf", [128, 2], "int32"), "zf": ("sbuf", [128, 1], "float32"),
-        "Y": ("sbuf", [128, 384], "float32"), "E2": ("sbuf", [128, 64], "float32"), "sU": ("sbuf", [128, 16], "uint16"),
+    f32, bf, f16, i32, u16 = "float32", "bfloat16", "float16", "int32", "uint16"
+    flat = {
+        "chi": (NB, i32), "Cw": (NW + 256, f32), "K": (NW, bf), "K0": (8, bf), "psend": (NT * NL, bf), "pin": (NT * NL, bf),
+        "hI": (64, i32), "ci": (8, i32), "cf": (16, f32), "U": (128, f32), "G2": (16, f32), "C16": (4, f32), "TB": (16, f32),
+        "SY": (16, bf), "SM": (16, bf), "EM": (128, f32), "I1": (128, bf), "I2": (128, bf), "LA": (128, bf), "LB": (128, bf),
+        "G8": (256, bf), "GQ": (256, bf), "BOb": (128, bf), "BOh": (128, f16), "ones": (128, bf), "R16": (128, f32),
+        "D0": (128, f32), "RS0": (256, f32), "RS1": (256, f32), "OH": (REST + 16, bf),
+        "mk": (112, f32), "C32": (128, f32), "Dq": (128, f32), "Dt": (256, f32), "R2": (128, bf), "DG": (128, bf), "ND": (32, bf),
+        "GT": (16, bf), "E1": (16, bf), "TG0": (8, f32), "TG": (16, f32), "Dm": (16, f32), "qoff": (2, u16),
+        "NO": (NT * 128, f32), "Z": (224, f16), "X": (704, bf), "LG": (512, bf), "sm": (64, f32), "nm": (8, f32), "qsc": (128, f32),
+        "sl": (4, bf), "zi": (2, i32), "zf": (1, f32), "V": (384, f32), "E2": (64, f32), "sU": (16, u16), "jF": (8, f32), "jU": (8, u16),
     }
-    if cfg["misc"] == "misc":
-        sc["misc"] = ("psum", [128, 512], "float32")
-    sc["LT"] = ("sbuf", [128, 16], "float32")
-    sc["R2"] = ("sbuf", [128, 128], "bfloat16")
-    sc["DG"] = ("sbuf", [128, 128], "bfloat16")
-    sc["ND"] = ("sbuf", [128, 32], "bfloat16")
-    sc["LG"] = ("sbuf", [128, 512], "bfloat16")
-    sc["EQ"] = ("sbuf", [128, 16], "float32")
-    sc["K0"] = ("sbuf", [128, 8], "bfloat16")
-    for L in sorted(set(ch)):
-        sc["OH%d" % L] = ("sbuf", [128, 18 * L], "bfloat16")
-        sc["RJ%d" % L] = ("sbuf", [128, L], "bfloat16")
-        sc["RS%d" % L] = ("sbuf", [128, L], "float32")
-        sc["xi%d" % L] = ("sbuf", [128, 8], "int32")
-        sc["xo%d" % L] = ("sbuf", [128, 8], "uint16")
     for t in range(NT):
-        sc["q%d" % t] = ("sbuf", [128, NL], "bfloat16")
-        sc["hb%d" % t] = ("sbuf", [128, 80], "int32")
-    for c, L in enumerate(ch):
-        n = L // 16
-        sc["W%d" % c] = ("sbuf", [128, 5 * 17 * L], "bfloat16")
-        sc["key%d" % c] = ("sbuf", [128, 16 * L], "bfloat16")
-        sc["M%d" % c] = ("sbuf", [128, 16 * L], "bfloat16")
-        sc["kU%d" % c] = ("sbuf", [128, L], "uint16")
-        sc["kF%d" % c] = ("sbuf", [128, 2 * L], "float32")
-        sc["pr%d" % c] = ("sbuf", [128, L], "float32")
-        sc["sc%d" % c] = ("sbuf", [128, L], "float32")
-        sc["m%d" % c] = ("sbuf", [128, L], "float32")
-        sc["ex%d" % c] = ("sbuf", [128, 128], "float32")
-        if L == 64:
-            sc["w2%d" % c] = ("sbuf", [128, n], "float32")
-        sc["wi%d" % c] = ("sbuf", [128, n], "int32")
-        sc["ni%d" % c] = ("sbuf", [128, 3 * n], "int32")
-        sc["nU%d" % c] = ("sbuf", [128, 3 * n], "uint16")
-        sc["vU%d" % c] = ("sbuf", [128, 2 * n], "uint16")
-    nq = 8 - (cfg["misc"] == "misc") - cfg["nd"] - cfg["ns"]
-    for k in range(cfg["nd"]):
-        sc["d%d" % k] = ("psum", [128, 512], "float32")
-    for k in range(cfg["ns"]):
-        sc["s%d" % k] = ("psum", [128, 512], "float32")
-    for k in range(nq):
-        sc["qp%d" % k] = ("psum", [128, 512], "float32")
-    place, share = {}, len(ch) - nq
-    small = [c for c in range(len(ch)) if ch[c] == 64]
-    b = 0
-    while share > 0:
-        place[small.pop(0)] = (b, 0, 256)
-        place[small.pop(-1)] = (b, 256, 256)
-        b += 1
-        share -= 1
-    for c in range(len(ch)):
-        if c not in place:
-            place[c] = (b, 0, 512)
-            b += 1
+        flat["q%d" % t] = (NL, bf)
+        flat["hU%d" % t] = (64, u16)
+        flat["Q%d" % t] = ((RB + 1) * NL, bf)
+    NC = len(cfg["chunks"])
+    for c, L in enumerate(cfg["chunks"]):
+        runs = (RB + 1) * (16 // RB) * L
+        for name, n, ty in (("key", REST + 16, bf), ("kU", L, u16), ("kF", 2 * L, f16), ("pr", L, f16), ("sc", L, f32), ("m", 256, f32),
+                            ("lo", 144, f16), ("nU", 8, u16), ("vU", 16, u16),
+                            ("p", L, bf), ("pd", L, bf), ("Y", runs, bf), ("M", runs, bf)):
+            flat["%s%d" % (name, c)] = (n, ty)
+    sc = {k: ("sbuf", [128, n], ty) for k, (n, ty) in flat.items()}
+    for k in ["d%d" % k for k in range(cfg["nd"])] + ["s%d" % c for c in range(NC)] + (["misc"] if cfg["nd"] + NC < 8 else []):
+        sc[k] = ("psum", [128, 512], f32)
     sems = ["cv", "cs", "ct", "cg", "ls", "rq", "aq1", "aq2", "aq3", "lq", "lh", "lk", "lk0", "lc0", "lc1", "lc2", "lc3", "syc"]
-    for c in range(len(ch)):
+    for c in range(NC):
         sems.append("syp%d" % c)
         for t in range(NT):
             sems.append("ap%d_%d" % (t, c))
-    return sc, sems, place
+    return sc, sems
 
 
-SCRATCH, SEMAPHORES, _PLACE = layout(CFG)
+SCRATCH, SEMAPHORES = layout(CFG)
 
 
 def R(name, a, b, step=1):
     return (name, a, b, step)
 
 
+def B(name, a, b, u, w=None):
+    return ("box", name, a, b, u, w)
+
+
+def IND(win, off):
+    return ("ind", win, off)
+
+
 def cnt(x):
     if x[0] == "ind":
         return 16 * cnt(x[2])
+    if x[0] == "box":
+        return (x[3] - x[2]) * (1 if x[5] is None else x[5] - x[4])
     return len(range(x[1], x[2], x[3]))
 
 
@@ -119,58 +79,58 @@ def ap(T, x):
         return x
     if x[0] == "ind":
         return ap(T, x[1]).indirect(ap(T, x[2]))
+    if x[0] == "box":
+        w = RB + 1
+        return T[x[1]][:, w * x[2] + x[4]:w * x[3]:w] if x[5] is None else T[x[1]][:, w * x[2]:w * x[3]]
+    if len(x) > 4 and x[4] < 128:
+        return T[x[0]][0:x[4], x[1]:x[2]:x[3]]
     if x[3] == 1:
         return T[x[0]][:, x[1]:x[2]]
     return T[x[0]][:, x[1]:x[2]:x[3]]
 
 
-def IND(win, off):
-    return ("ind", win, off)
+def named(x):
+    return named(x[1]) if x[0] == "ind" else x[1] if x[0] == "box" else x[0]
 
 
-def regions(xs):
-    out = []
-    for x in xs:
-        if isinstance(x, tuple):
-            if x[0] == "ind":
-                out += [x[1], x[2]]
-            else:
-                out.append(x)
-    return out
+def area(x):
+    if x[0] == "box":
+        return (x[1], x[2], x[3], x[4], x[4] + 1 if x[5] is None else x[5], True)
+    return (x[0], x[1], x[2], 0, 1, x[3] == 1)
 
 
 def build(cfg):
-    sc, _, place = layout(cfg)
-    ch = cfg["chunks"]
-    G, cyc = cfg["G"], cfg["cyc"]
+    sc, _ = layout(cfg)
+    G, cyc, ch = cfg["G"], cfg["cyc"], cfg["chunks"]
+    NC = len(ch)
     ops, hist, banks, age = [], {}, {}, [99]
 
     def add(eng, cost, reads, writes, calls, sem=None, lat=0.0, after=(), tag=""):
         k = len(ops)
         deps, order = set(after), set()
-        acc = [(x, False) for x in regions(reads)]
-        for x in writes:
-            if x[0] == "ind":
-                acc += [(x[1], True), (x[2], False)]
-            else:
-                acc.append((x, True))
-        for x, w in acc:
-            name = x[0]
+        acc = []
+        for xs, w in ((reads, False), (writes, True)):
+            for x in xs:
+                if isinstance(x, tuple):
+                    if x[0] == "ind":
+                        acc += [(area(x[1])[:5] + (False,), w), (area(x[2]), False)]
+                    else:
+                        acc.append((area(x), w))
+        for (name, a, b, u, v, full), w in acc:
             if name not in sc:
                 continue
             ps = sc[name][0] == "psum"
-            h = hist.setdefault(name, [])
             keep = []
-            for e in h:
-                o, a, b, ow = e
-                if o != k and a < x[2] and x[1] < b and (w or ow):
+            for e in hist.setdefault(name, []):
+                o, a2, b2, u2, v2, ow = e
+                if o != k and a2 < b and a < b2 and u2 < v and u < v2 and (w or ow):
                     if ps and ops[o]["eng"] == eng and eng == "t":
                         order.add(o)
                     else:
                         deps.add(o)
-                if not (w and x[3] == 1 and x[1] <= a and b <= x[2]):
+                if not (w and full and a <= a2 and b2 <= b and u <= u2 and v2 <= v):
                     keep.append(e)
-            keep.append((k, x[1], x[2], w))
+            keep.append((k, a, b, u, v, w))
             hist[name] = keep
             if ps:
                 st = banks.setdefault(name, [None, [], []])
@@ -183,28 +143,27 @@ def build(cfg):
                     st[1].append(k)
         deps.discard(k)
         ops.append({"eng": eng, "cost": cost, "deps": deps, "order": order - deps, "calls": calls, "sem": sem, "lat": lat, "tag": tag,
-                    "alt": None, "swap": None, "age": age[0]})
+                    "swap": None, "age": age[0]})
         return k
 
     def two(*xs):
-        return all(sc[(x[1] if x[0] == "ind" else x)[0]][2] in ("bfloat16", "uint16") for x in xs)
+        return all(sc[named(x)][2] in ("bfloat16", "float16", "uint16") for x in xs)
 
     def vcost(n, rate):
         return cfg["ov"] + max(n * rate, cfg["mn"]) * cyc + (cfg["oi"] if rate in (G, cfg["SC"]) else 0)
 
+    def scost(a):
+        return cfg["os"] + (cnt(a) * cyc * G + cfg["oi"] if a[0] == "ind" else max(cnt(a), cfg["mn"]) * cyc)
+
     def rate(out, a, plain):
-        if a[0] == "ind":
-            return G
-        if out[0] == "ind":
-            return cfg["SC"]
-        return plain
+        return G if a[0] == "ind" else cfg["SC"] if out[0] == "ind" else plain
 
     def copy(out, a, tag=""):
         return add("v", vcost(cnt(a), rate(out, a, 0.5 if two(out, a) else 1)), [a], [out],
                    [lambda q, T: q.tensor_copy(ap(T, out), ap(T, a))], tag=tag)
 
     def tt(out, a, b, op, tag=""):
-        ps = any(x[0] != "ind" and sc[x[0]][0] == "psum" for x in (a, b))
+        ps = any(sc[named(x)][0] == "psum" for x in (a, b))
         return add("v", vcost(cnt(a), rate(out, a, 1 if ps else 2)), [a, b], [out],
                    [lambda q, T: q.tensor_tensor(ap(T, out), ap(T, a), ap(T, b), op)], tag=tag)
 
@@ -218,12 +177,9 @@ def build(cfg):
     def mset(out, val):
         return add("v", vcost(cnt(out), 0.5 if two(out) else 1), [], [out], [lambda q, T: q.memset(ap(T, out), val)])
 
-    def scan(out, d0, d1, op1, tag=""):
-        return add("v", vcost(cnt(d1), 1), [d0, d1], [out],
-                   [lambda q, T: q.tensor_tensor_scan(ap(T, out), ap(T, d0), ap(T, d1), 0.0, ALU.add, op1)], tag=tag)
-
-    def rmin(out, a):
-        return add("v", vcost(cnt(a), 1), [a], [out], [lambda q, T: q.tensor_reduce(ap(T, out), ap(T, a), AX.X, ALU.min)], tag="red")
+    def scan(out, d0, d1, op0, op1, tag=""):
+        return add("v", vcost(cnt(d1), 0.5 if two(out, d0, d1) else 1), [d0, d1], [out],
+                   [lambda q, T: q.tensor_tensor_scan(ap(T, out), ap(T, d0), ap(T, d1), 0.0, op0, op1)], tag=tag)
 
     def act(out, a, func, tag="", scale=None, bias=None):
         if scale is not None:
@@ -232,31 +188,39 @@ def build(cfg):
             f = lambda q, T: q.activation(ap(T, out), ap(T, a), func, bias=ap(T, bias))
         else:
             f = lambda q, T: q.activation(ap(T, out), ap(T, a), func)
-        return add("s", cfg["os"] + (cnt(a) * cyc * G + cfg["oi"] if a[0] == "ind" else max(cnt(a), cfg["mn"]) * cyc),
-                   [a, scale, bias], [out], [f], tag=tag)
+        return add("s", scost(a), [a, scale, bias], [out], [f], tag=tag)
 
-    def gather(eng, out, a, tag=""):
-        eng = cfg["small"] if eng == "x" else eng
+    def either(eng, out, a, tag=""):
         k = act(out, a, AF.Copy, tag)
         ops[k]["swap"] = {"s": (ops[k]["cost"], ops[k]["calls"]),
-                          "v": (vcost(cnt(a), G), [lambda q, T: q.tensor_copy(ap(T, out), ap(T, a))])}
+                          "v": (vcost(cnt(a), rate(out, a, 0.5 if two(out, a) else 1)), [lambda q, T: q.tensor_copy(ap(T, out), ap(T, a))])}
         ops[k]["eng"] = eng
         ops[k]["cost"], ops[k]["calls"] = ops[k]["swap"][eng]
+        return k
+
+    def affine(out, a, scale, bias, tag=""):
+        k = ts(out, a, scale, ALU.mult, bias, ALU.add, tag)
+        ops[k]["swap"] = {"v": (ops[k]["cost"], ops[k]["calls"]),
+                          "s": (scost(a), [lambda q, T: q.activation(ap(T, out), ap(T, a), AF.Identity, bias=ap(T, bias), scale=ap(T, scale))])}
         return k
 
     def mm(lst, tag=""):
         cost, calls = 0.0, []
         for (o, l, r, st, sp) in lst:
-            cost += max(64, cnt(r)) * cfg["pe"] * (4 if sc[l[0]][2] == "float32" else 1)
+            cost += max(64, cnt(r)) * cfg["pe"] * (4 if sc[named(l)][2] == "float32" else 1)
             calls.append(lambda q, T, o=o, l=l, r=r, st=st, sp=sp: q.matmul(ap(T, o), ap(T, l), ap(T, r), st, sp))
         return add("t", cost, [x[1] for x in lst] + [x[2] for x in lst], [x[0] for x in lst], calls, lat=60.0, tag=tag)
 
     def iota(out, pat, base, cm=0):
-        if sc[out[0]][2] == "int32":
+        if sc[named(out)][2] == "int32":
             f = lambda q, T: q.iota(ap(T, out), pat, base, cm)
         else:
             f = lambda q, T: q.iota(ap(T, out), pat, base, cm, allow_small_or_imprecise_dtypes=True)
         return add("g", 160 + 2 * cyc * cnt(out), [], [out], [f])
+
+    def gcopy(out, a, after=()):
+        return add("g", 210 + 2 * cyc * cnt(a), [a], [out],
+                   [lambda q, T: q.affine_select(ap(T, out), ap(T, a), [[0, cnt(a)]], ALU.is_ge, 0.0, 0, 0)], after=after, tag="rep")
 
     def dma(eng, out, a, sem, lat):
         return add(eng, 60.0, [a], [out], [lambda q, T: q.dma_start(ap(T, out), ap(T, a))], sem=sem, lat=lat, tag="dma")
@@ -267,7 +231,7 @@ def build(cfg):
     def whole(n):
         return R(n, 0, sc[n][1][1])
 
-    dma("y", R("hb0", 0, 64), R("hv", 0, 64), "lh", 2000)
+    dma("y", whole("hI"), R("hv", 0, 64), "lh", 2000)
     for k in range(4):
         dma("y", R("chi", 320 * k, 320 * k + 320), R("ch", 320 * k, 320 * k + 320), "lc%d" % k, 2300 + 500 * k)
     dma("s", whole("q0"), R("qs", 0, NL), "lq", 2000)
@@ -276,60 +240,53 @@ def build(cfg):
 
     iota(R("ci", 0, 1), [[0, 1]], 0, 1)
     iota(col(3), [[0, 1]], 0, 1)
-    iota(whole("U"), [[1, 144]], 0)
+    iota(whole("U"), [[1, 128]], 0)
+    iota(whole("R16"), [[0, 8], [1, 16]], 0)
     ts(R("ci", 1, 2), R("ci", 0, 1), 15, ALU.bitwise_and)
     ts(R("ci", 2, 3), R("ci", 0, 1), 4, ALU.arith_shift_right)
     ts(R("ci", 3, 4), R("ci", 0, 1), 14, ALU.bitwise_and)
     ts(R("ci", 4, 5), R("ci", 0, 1), 3, ALU.bitwise_and)
-    copy(R("cf", 0, 2), R("ci", 1, 3))
-    ts(col(2), R("ci", 2, 3), 16, ALU.mult, 15, ALU.add)
-    ts(col(4), R("ci", 1, 2), -2048, ALU.mult, 15 * 2048, ALU.add)
-    ts(col(5), R("ci", 3, 4), 2, ALU.mult)
-    ts(col(6), R("ci", 3, 4), -2 ** 20, ALU.mult, 28 * 2 ** 19, ALU.add)
-    ts(col(10), R("ci", 3, 4), 2 ** 20, ALU.mult, -28 * 2 ** 19, ALU.add)
-    ts(col(7), R("ci", 3, 4), 2, ALU.mult, 3, ALU.add)
-    ts(col(8), R("ci", 1, 2), 2, ALU.mult)
+    copy(R("cf", 0, 3), R("ci", 1, 4))
+    affine(col(4), col(0), -2048.0, 15 * 2048.0)
+    affine(col(5), col(2), 2.0, 0.0)
+    affine(col(6), col(2), -2.0 ** 20, 28 * 2.0 ** 19)
+    affine(col(10), col(2), 2.0 ** 20, -28 * 2.0 ** 19)
+    affine(col(7), col(2), 2.0, 3.0)
+    affine(col(8), col(0), 2.0, 0.0)
+    affine(col(9), col(0), -1.0, 0.0)
+    affine(col(11), col(0), 1.0, -1.0)
+    affine(col(15), col(0), 16.0, 0.0)
+    ts(R("cf", 12, 14), R("U", 0, 2), col(3), ALU.is_equal)
+    affine(col(14), col(12), 16.0, 0.0)
     ts(R("qoff", 0, 1), R("ci", 4, 5), 32, ALU.mult, 31, ALU.add)
-    ts(whole("I1"), R("U", 0, 128), col(3), ALU.is_equal)
-    ts(whole("I2"), R("U", 0, 128), col(3), ALU.is_equal, -1.0, ALU.mult)
-    ts(whole("LY"), whole("U"), col(2), ALU.is_equal, float(MUL), ALU.mult)
-    first = [sum(ch[:c]) for c in range(len(ch))]
-    for c, L in enumerate(ch):
-        iota(R("CI", first[c] // 16, (first[c] + L) // 16), [[16, L // 16]], MUL * TH + 16 * L)
-        mset(R("W%d" % c, 16 * L, 17 * L), 0.0)
-    ts(whole("CI"), whole("CI"), col(0), ALU.add)
-    for L in sorted(set(ch)):
-        iota(whole("RJ%d" % L), [[0, 8], [128, L // 8]], 0)
-        mset(whole("RS%d" % L), 0.0)
-        mset(R("RS%d" % L, 0, L, L // 8), float(2 ** 28))
-        iota(whole("xi%d" % L), [[L // 8, 8]], L // 8 - 1)
-        copy(whole("xo%d" % L), whole("xi%d" % L))
-    iota(whole("RP"), [[0, 128]], 0, 1)
-    iota(whole("G8"), [[1, 8], [0, 16]], 0)
-    ts(whole("BOf"), whole("G8"), col(1), ALU.is_equal)
-    ts(whole("BOb"), whole("G8"), col(1), ALU.is_equal, 2048.0, ALU.mult)
-    mset(whole("ones"), 1.0)
-    iota(whole("R16"), [[0, 8], [1, 16]], 0)
-    age[0] = 0
+    ts(whole("I1"), whole("U"), col(3), ALU.is_equal)
+    affine(whole("I2"), whole("I1"), -1.0, 0.0)
+    affine(whole("LA"), whole("U"), col(12), col(13))
+    affine(whole("LB"), whole("R16"), col(13), col(14))
+    for u in range(2):
+        iota(whole("RS%d" % u), [[0, 256]], 0)
+    iota(whole("TB"), [[REST, 2], [0, 8]], MUL * TH)
+    iota(whole("G8"), [[0, 2], [1, 8], [0, 16]], 0)
+    ts(whole("GQ"), whole("G8"), col(1), ALU.is_equal, float(MUL), ALU.mult)
+    ts(whole("BOh"), R("G8", 0, 128), col(1), ALU.is_equal)
+    affine(whole("BOb"), R("GQ", 0, 128), 0.5, 0.0)
+    iota(whole("ones"), [[0, 128]], 1)
     ts(whole("EM"), whole("R16"), col(0), ALU.is_equal)
-    ts(whole("LT"), R("U", 0, 16), col(0), ALU.is_lt)
-    ts(whole("EQ"), R("U", 0, 16), col(0), ALU.is_equal)
-    for L in sorted(set(ch)):
-        mset(R("OH%d" % L, 16 * L, 18 * L), 0.0)
-        for u in range(16):
-            act(R("OH%d" % L, u * L, u * L + L), R("ones", 0, L), AF.Copy, tag="tab", scale=R("EQ", u, u + 1))
-    L = ch[0]
-    mset(R("GT", 15 * L, 17 * L), 0.0)
-    for u in range(15):
-        if cfg["gt"] == "s":
-            act(R("GT", u * L, u * L + L), R("ones", 0, L), AF.Copy, tag="tab", scale=R("LT", u, u + 1))
-        else:
-            ts(R("GT", u * L, u * L + L), R("ones", 0, L), R("LT", u, u + 1), ALU.mult)
-    age[0] = cfg["cage"]
-    ts(whole("SY"), R("U", 0, 8), col(1), ALU.is_equal, float(MUL), ALU.mult)
-    ts(whole("SM"), R("U", 0, 8), col(1), ALU.is_equal, -2.0 * MUL, ALU.mult)
-    ts(whole("D0"), whole("EM"), 65536.0 + 2048.0, ALU.mult, -2048.0, ALU.add)
-    ts(col(9), R("ci", 1, 2), -1, ALU.mult)
+    either("s", R("OH", 0, 128), whole("EM"))
+    for w in (128, 256, 512, 1024):
+        if w < 16 * max(ch):
+            act(R("OH", w, 2 * w), R("OH", 0, w), AF.Copy, "tab")
+    iota(R("OH", REST, REST + 16), [[0, 16]], 0)
+    for c in range(NC):
+        iota(R("key%d" % c, 16 * ch[c], REST + 16), [[0, REST + 16 - 16 * ch[c]]], 0)
+        iota(B("Y%d" % c, 0, 16 // RB * ch[c], RB), [[0, 16 // RB * ch[c]]], 0)
+        mset(whole("lo%d" % c), 0.0)
+    either("v", whole("SY"), R("GQ", 0, 256, 16))
+    affine(whole("SM"), R("GQ", 0, 256, 16), -2.0, 0.0)
+    affine(whole("D0"), whole("EM"), 65536.0 + 2048.0, -2048.0)
+    affine(whole("C16"), R("U", 0, 4), 256.0, col(15))
+    ts(whole("GT"), R("U", 0, 16), col(0), ALU.is_lt)
+    ts(whole("E1"), R("U", 0, 16), col(11), ALU.is_equal)
     act(whole("mk"), R("R16", 0, 112), AF.Sign, bias=col(9))
     iota(R("mk", 16, 64), [[0, 48]], 1)
     iota(whole("C32"), [[0, 4], [1, 32]], 0)
@@ -341,139 +298,143 @@ def build(cfg):
     ts(R("Dt", 128, 256), whole("C32"), col(7), ALU.is_gt, float(2 ** 19), ALU.mult)
     tt(R("Dt", 0, 128), R("Dt", 0, 128), R("Dt", 128, 256), ALU.add)
     tt(whole("Dq"), whole("Dq"), R("Dt", 0, 128), ALU.add)
-    iota(whole("TG0"), [[1, 2], [32, 4]], NB)
-    iota(whole("Dm"), [[16, 16]], NW)
-    ts(whole("Dm"), whole("Dm"), col(0), ALU.add)
+    iota(whole("TG0"), [[1, 2], [32, 4]], 0)
+    affine(whole("TG0"), whole("TG0"), 1.0, col(8))
+    iota(whole("Dm"), [[128 + NB, 2], [16, 8]], NW - NB)
+    affine(whole("Dm"), whole("Dm"), 1.0, col(0))
     for t in range(NT):
         iota(R("NO", 128 * t, 128 * t + 64), [[-2, 64]], -(NB + 128 * t + 1))
         iota(R("NO", 128 * t + 64, 128 * t + 128), [[4, 32], [-2, 2]], NB + 128 * t + 2)
 
     iota(R("Cw", NB, NW + 256), [[0, NW + 256 - NB]], 0)
-    iota(R("Y", 64, 128), [[0, 64]], 0)
+    iota(R("V", 64, 128), [[0, 64]], 0)
     mset(R("Cw", 0, 1), 0.0)
     for k in range(4):
         a = max(1, 320 * k)
         copy(R("Cw", a, 320 * k + 320), R("chi", a, 320 * k + 320))
-    mset(R("K", 0, 1), 2048.0)
+    mset(R("K", 0, 1), -2048.0)
     copy(R("K", 1, 8), R("K0", 1, 8))
+    for u in range(RB + 1):
+        gcopy(B("Q0", 0, NL, u), whole("q0"))
 
-    misc = cfg["misc"]
-    mm([(R(misc, 336, 352), R("LY", 15 - r, 143 - r), R("q0", r, NL, 16), r == 0, r == 15) for r in range(16)])
-    tt(R("hb0", 64, 80), whole("CI"), R(misc, 336, 352), ALU.subtract)
-    k = add("g", 3000.0, [whole("q0"), whole("hb0")], [], [("sendq",)], sem="ls")
+    misc = "misc" if "misc" in sc else "s0"
+    copy(whole("hU0"), whole("hI"))
+    k = add("g", 3000.0, [whole("q0"), whole("hU0")], [], [("sendq",)], sem="ls")
     for t in range(1, NT):
-        add("n", 0.0, [], [whole("q%d" % t), whole("hb%d" % t)], [], sem="aq%d" % t, lat=3 * cfg["hop"], after=[k])
+        add("n", 0.0, [], [whole("q%d" % t), whole("hU%d" % t)], [], sem="aq%d" % t, lat=3 * cfg["hop"], after=[k])
 
-    turn = [0, 0]
+    turn, sent = [0], []
 
     def step(t, c, s):
-        L, f0 = ch[c], first[c]
-        n = L // 16
-        Wn, key, M = "W%d" % c, "key%d" % c, "M%d" % c
-        w = 17 * L * (4 if s == 1 else t)
-        wn = 17 * L * (4 if s == 0 else t)
+        L, f0 = ch[c], sum(ch[:c])
+        NH = L // 16
+        key, Y, M, S = "key%d" % c, "Y%d" % c, "M%d" % c, "s%d" % c
+        kU, own = "kU%d" % c, whole("p%d" % c)
+        p = R("pin", NL * (t - 1) + f0, NL * (t - 1) + f0 + L) if s == 0 else own
+        plain = t + s == 0
         base = NB + 128 * t
-        voff = R("hU", 16 * t + f0 // 16, 16 * t + f0 // 16 + n) if s == 0 else R("vU%d" % c, (s - 1) * n, s * n)
-        kids = IND(whole("chi") if t + s == 0 and cfg["kf"] == "v" else R("Cw", 0, NW), voff)
-        copy(whole("kU%d" % c), kids, "gC")
-        if s == 2 and c == 0:
-            copy(R("Y", 320, 384), R("kU0", 0, 64), "gCf")
-        elif s < 2:
-            if cfg["kf"] == "v":
-                copy(R("kF%d" % c, s * L, s * L + L), whole("kU%d" % c), "gCf")
-            else:
-                gather("s", R("kF%d" % c, s * L, s * L + L), kids, "gCf")
-        cut = cfg["fvs"].get(age[0], 2 * int(round(L * cfg["fv"][s == 0 and c == 0] / 2)))
-        for eng, a0, b0 in (("v", 0, cut), ("s", cut, L)):
-            m = -(-(b0 - a0) // cfg["piece"][eng])
-            for u in range(m):
-                a, b = a0 + 2 * ((b0 - a0) // 2 * u // m), a0 + 2 * ((b0 - a0) // 2 * (u + 1) // m)
-                gather(eng, R(key, 16 * a, 16 * b), IND(R("K", 0, base), R("kU%d" % c, a, b)), "gK")
-        qb, qa, qw = place[c]
-        if s == 0:
-            mm([(R("qp%d" % qb, qa + u, qa + u + L), whole("I1"), R("q%d" % t, f0, f0 + L), True, True) for u in range(0, qw, L)], "q")
-        per, J = 512 // L, L // 8
-        S = "s%d" % ((c if cfg["ns"] >= len(ch) else turn[1]) % cfg["ns"])
-        turn[1] += 1
-        mm([(R(S, 0, L), whole("I1"), whole("RJ%d" % L), True, False), (R(S, 0, L), whole("I1"), R("RP", 0, L), False, False)], "low")
-        p = R(Wn, w + 16 * L, w + 17 * L)
-        for j0 in range(0, 16, per):
-            d = "d%d" % (2 * c + turn[0] % 2 if cfg["own"] else turn[0] % cfg["nd"])
-            turn[0] += 1
-            h = cfg["half"]
-            for i0 in range(0, L, h):
-                lst, i1 = [], min(L, i0 + h)
-                for u in range(per):
-                    o = R(d, u * L + i0, u * L + i1)
-                    alone = t == 0 and s == 0
-                    lst.append((o, whole("I1"), R(key, 16 * i0 + j0 + u, 16 * i1, 16), True, alone))
-                    if not alone:
-                        lst.append((o, whole("I2"), R(Wn, p[1] + i0, p[1] + i1), False, True))
-                mm(lst, "d")
-            act(R(Wn, w + j0 * L, w + j0 * L + 512), whole(d), AF.Abs, "abs")
-            for u in range(0, 512, qw):
-                a = j0 * L + u
-                tt(R(M, a, a + qw), R(Wn, w + a, w + a + qw), R("qp%d" % qb, qa, qa + qw), ALU.min, "min")
-            tiles = range(j0 * L // 128, j0 * L // 128 + 4)
-            mm([(R(S, u, L, J), R(Wn, w + 128 * u, w + 128 * u + 128), whole("SY"), False, False) for u in tiles]
-               + [(R(S, u, L, J), R(M, 128 * u, 128 * u + 128), whole("SM"), False, u == J - 1) for u in tiles], "sum")
-        scan(whole("m%d" % c), whole("RS%d" % L), R(S, 0, L), ALU.min, "amin")
-        tt(whole("ex%d" % c), IND(whole("m%d" % c), whole("xo%d" % L)), whole("EM"), ALU.mult, "ex")
-        mm([(R(S, 256, 264), whole("ex%d" % c), R("BOf", 0, 128, 16), True, True)], "exm")
-        bound = R("thr", 16 * t + f0 // 16, 16 * t + f0 // 16 + n)
-        if L == 64:
-            tt(whole("w2%d" % c), R(S, 260, 264), bound, ALU.min, "A0")
-            bound = whole("w2%d" % c)
-        tt(whole("wi%d" % c), R(S, 256, 256 + n), bound, ALU.min, "A")
-        ni, nU = R("ni%d" % c, s * n, s * n + n), R("nU%d" % c, s * n, s * n + n)
-        ts(ni, whole("wi%d" % c), MUL - 1, ALU.bitwise_and, tag="B")
-        copy(nU, ni, "C")
+        voff = R("hU%d" % t, 16 * t + f0 // 16, 16 * t + f0 // 16 + NH) if s == 0 else R("vU%d" % c, (s - 1) * 8, (s - 1) * 8 + NH)
+        copy(whole(kU), IND(whole("chi") if plain else R("Cw", 0, NB if s == 0 else NW), voff), "gC")
+        kF = R("kF%d" % c, s * L, s * L + L)
         if s < 2:
-            gather("x", R(Wn, wn + 16 * L, wn + 17 * L), IND(R(Wn, w, w + 17 * L), nU), "gp")
-            pr = "pr%d" % c
-            tt(whole(pr), IND(R("OH%d" % L, 0, 17 * L), nU), R("kF%d" % c, s * L, s * L + L), ALU.mult, "oh")
-            lst = [(R(S, 272, 272 + L), whole("BOf"), whole(pr), True, True)]
-            if c == 0:
-                if L > 64:
-                    lst.append((R(S, 272 + L, 272 + L + 64), whole("BOf"), R(pr, 0, 64), True, True))
-                z = 272 if L == 64 else 272 + L
-                lst.append((R(S, z + 64, z + 112), whole("BOf"), R(pr, 16, 64), True, True))
-            mm(lst, "vrep")
-            scan(whole("sc%d" % c), R("D0", 0, L), R(S, 272, 272 + L), ALU.min, "scan")
-            ts(R("vU%d" % c, s * n, s * n + n), R("sc%d" % c, 15, L, 16), col(4), ALU.add, tag="cvt")
-            if c == 0:
-                tt(R("Z", s, 224, 2), R(S, z, z + 112), whole("mk"), ALU.mult)
-                act(R("TG", 8 + 4 * s, 12 + 4 * s), R("sc0", 15, 64, 16), AF.Identity, bias=col(4))
-                if t < NT - 1:
-                    gather("x", R("K", base + s, base + 128, 2), IND(R("K", 0, base), R("vU0", n * s, n * s + 4)))
+            copy(kF, whole(kU), "gCf")
+        elif c == 0:
+            copy(R("V", 320, 384), R(kU, 0, NS), "gCf")
+        m = -(-L // cfg["piece"])
+        for u in range(m):
+            a, b = 2 * (L // 2 * u // m), 2 * (L // 2 * (u + 1) // m)
+            either("s", R(key, 16 * a, 16 * b), IND(R("K", 0, base), R(kU, a, b)), "gK")
+        mm([(R(S, 0, 256) + (L,), R("q%d" % t, f0, f0 + L), whole("GQ"), True, False)], "low")
+
+        def sums(src, weight, blocks, slots, last):
+            lst = [(R(S, RB * b + u, 256, 16) + (L,), B(src, L * b, L * b + L, u), whole(weight), False, False) for b in blocks for u in slots]
+            mm(lst + [(R(S, 128, 256) + (L,), R("LA", 0, L), whole("LB"), False, True)] * last, "sum")
+
+        ab = cfg["ab"]
+        fit = 512 // (ab * L)
+        halves = [(0, L)] if L < 2 * cfg["half"] else [(0, L // 2), (L // 2, L)]
+        for b0 in range(0, 16 // RB, ab):
+            blocks = range(b0, b0 + ab)
+            for u0 in range(0, RB, fit):
+                slots = range(u0, min(u0 + fit, RB))
+                if plain:
+                    for u in slots:
+                        for b in blocks:
+                            either("v", B(Y, L * b, L * b + L, u), R(key, RB * b + u, 16 * L, 16), "abs")
+                else:
+                    d = "d%d" % (turn[0] % cfg["nd"])
+                    turn[0] += 1
+                    rows = [RB * b + u for u in slots for b in blocks]
+                    parts = [[(R(d, L * n + i0, L * n + i1), whole("I1"), R(key, 16 * i0 + j, 16 * i1, 16)) for n, j in enumerate(rows)]
+                             for i0, i1 in halves]
+                    minus = [(R(d, L * n, L * n + L), whole("I2"), p) for n in range(len(rows))]
+                    parts = [minus] + parts if s > 0 and cfg["early"] else parts + [minus]
+                    for n, part in enumerate(parts):
+                        mm([x + (n + u == 0, n == len(parts) - 1 and u == len(part) - 1) for u, x in enumerate(part)], "d")
+                    for n, u in enumerate(slots):
+                        act(B(Y, L * b0, L * (b0 + ab), u), R(d, ab * L * n, ab * L * (n + 1)), AF.Abs, "abs")
+                sums(Y, "SY", blocks, slots, False)
+            for b in blocks:
+                scan(B(M, L * b, L * b + L, 0, RB + 1), B("Q%d" % t, f0, f0 + L, 0, RB + 1), B(Y, L * b, L * b + L, 0, RB + 1),
+                     ALU.max, ALU.min, "min")
+                sums(M, "SM", [b], range(RB), b == 16 // RB - 1)
+        m, lo = "m%d" % c, "lo%d" % c
+        scan(whole(m) + (L,), whole("RS%d" % (t % 2)) + (L,), R(S, 0, 256) + (L,), ALU.max, ALU.min, "amin")
+        tt(R(lo, 15, 143, 16) + (L,), R(m, 143, 256, 16) + (L,), R(m, 15, 128, 16) + (L,), ALU.subtract, "ex")
+        mm([(R(S, 256, 256 + NH), R(lo, 15 - r, 143 - r), R("I1", r, L, 16), r == 0, r == 15) for r in range(16)], "exm")
+        nU = R("nU%d" % c, 0, NH)
+        copy(nU, R(S, 256, 256 + NH), "C")
+        if c == 0 and s > 0:
+            tt(R("jF", 4 * s - 4, 4 * s), R(S, 256, 260), whole("C16"), ALU.subtract, "pre")
+        new = own if s < 2 else R("psend", NL * t + f0, NL * t + f0 + L)
+        if plain:
+            either("s", new, IND(whole(key), nU), "gp")
+        elif cfg.get("gp") == "pe" or (cfg.get("gp") == "pe2" and s < 2):
+            either("s", whole("pd%d" % c), IND(whole(key), nU), "gp")
+            mm([(R(misc, 0, L), whole("I1"), whole("pd%d" % c), True, False), (R(misc, 0, L), whole("I2"), p, False, True)], "gp")
+            act(new, R(misc, 0, L), AF.Abs, "gp")
         else:
-            src = R("psend", NL * t + f0, NL * t + f0 + L)
-            dst = R(Wn, 17 * L * (t + 1) + 16 * L, 17 * L * (t + 2)) if t < NT - 1 else R("pfin", f0, f0 + L)
-            gather("x", src, IND(R(Wn, w, w + 17 * L), nU), "gp")
-            k = add("g", 300.0, [src], [], [("sendp", src, dst, "ap%d_%d" % (t, c))], sem="ls")
+            tt(whole("pd%d" % c), IND(whole(key), nU), p, ALU.subtract, "gp")
+            act(new, whole("pd%d" % c), AF.Abs, "gp")
+        if s < 2:
+            pr, vU = "pr%d" % c, R("vU%d" % c, s * 8, s * 8 + NH)
+            tt(whole(pr), IND(whole("OH"), nU), kF, ALU.mult, "oh")
+            lst = [(R(S, 272, 272 + L), whole("BOh"), whole(pr), True, True)]
+            if c == 0:
+                lst.append((R(S, 400, 464), whole("BOh"), R(pr, 0, 64), True, True))
+                lst.append((R(S, 464, 512), whole("BOh"), R(pr, 16, 64), True, True))
+            mm(lst, "vrep")
+            scan(whole("sc%d" % c), R("D0", 0, L), R(S, 272, 272 + L), ALU.add, ALU.min, "scan")
+            ts(vU, R("sc%d" % c, 15, L, 16), col(4), ALU.add, tag="cvt")
+            if c == 0:
+                tt(R("Z", s, 224, 2), R(S, 400, 512), whole("mk"), ALU.mult)
+                affine(R("TG", 8 + 4 * s, 12 + 4 * s), R("sc0", 15, 64, 16), 1.0, col(4))
+                if t < NT - 1:
+                    either("s", R("K", base + s, base + 128, 2), IND(R("K", 0, base), R("vU0", 8 * s, 8 * s + 4)))
+        else:
+            dst = R("pin", NL * t + f0, NL * t + f0 + L)
+            k = add("g", 300.0, [new], [], [("sendp", new, dst, "ap%d_%d" % (t, c))], sem="ls")
+            sent.append(k)
             add("n", 0.0, [], [dst], [], sem="ap%d_%d" % (t, c), lat=2 * cfg["hop"], after=[k])
             if t == NT - 1:
                 dma("y", R("yp", f0, f0 + L), dst, "syp%d" % c, 2200)
 
     def slices(t):
-        ts(R("TG", 0, 8), whole("TG0"), col(8), ALU.add, float(128 * t), ALU.add)
+        affine(R("TG", 0, 8), whole("TG0"), 1.0, float(128 * t))
         tt(R("sm", 0, 4), R("TG", 8, 12), R("TG", 12, 16), ALU.not_equal)
-        L = ch[0]
-        n = L // 16
-        ts(R("sm", 4, 8), R("ni0", n, n + 4), 15 * L, ALU.is_lt, tag="pre")
+        for u in range(2):
+            ts(R("jU", 4 * u, 4 * u + 4), R("jF", 4 * u, 4 * u + 4), 15.0, ALU.min, tag="pre")
+        ts(R("sm", 4, 8), R("jF", 0, 4), 15.0, ALU.is_lt, tag="pre")
         tt(R("sm", 8, 12), R("sm", 0, 4), R("sm", 4, 8), ALU.mult, "pre")
         for u in range(2):
             tt(R("nm", 4 * u, 4 * u + 4), R("TG", 8 + 4 * u, 12 + 4 * u), R("sm", 8, 12), ALU.mult, "pre")
-        act(R("sm", 16, 32), whole("TG"), AF.Identity, "pre", bias=col(10))
-        tt(R("sm", 12, 16), R("wi0", 0, 4), R("thr", 16 * t, 16 * t + 4), ALU.is_lt, "go")
+        affine(R("sm", 16, 32), whole("TG"), 1.0, col(10), "pre")
+        ts(R("sm", 12, 16), R("jF", 4, 8), 16.0, ALU.is_lt, tag="go")
         seg = [(0, 128, [(0, 128, 0)]), (64, 160, [(0, 64, 64), (64, 96, 32)]), (96, 192, [(0, 32, 96), (64, 96, 64)]), (192, 224, [(0, 32, 96)])]
         lst, x = [(R(misc, 256, 384), whole("BOb"), whole("DG"), True, False)], 0
         for c, (a, b, parts) in enumerate(seg):
             lg = R("LG", 128 * c, 128 * c + 128)
-            if cfg["lg"] == "v":
-                ts(lg, whole("BOb"), R("sm", 12 + c, 13 + c), ALU.mult, tag="go")
-            else:
-                act(lg, whole("BOb"), AF.Copy, "go", scale=R("sm", 12 + c, 13 + c))
+            affine(lg, whole("BOb"), R("sm", 12 + c, 13 + c), 0.0, "go")
             lst.append((R(misc, 256 + 32 * c, 288 + 32 * c), lg, whole("ND"), False, False))
             for u in range(2):
                 ts(R("X", x, x + b - a), R("Z", a, b), R("nm", 4 * u + c, 4 * u + c + 1), ALU.is_equal, tag="cmp")
@@ -481,16 +442,16 @@ def build(cfg):
                     lst.append((R(misc, 256 + to, 256 + to + i1 - i0), lg, R("X", x + i0, x + i1), False, c == 3 and u == 1))
                 x += b - a
         mm(lst, "cnt")
-        scan(whole("qsc"), whole("Dq"), R(misc, 256, 384), ALU.max, "post")
+        scan(whole("qsc"), whole("Dq"), R(misc, 256, 384), ALU.add, ALU.max, "post")
         tt(R("sm", 32, 48), IND(whole("qsc"), R("qoff", 0, 1)), R("sm", 16, 32), ALU.add, "post")
         tt(R("sm", 48, 64), R("sm", 32, 48), whole("Dm"), ALU.min, "post")
         copy(whole("sU"), R("sm", 48, 64), "post")
-        ra, rb = R("kF0", L, L + 64), R("Y", 320, 384)
-        for u, old in enumerate((ra, rb)):
-            tt(R("Y", 128 + 64 * u, 192 + 64 * u), IND(whole("GT"), R("nU0", n * (u + 1), n * (u + 1) + 4)), old, ALU.mult, "v4")
-        tt(R("Y", 0, 64), IND(R("OH%d" % L, 0, 17 * L), R("nU0", n, n + 4)), R("NO", 128 * t, 128 * t + 64), ALU.mult, "v4")
-        tt(whole("E2"), IND(R("OH%d" % L, L, 18 * L), R("nU0", n, n + 4)), R("NO", 128 * t + 64, 128 * t + 128), ALU.mult, "v4")
-        tt(R("Y", 256, 320), whole("E2"), ra, ALU.add, "v4")
+        ra, rb, jj, kk = R("kF0", ch[0], ch[0] + NS), R("V", 320, 384), R("jU", 0, 4), R("jU", 4, 8)
+        tt(R("V", 128, 192), IND(whole("GT"), jj), ra, ALU.mult, "v4")
+        tt(R("V", 192, 256), IND(whole("GT"), kk), rb, ALU.mult, "v4")
+        tt(R("V", 0, 64), IND(R("OH", 0, 16), jj), R("NO", 128 * t, 128 * t + 64), ALU.mult, "v4")
+        tt(whole("E2"), IND(whole("E1"), jj), R("NO", 128 * t + 64, 128 * t + 128), ALU.mult, "v4")
+        tt(R("V", 256, 320), whole("E2"), ra, ALU.add, "v4")
         if t < NT - 1:
             ts(whole("sl"), R("qsc", 31, 128, 32), col(6), ALU.is_equal)
             mm([(R(misc, 384, 385), whole("ones"), R("sl", u, u + 1), u == 0, u == 3) for u in range(4)])
@@ -498,26 +459,30 @@ def build(cfg):
             ts(R("zi", 1, 2), R("zi", 0, 1), 63, ALU.bitwise_and)
             ts(whole("zf"), R("zi", 1, 2), MUL, ALU.mult)
 
+    order = [(c, s) for s in range(3) for c in range(NC)]
     for t in range(NT):
-        order = cfg["order"][0 if t == 0 else 2 if t == NT - 1 else 1]
         age[0] = t * len(order)
-        copy(R("hU", 16 * t, 16 * t + 16), R("hb%d" % t, 16 * t, 16 * t + 16))
-        if t == 0:
-            copy(R("thr", 0, 16), R("hb0", 64, 80))
-        else:
-            ts(R("thr", 16 * t, 16 * t + 16), R("hb%d" % t, 64, 80), whole("zf"), ALU.add)
-        at = min(order.index((0, 2)) + cfg["sl_after"], len(order) - 1)
+        affine(R("RS%d" % (t % 2), 0, 256, 16), whole("TB"), 1.0, whole("zf") if t else 0.0)
+        if t < NT - 1:
+            for u in range(RB + 1):
+                gcopy(B("Q%d" % (t + 1), 0, NL, u), whole("q%d" % (t + 1)), after=sent[-NC:])
         for u, (c, s) in enumerate(order):
             age[0] = t * len(order) + u
             step(t, c, s)
-            if u == at:
-                age[0] = t * len(order) + order.index((0, 2)) + cfg["sl_age"]
+            if (c, s) == (0, 2):
                 slices(t)
-        age[0] = (t + 1) * len(order) - 1
-        tt(IND(whole("Cw"), whole("sU")), R("Y", 128, 384), R("Y", 0, 256), ALU.subtract, "scat")
+        tt(IND(whole("Cw"), R("sU", 8, 16)), R("V", 256, 384), R("V", 128, 256), ALU.subtract, "scat")
+        tt(IND(R("Cw", NB, NW + 256), R("sU", 0, 8)), R("V", 128, 256), R("V", 0, 128), ALU.subtract, "scat")
     copy(R("Cw", 0, 1), R("chi", 0, 1))
     dma("y", R("yc", 0, NW), R("Cw", 0, NW), "syc", 5000)
     return ops
+
+
+QUEUES = "vstgyn"
+
+
+def price(o, e):
+    return o["swap"][e][0] if o["swap"] else o["cost"]
 
 
 def schedule(ops, cfg):
@@ -534,100 +499,92 @@ def schedule(ops, cfg):
     age = [o["age"] for o in ops]
     for k in range(n - 1, -1, -1):
         age[k] = min([age[k]] + [age[x] for x in succ[k]])
-        if ops[k]["tag"] == "tab":
-            age[k], prio[k] = -1, prio[0]
-        prio[k] += cfg["bias"].get(ops[k]["tag"] + str(age[k]), 0) - cfg["wage"] * age[k]
-    ready = {e: [] for e in "vstgyn"}
+        prio[k] -= cfg["wage"] * age[k]
+    ready = {e: [] for e in QUEUES}
     at = [0.0] * n
-
-    def offer(k):
-        for e in (ops[k]["alt"] or ops[k]["eng"]):
-            ready[e].append(k)
-
+    homes = ["vs" if o["swap"] else o["eng"] for o in ops]
     for k in range(n):
         if left[k] == 0:
-            offer(k)
+            for e in homes[k]:
+                ready[e].append(k)
     free = {e: 0.0 for e in ready}
-    seq, start, end = [], [0.0] * n, [0.0] * n
+    seq, on = [], [""] * n
     while len(seq) < n:
-        best = None
-        for e, lst in ready.items():
-            if lst:
-                t0 = max(free[e], min(at[k] for k in lst))
-                if best is None or t0 < best[0]:
-                    best = (t0, e)
-        t0, e = best
-        k = max((x for x in ready[e] if at[x] <= t0 + 1e-6), key=lambda x: (prio[x], -x))
-        soon = [x for x in ready[e] if t0 + 1e-6 < at[x] <= t0 + min(cfg["look"], cfg["part"] * ops[k]["cost"])
-                and prio[x] > prio[k] and ops[x]["cost"] < cfg["short"]]
+        t0, e = min((max(free[e], min(at[k] for k in lst)), e) for e, lst in ready.items() if lst)
+
+        def worth(x):
+            return prio[x] - (cfg["steal"] if e == "v" and ops[x]["swap"] else 0.0)
+
+        k = max((x for x in ready[e] if at[x] <= t0 + 1e-6), key=lambda x: (worth(x), -x))
+        soon = [x for x in ready[e] if t0 + 1e-6 < at[x] <= t0 + min(cfg["look"], 0.5 * price(ops[k], e)) and worth(x) > worth(k)]
         if soon:
             k = min(soon, key=lambda x: at[x])
             t0 = at[k]
-        for e2 in (ops[k]["alt"] or e):
-            ready[e2].remove(k)
-        if ops[k]["alt"]:
-            ops[k]["eng"] = e
-            ops[k]["cost"], ops[k]["calls"] = ops[k]["alt"][e]
-        start[k] = t0
-        free[e] = t0 + ops[k]["cost"]
-        end[k] = free[e] + ops[k]["lat"]
+        for h in homes[k]:
+            ready[h].remove(k)
+        on[k] = e
+        free[e] = t0 + price(ops[k], e)
         seq.append(k)
         for x in succ[k]:
-            at[x] = max(at[x], end[k] + lat if k in ops[x]["deps"] else free[e])
+            at[x] = max(at[x], free[e] + ops[k]["lat"] + lat if k in ops[x]["deps"] else free[e])
             left[x] -= 1
             if left[x] == 0:
-                offer(x)
-    return seq, start, end
+                for h in homes[x]:
+                    ready[h].append(x)
+    return seq, on
 
 
-def polish(ops, seq, cfg):
-    n, lat = len(ops), cfg["lat"]
-    code = {e: u for u, e in enumerate("vstgyn")}
-    eng = [code[o["eng"]] for o in ops]
-    cost = [o["cost"] for o in ops]
-    tail = [o["lat"] + lat for o in ops]
+def polish(plans, seq, on, rounds, heat):
+    ops = plans[0][0]
+    n = len(ops)
+    eng = [QUEUES.index(e) for e in on]
     deps = [tuple(o["deps"]) for o in ops]
     pred = [o["deps"] | o["order"] for o in ops]
-    other = [(o["swap"]["v"][0], o["swap"]["s"][0]) if o["swap"] else None for o in ops]
+    sets = [([price(o, "v") for o in x], [price(o, "s") for o in x], [o["lat"] + lat for o in x], w) for x, lat, w in plans]
 
     def run(sq):
-        free, last = [0.0] * 6, [-1] * 6
-        end, start, why = [0.0] * n, [0.0] * n, [-1] * n
-        for k in sq:
-            e = eng[k]
-            t, w = free[e], last[e]
-            for d in deps[k]:
-                if end[d] > t:
-                    t, w = end[d], n + d
-            start[k], why[k] = t, w
-            t += cost[k]
-            free[e], last[e] = t, k
-            end[k] = t + tail[k]
-        return max(end), start, why, end
+        out = []
+        for a, b, tail, w in sets:
+            free, last = [0.0] * 6, [-1] * 6
+            end, start, why = [0.0] * n, [0.0] * n, [-1] * n
+            for k in sq:
+                e = eng[k]
+                t, y = free[e], last[e]
+                for d in deps[k]:
+                    if end[d] > t:
+                        t, y = end[d], n + d
+                start[k], why[k] = t, y
+                t += b[k] if e else a[k]
+                free[e], last[e] = t, k
+                end[k] = t + tail[k]
+            out.append((max(end) * w, start, why, end))
+        return sum(r[0] for r in out), out
 
-    state = [cfg["seed"]]
+    state = [1]
 
     def rnd():
         state[0] = (state[0] * 6364136223846793005 + 1442695040888963407) % 2 ** 64
         return (state[0] >> 11) / 2.0 ** 53
 
-    now, start, why, end = run(seq)
+    now, res = run(seq)
     best, keep = now, (list(seq), list(eng))
     arcs = None
-    for it in range(cfg["polish"]):
+    for it in range(rounds):
         if arcs is None:
+            start = res[0][1]
             seq = [k for _, _, k in sorted((start[k], u, k) for u, k in enumerate(seq))]
-            arcs, k = [], max(range(n), key=lambda x: end[x])
-            while k >= 0:
-                w = why[k]
-                if 0 <= w < n:
-                    arcs.append((w, k))
-                k = w - n if w >= n else w
+            arcs = []
+            for _, _, why, end in res:
+                k = max(range(n), key=lambda x: end[x])
+                while k >= 0:
+                    w = why[k]
+                    if 0 <= w < n:
+                        arcs.append((w, k))
+                    k = w - n if w >= n else w
         u, v = arcs[int(rnd() * len(arcs))]
-        flip = u if other[u] else v if other[v] else -1
+        flip = u if ops[u]["swap"] else v if ops[v]["swap"] else -1
         if flip >= 0 and rnd() < 0.3:
             eng[flip] ^= 1
-            cost[flip] = other[flip][eng[flip]]
             new = seq
         else:
             flip = -1
@@ -655,29 +612,32 @@ def polish(ops, seq, cfg):
                 early.reverse()
                 new = seq[:a] + early + [x for x in seq[a:b] if x not in early] + seq[b + 1:]
         r = run(new)
-        if r[0] <= now + cfg["heat"] * (1.0 - it / cfg["polish"]) * rnd() ** 3:
-            now, start, why, end = r
+        if r[0] <= now + heat * (1.0 - it / rounds) * rnd() ** 3:
+            now, res = r
             seq, arcs = new, None
             if now < best:
                 best, keep = now, (list(seq), list(eng))
         elif flip >= 0:
             eng[flip] ^= 1
-            cost[flip] = other[flip][eng[flip]]
-    seq, eng = keep
-    for k, o in enumerate(ops):
-        if o["swap"]:
-            o["eng"] = "vs"[eng[k]]
-            o["cost"], o["calls"] = o["swap"][o["eng"]]
-    return seq, best
+    return best, keep[0], [QUEUES[e] for e in keep[1]]
 
 
 _PLAN = {}
 
 
-def plan():
+def plan(cfg=CFG):
     if not _PLAN:
-        _PLAN["ops"] = build(CFG)
-        _PLAN["seq"] = polish(_PLAN["ops"], schedule(_PLAN["ops"], CFG)[0], CFG)[0]
+        sets = [dict(cfg, **c) for c in COSTS]
+        plans = [(build(c), c["lat"], c["weight"]) for c in sets]
+        tries = [polish(plans, *schedule(x[0], dict(c, wage=w, steal=s)), 0, 0.0) for x, c in zip(plans, sets)
+                 for w in cfg["wage"] for s in cfg["steal"]]
+        _PLAN["score"], seq, on = polish(plans, *min(tries)[1:], cfg["polish"], cfg["heat"])
+        ops = plans[0][0]
+        for o, e in zip(ops, on):
+            if o["swap"]:
+                o["eng"] = e
+                o["cost"], o["calls"] = o["swap"][e]
+        _PLAN["ops"], _PLAN["seq"] = ops, seq
     return _PLAN["ops"], _PLAN["seq"]
 
 
@@ -694,7 +654,7 @@ def put(g, T, topo, core, dst_core, out, src, sem):
 
 
 def bundle(t):
-    return [R("q%d" % t, 0, NL), R("hb%d" % t, 0, 80)]
+    return [R("q%d" % t, 0, NL), R("hU%d" % t, 0, 64)]
 
 
 def last_hop(T, topo, src_rank, dst_rank):

@@ -3,29 +3,35 @@ from concourse.mybir import AluOpType as ALU, ActivationFunctionType as AF
 
 NB, NL, NS, NT, TH = 1280, 256, 64, 4, 1250
 NW = NB + 2 * NS * NT
-MUL = 4096
+MUL = 2048
 RB = 4
-REST = 2048
+HEAD = 96
 
 CFG = {
-    "chunks": [96, 96, 64], "ab": 4, "nd": 4, "piece": 24, "half": 64, "early": True,
-    "wage": (1000, 2000), "steal": (1500, 5000), "look": 60.0, "polish": 14000, "heat": 150.0,
+    "chunks": [96, 96, 64], "ab": 4, "nd": 4, "piece": 12, "half": 64, "early": True, "mask": (),
+    "wage": (700, 900, 1200), "steal": (3000, 4000), "look": 100.0, "polish": 30000, "heat": 60.0,
+    "bias": dict([(x, 4000.0) for x in ("exm", "C", "vrep", "cvt")] + [(x, 2000.0) for x in ("amin", "ex", "post")]
+                 + [(x, -1000.0) for x in ("gCf", "v4", "scat")] + [(x, -1800.0) for x in ("", "cmp", "min", "gp", "cnt")]),
     "ov": 20.0, "os": 30.0, "mn": 50, "oi": 45.0, "hop": 2500.0,
 }
-COSTS = [{"cyc": 0.88, "pe": 0.44, "lat": 160.0, "G": 1.5, "SC": 3.5, "weight": 0.5},
-         {"cyc": 1.2, "pe": 0.6, "lat": 120.0, "G": 1.9, "SC": 5.0, "weight": 0.385}]
+COSTS = [{"cyc": 0.84, "pe": 0.42, "lat": 185.0, "G": 1.56, "SC": 3.8, "ov": 6.0, "os": 12.0, "mn": 61, "hop": 1800.0, "weight": 0.55},
+         {"cyc": 1.2, "pe": 0.6, "lat": 170.0, "G": 1.9, "SC": 5.0, "ov": 8.0, "os": 16.0, "mn": 60, "hop": 2300.0, "weight": 0.33}]
+
+
+def span(L):
+    return -(-(HEAD + 20 * L) // 80) * 80
 
 
 def layout(cfg):
     f32, bf, f16, i32, u16 = "float32", "bfloat16", "float16", "int32", "uint16"
     flat = {
-        "chi": (NB, i32), "Cw": (NW + 256, f32), "K": (NW, bf), "K0": (8, bf), "psend": (NT * NL, bf), "pin": (NT * NL, bf),
-        "hI": (64, i32), "ci": (8, i32), "cf": (16, f32), "U": (128, f32), "G2": (16, f32), "C16": (4, f32), "TB": (16, f32),
-        "SY": (16, bf), "SM": (16, bf), "EM": (128, f32), "I1": (128, bf), "I2": (128, bf), "LA": (128, bf), "LB": (128, bf),
-        "G8": (256, bf), "GQ": (256, bf), "BOb": (128, bf), "BOh": (128, f16), "ones": (128, bf), "R16": (128, f32),
-        "D0": (128, f32), "RS0": (256, f32), "RS1": (256, f32), "OH": (REST + 16, bf),
+        "chi": (NB, i32), "Cw": (NW + 256, f32), "K": (NW, bf), "K0": (8, bf), "psend": (NT * NL, bf), "pin": (NL, bf),
+        "hI": (64, i32), "ci": (8, i32), "cf": (16, f32), "U": (128, f32), "C5": (4, f32), "xo": (8, u16), "TB": (16, f32), "RS": (512, f32), "JJ": (5 * HEAD, bf),
+        "SY": (16, bf), "SM": (16, bf), "EM": (128, f32), "I1": (128, bf), "I2": (128, bf), "LA": (128, bf),
+        "G8": (256, bf), "GQ": (256, bf), "BOr": (128, bf), "BOh": (128, f16), "ones": (128, bf), "R16": (128, f32),
+        "D0": (128, f32), "SP": (15 * cfg["chunks"][0] + 32, bf),
         "mk": (112, f32), "C32": (128, f32), "Dq": (128, f32), "Dt": (256, f32), "R2": (128, bf), "DG": (128, bf), "ND": (32, bf),
-        "GT": (16, bf), "E1": (16, bf), "TG0": (8, f32), "TG": (16, f32), "Dm": (16, f32), "qoff": (2, u16),
+        "TG0": (8, f32), "TG": (16, f32), "Dm": (16, f32), "qoff": (2, u16),
         "NO": (NT * 128, f32), "Z": (224, f16), "X": (704, bf), "LG": (512, bf), "sm": (64, f32), "nm": (8, f32), "qsc": (128, f32),
         "sl": (4, bf), "zi": (2, i32), "zf": (1, f32), "V": (384, f32), "E2": (64, f32), "sU": (16, u16), "jF": (8, f32), "jU": (8, u16),
     }
@@ -35,11 +41,11 @@ def layout(cfg):
         flat["Q%d" % t] = ((RB + 1) * NL, bf)
     NC = len(cfg["chunks"])
     for c, L in enumerate(cfg["chunks"]):
-        runs = (RB + 1) * (16 // RB) * L
-        for name, n, ty in (("key", REST + 16, bf), ("kU", L, u16), ("kF", 2 * L, f16), ("pr", L, f16), ("sc", L, f32), ("m", 256, f32),
-                            ("lo", 144, f16), ("nU", 8, u16), ("vU", 16, u16),
-                            ("p", L, bf), ("pd", L, bf), ("Y", runs, bf), ("M", runs, bf)):
+        for name, n, ty in (("key", 16 * L, bf), ("kU", L, u16), ("kF", 2 * L, f16), ("pr", L, f16), ("sc", L, f32), ("m", 256, f32),
+                            ("lo", 144, f16), ("l8", 8, f32), ("nU", 8, u16), ("vU", 16, u16), ("Y", (NT + 1) * span(L), bf), ("M", 20 * L, bf)):
             flat["%s%d" % (name, c)] = (n, ty)
+        for name, n, ty in (("OH", HEAD + 20 * L, bf), ("LB", 128, f16), ("RJ", 128, f32)):
+            flat["%s_%d" % (name, L)] = (n, ty)
     sc = {k: ("sbuf", [128, n], ty) for k, (n, ty) in flat.items()}
     for k in ["d%d" % k for k in range(cfg["nd"])] + ["s%d" % c for c in range(NC)] + (["misc"] if cfg["nd"] + NC < 8 else []):
         sc[k] = ("psum", [128, 512], f32)
@@ -80,8 +86,8 @@ def ap(T, x):
     if x[0] == "ind":
         return ap(T, x[1]).indirect(ap(T, x[2]))
     if x[0] == "box":
-        w = RB + 1
-        return T[x[1]][:, w * x[2] + x[4]:w * x[3]:w] if x[5] is None else T[x[1]][:, w * x[2]:w * x[3]]
+        w, a = RB + 1, HEAD % (RB + 1) if x[1][0] == "Y" else 0
+        return T[x[1]][:, a + w * x[2] + x[4]:a + w * x[3]:w] if x[5] is None else T[x[1]][:, a + w * x[2]:a + w * x[3]]
     if len(x) > 4 and x[4] < 128:
         return T[x[0]][0:x[4], x[1]:x[2]:x[3]]
     if x[3] == 1:
@@ -96,6 +102,8 @@ def named(x):
 def area(x):
     if x[0] == "box":
         return (x[1], x[2], x[3], x[4], x[4] + 1 if x[5] is None else x[5], True)
+    if x[0][0] == "Y":
+        return (x[0], (x[1] - HEAD % 5) // 5, -(-(x[2] - HEAD % 5) // 5), 0, 5, False)
     return (x[0], x[1], x[2], 0, 1, x[3] == 1)
 
 
@@ -143,7 +151,7 @@ def build(cfg):
                     st[1].append(k)
         deps.discard(k)
         ops.append({"eng": eng, "cost": cost, "deps": deps, "order": order - deps, "calls": calls, "sem": sem, "lat": lat, "tag": tag,
-                    "swap": None, "age": age[0]})
+                    "swap": None, "part": None, "age": age[0]})
         return k
 
     def two(*xs):
@@ -190,10 +198,13 @@ def build(cfg):
             f = lambda q, T: q.activation(ap(T, out), ap(T, a), func)
         return add("s", scost(a), [a, scale, bias], [out], [f], tag=tag)
 
+    def copies(out, a):
+        return {"s": [lambda q, T: q.activation(ap(T, out), ap(T, a), AF.Copy)], "v": [lambda q, T: q.tensor_copy(ap(T, out), ap(T, a))]}
+
     def either(eng, out, a, tag=""):
         k = act(out, a, AF.Copy, tag)
         ops[k]["swap"] = {"s": (ops[k]["cost"], ops[k]["calls"]),
-                          "v": (vcost(cnt(a), rate(out, a, 0.5 if two(out, a) else 1)), [lambda q, T: q.tensor_copy(ap(T, out), ap(T, a))])}
+                          "v": (vcost(cnt(a), rate(out, a, 0.5 if two(out, a) else 1)), copies(out, a)["v"])}
         ops[k]["eng"] = eng
         ops[k]["cost"], ops[k]["calls"] = ops[k]["swap"][eng]
         return k
@@ -203,6 +214,11 @@ def build(cfg):
         ops[k]["swap"] = {"v": (ops[k]["cost"], ops[k]["calls"]),
                           "s": (scost(a), [lambda q, T: q.activation(ap(T, out), ap(T, a), AF.Identity, bias=ap(T, bias), scale=ap(T, scale))])}
         return k
+
+    def fill(out):
+        a = R("JJ", 0, cnt(out))
+        k = act(out, a, AF.Copy, scale=0.0)
+        ops[k]["swap"] = {"s": (ops[k]["cost"], ops[k]["calls"]), "v": (vcost(cnt(out), 0.5), [lambda q, T: q.memset(ap(T, out), 0.0)])}
 
     def mm(lst, tag=""):
         cost, calls = 0.0, []
@@ -242,6 +258,7 @@ def build(cfg):
     iota(col(3), [[0, 1]], 0, 1)
     iota(whole("U"), [[1, 128]], 0)
     iota(whole("R16"), [[0, 8], [1, 16]], 0)
+    iota(whole("JJ"), [[0, HEAD], [1, 5]], 0)
     ts(R("ci", 1, 2), R("ci", 0, 1), 15, ALU.bitwise_and)
     ts(R("ci", 2, 3), R("ci", 0, 1), 4, ALU.arith_shift_right)
     ts(R("ci", 3, 4), R("ci", 0, 1), 14, ALU.bitwise_and)
@@ -255,38 +272,47 @@ def build(cfg):
     affine(col(8), col(0), 2.0, 0.0)
     affine(col(9), col(0), -1.0, 0.0)
     affine(col(11), col(0), 1.0, -1.0)
-    affine(col(15), col(0), 16.0, 0.0)
+    affine(col(15), col(0), 5.0, float(HEAD))
     ts(R("cf", 12, 14), R("U", 0, 2), col(3), ALU.is_equal)
-    affine(col(14), col(12), 16.0, 0.0)
+    affine(col(14), col(12), 5.0, 0.0)
     ts(R("qoff", 0, 1), R("ci", 4, 5), 32, ALU.mult, 31, ALU.add)
     ts(whole("I1"), whole("U"), col(3), ALU.is_equal)
     affine(whole("I2"), whole("I1"), -1.0, 0.0)
     affine(whole("LA"), whole("U"), col(12), col(13))
-    affine(whole("LB"), whole("R16"), col(13), col(14))
+    for L in sorted(set(ch), reverse=True):
+        iota(whole("RJ_%d" % L), [[0, 8], [5 * L, 4], [1, 4]], HEAD)
+        ts(whole("LB_%d" % L), whole("RJ_%d" % L), col(13), ALU.mult, col(14), ALU.add)
+        fill(R("OH_%d" % L, 0, HEAD))
+        for b in range(4):
+            ts(R("OH_%d" % L, HEAD + 5 * L * b, HEAD + 5 * L * (b + 1)), R("JJ", 0, 5 * L), float(4 * b), ALU.add, col(0), ALU.is_equal)
     for u in range(2):
-        iota(whole("RS%d" % u), [[0, 256]], 0)
-    iota(whole("TB"), [[REST, 2], [0, 8]], MUL * TH)
+        iota(R("RS", 256 * u, 256 * u + 256), [[0, 256]], 0)
+    iota(R("TB", 0, 8), [[0, 8]], MUL * TH + HEAD + 20 * max(ch))
+    iota(R("TB", 8, 16), [[0, 8]], MUL * TH + HEAD + 20 * max(ch), 1)
     iota(whole("G8"), [[0, 2], [1, 8], [0, 16]], 0)
     ts(whole("GQ"), whole("G8"), col(1), ALU.is_equal, float(MUL), ALU.mult)
     ts(whole("BOh"), R("G8", 0, 128), col(1), ALU.is_equal)
-    affine(whole("BOb"), R("GQ", 0, 128), 0.5, 0.0)
+    affine(whole("BOr"), R("GQ", 0, 128), HEAD / MUL - 1.0, float(MUL))
     iota(whole("ones"), [[0, 128]], 1)
     ts(whole("EM"), whole("R16"), col(0), ALU.is_equal)
-    either("s", R("OH", 0, 128), whole("EM"))
-    for w in (128, 256, 512, 1024):
-        if w < 16 * max(ch):
-            act(R("OH", w, 2 * w), R("OH", 0, w), AF.Copy, "tab")
-    iota(R("OH", REST, REST + 16), [[0, 16]], 0)
-    for c in range(NC):
-        iota(R("key%d" % c, 16 * ch[c], REST + 16), [[0, REST + 16 - 16 * ch[c]]], 0)
-        iota(B("Y%d" % c, 0, 16 // RB * ch[c], RB), [[0, 16 // RB * ch[c]]], 0)
-        mset(whole("lo%d" % c), 0.0)
+    for c, L in enumerate(ch):
+        for w in range(NT + 1):
+            a = (w * span(L) + HEAD) // 5
+            zero = fill if w in (0, NT) else lambda x: iota(x, [[0, cnt(x)]], 0)
+            zero(B("Y%d" % c, a, a + 4 * L, RB))
+            if w == 0 or L < HEAD:
+                zero(R("Y%d" % c, w * span(L) + (L if w else 0), w * span(L) + HEAD))
+        mset(whole(("l8%d" if c in cfg["mask"] else "lo%d") % c), 0.0)
+    if cfg["mask"]:
+        copy(whole("xo"), R("U", 0, 8))
     either("v", whole("SY"), R("GQ", 0, 256, 16))
     affine(whole("SM"), R("GQ", 0, 256, 16), -2.0, 0.0)
     affine(whole("D0"), whole("EM"), 65536.0 + 2048.0, -2048.0)
-    affine(whole("C16"), R("U", 0, 4), 256.0, col(15))
-    ts(whole("GT"), R("U", 0, 16), col(0), ALU.is_lt)
-    ts(whole("E1"), R("U", 0, 16), col(11), ALU.is_equal)
+    affine(whole("C5"), R("U", 0, 4), 80.0, col(15))
+    iota(whole("SP"), [[0, 15 * ch[0] + 32]], 0)
+    for b in range(4):
+        ts(R("SP", 5 * ch[0] * b, 5 * ch[0] * b + 4), R("U", 4 * b, 4 * b + 4), col(0), ALU.is_lt)
+        ts(R("SP", 5 * ch[0] * b + 16, 5 * ch[0] * b + 20), R("U", 4 * b, 4 * b + 4), col(11), ALU.is_equal)
     act(whole("mk"), R("R16", 0, 112), AF.Sign, bias=col(9))
     iota(R("mk", 16, 64), [[0, 48]], 1)
     iota(whole("C32"), [[0, 4], [1, 32]], 0)
@@ -329,8 +355,14 @@ def build(cfg):
         L, f0 = ch[c], sum(ch[:c])
         NH = L // 16
         key, Y, M, S = "key%d" % c, "Y%d" % c, "M%d" % c, "s%d" % c
-        kU, own = "kU%d" % c, whole("p%d" % c)
-        p = R("pin", NL * (t - 1) + f0, NL * (t - 1) + f0 + L) if s == 0 else own
+        kU = "kU%d" % c
+        w0 = span(L) * (NT if s == 1 else t)
+        r0 = (w0 + HEAD) // 5
+
+        def p_of(w):
+            return R(Y, span(L) * w, span(L) * w + L)
+
+        p = p_of(NT if s == 1 else t)
         plain = t + s == 0
         base = NB + 128 * t
         voff = R("hU%d" % t, 16 * t + f0 // 16, 16 * t + f0 // 16 + NH) if s == 0 else R("vU%d" % c, (s - 1) * 8, (s - 1) * 8 + NH)
@@ -343,12 +375,17 @@ def build(cfg):
         m = -(-L // cfg["piece"])
         for u in range(m):
             a, b = 2 * (L // 2 * u // m), 2 * (L // 2 * (u + 1) // m)
-            either("s", R(key, 16 * a, 16 * b), IND(R("K", 0, base), R(kU, a, b)), "gK")
-        mm([(R(S, 0, 256) + (L,), R("q%d" % t, f0, f0 + L), whole("GQ"), True, False)], "low")
+            k = either("s", R(key, 16 * a, 16 * b), IND(R("K", 0, base), R(kU, a, b)), "gK")
+            ops[k]["part"] = ((t, c, s), (cfg["ov"] + cfg["oi"], cfg["os"] + cfg["oi"]), b - a,
+                              lambda e, a, b: copies(R(key, 16 * a, 16 * b), IND(R("K", 0, base), R(kU, a, b)))[e])
+        mm([(R(S, 0, 256) + (L,), R("q%d" % t, f0, f0 + L), whole("GQ"), True, False),
+            (R(S, 128, 256) + (L,), R("LA", 0, L), whole("LB_%d" % L), False, False)], "low")
 
         def sums(src, weight, blocks, slots, last):
-            lst = [(R(S, RB * b + u, 256, 16) + (L,), B(src, L * b, L * b + L, u), whole(weight), False, False) for b in blocks for u in slots]
-            mm(lst + [(R(S, 128, 256) + (L,), R("LA", 0, L), whole("LB"), False, True)] * last, "sum")
+            a = r0 if src == Y else 0
+            lst = [(R(S, RB * b + u, 256, 16) + (L,), B(src, a + L * b, a + L * b + L, u), whole(weight), False, False)
+                   for b in blocks for u in slots]
+            mm(lst[:-1] + [lst[-1][:4] + (last,)], "sum")
 
         ab = cfg["ab"]
         fit = 512 // (ab * L)
@@ -360,7 +397,7 @@ def build(cfg):
                 if plain:
                     for u in slots:
                         for b in blocks:
-                            either("v", B(Y, L * b, L * b + L, u), R(key, RB * b + u, 16 * L, 16), "abs")
+                            either("v", B(Y, r0 + L * b, r0 + L * b + L, u), R(key, RB * b + u, 16 * L, 16), "abs")
                 else:
                     d = "d%d" % (turn[0] % cfg["nd"])
                     turn[0] += 1
@@ -372,33 +409,33 @@ def build(cfg):
                     for n, part in enumerate(parts):
                         mm([x + (n + u == 0, n == len(parts) - 1 and u == len(part) - 1) for u, x in enumerate(part)], "d")
                     for n, u in enumerate(slots):
-                        act(B(Y, L * b0, L * (b0 + ab), u), R(d, ab * L * n, ab * L * (n + 1)), AF.Abs, "abs")
+                        act(B(Y, r0 + L * b0, r0 + L * (b0 + ab), u), R(d, ab * L * n, ab * L * (n + 1)), AF.Abs, "abs")
                 sums(Y, "SY", blocks, slots, False)
             for b in blocks:
-                scan(B(M, L * b, L * b + L, 0, RB + 1), B("Q%d" % t, f0, f0 + L, 0, RB + 1), B(Y, L * b, L * b + L, 0, RB + 1),
-                     ALU.max, ALU.min, "min")
+                scan(B(M, L * b, L * b + L, 0, RB + 1), B("Q%d" % t, f0, f0 + L, 0, RB + 1),
+                     B(Y, r0 + L * b, r0 + L * b + L, 0, RB + 1), ALU.max, ALU.min, "min")
                 sums(M, "SM", [b], range(RB), b == 16 // RB - 1)
         m, lo = "m%d" % c, "lo%d" % c
-        scan(whole(m) + (L,), whole("RS%d" % (t % 2)) + (L,), R(S, 0, 256) + (L,), ALU.max, ALU.min, "amin")
-        tt(R(lo, 15, 143, 16) + (L,), R(m, 143, 256, 16) + (L,), R(m, 15, 128, 16) + (L,), ALU.subtract, "ex")
-        mm([(R(S, 256, 256 + NH), R(lo, 15 - r, 143 - r), R("I1", r, L, 16), r == 0, r == 15) for r in range(16)], "exm")
+        scan(whole(m) + (L,), R("RS", 256 * (t % 2), 256 * (t % 2) + 256) + (L,), R(S, 0, 256) + (L,), ALU.max, ALU.min, "amin")
+        if c in cfg["mask"]:
+            tt(whole("l8%d" % c) + (L,), R(m, 143, 256, 16) + (L,), R(m, 15, 128, 16) + (L,), ALU.subtract, "ex")
+            tt(R(lo, 0, 128), IND(whole("l8%d" % c), whole("xo")), whole("EM"), ALU.mult, "ex")
+            mm([(R(S, 256, 256 + NH), R(lo, 0, 128), R("BOh", 0, L, 16), True, True)], "exm")
+        else:
+            tt(R(lo, 15, 143, 16) + (L,), R(m, 143, 256, 16) + (L,), R(m, 15, 128, 16) + (L,), ALU.subtract, "ex")
+            mm([(R(S, 256, 256 + NH), R(lo, 15 - r, 143 - r), R("I1", r, L, 16), r == 0, r == 15) for r in range(16)], "exm")
         nU = R("nU%d" % c, 0, NH)
         copy(nU, R(S, 256, 256 + NH), "C")
+        if c == 0 and s == 2:
+            for u in range(4):
+                ts(R("LG", 128 * u, 128 * u + 128), whole("BOr"), R(S, 256 + u, 257 + u), ALU.is_le, 2048.0, ALU.mult, "go")
         if c == 0 and s > 0:
-            tt(R("jF", 4 * s - 4, 4 * s), R(S, 256, 260), whole("C16"), ALU.subtract, "pre")
-        new = own if s < 2 else R("psend", NL * t + f0, NL * t + f0 + L)
-        if plain:
-            either("s", new, IND(whole(key), nU), "gp")
-        elif cfg.get("gp") == "pe" or (cfg.get("gp") == "pe2" and s < 2):
-            either("s", whole("pd%d" % c), IND(whole(key), nU), "gp")
-            mm([(R(misc, 0, L), whole("I1"), whole("pd%d" % c), True, False), (R(misc, 0, L), whole("I2"), p, False, True)], "gp")
-            act(new, R(misc, 0, L), AF.Abs, "gp")
-        else:
-            tt(whole("pd%d" % c), IND(whole(key), nU), p, ALU.subtract, "gp")
-            act(new, whole("pd%d" % c), AF.Abs, "gp")
+            tt(R("jF", 4 * s - 4, 4 * s), R(S, 256, 260), whole("C5"), ALU.subtract, "pre")
+        new = p_of(t if s else NT) if s < 2 else R("psend", NL * t + f0, NL * t + f0 + L)
+        either("s", new, IND(R(Y, w0, w0 + HEAD + 20 * L), nU), "gp")
         if s < 2:
             pr, vU = "pr%d" % c, R("vU%d" % c, s * 8, s * 8 + NH)
-            tt(whole(pr), IND(whole("OH"), nU), kF, ALU.mult, "oh")
+            tt(whole(pr), IND(whole("OH_%d" % L), nU), kF, ALU.mult, "oh")
             lst = [(R(S, 272, 272 + L), whole("BOh"), whole(pr), True, True)]
             if c == 0:
                 lst.append((R(S, 400, 464), whole("BOh"), R(pr, 0, 64), True, True))
@@ -412,7 +449,7 @@ def build(cfg):
                 if t < NT - 1:
                     either("s", R("K", base + s, base + 128, 2), IND(R("K", 0, base), R("vU0", 8 * s, 8 * s + 4)))
         else:
-            dst = R("pin", NL * t + f0, NL * t + f0 + L)
+            dst = p_of(t + 1) if t < NT - 1 else R("pin", f0, f0 + L)
             k = add("g", 300.0, [new], [], [("sendp", new, dst, "ap%d_%d" % (t, c))], sem="ls")
             sent.append(k)
             add("n", 0.0, [], [dst], [], sem="ap%d_%d" % (t, c), lat=2 * cfg["hop"], after=[k])
@@ -420,21 +457,20 @@ def build(cfg):
                 dma("y", R("yp", f0, f0 + L), dst, "syp%d" % c, 2200)
 
     def slices(t):
+        top = 15 * ch[0] + 3
         affine(R("TG", 0, 8), whole("TG0"), 1.0, float(128 * t))
         tt(R("sm", 0, 4), R("TG", 8, 12), R("TG", 12, 16), ALU.not_equal)
         for u in range(2):
-            ts(R("jU", 4 * u, 4 * u + 4), R("jF", 4 * u, 4 * u + 4), 15.0, ALU.min, tag="pre")
-        ts(R("sm", 4, 8), R("jF", 0, 4), 15.0, ALU.is_lt, tag="pre")
+            copy(R("jU", 4 * u, 4 * u + 4), R("jF", 4 * u, 4 * u + 4), "pre")
+        ts(R("sm", 4, 8), R("jF", 0, 4), float(top), ALU.is_lt, tag="pre")
         tt(R("sm", 8, 12), R("sm", 0, 4), R("sm", 4, 8), ALU.mult, "pre")
         for u in range(2):
             tt(R("nm", 4 * u, 4 * u + 4), R("TG", 8 + 4 * u, 12 + 4 * u), R("sm", 8, 12), ALU.mult, "pre")
         affine(R("sm", 16, 32), whole("TG"), 1.0, col(10), "pre")
-        ts(R("sm", 12, 16), R("jF", 4, 8), 16.0, ALU.is_lt, tag="go")
         seg = [(0, 128, [(0, 128, 0)]), (64, 160, [(0, 64, 64), (64, 96, 32)]), (96, 192, [(0, 32, 96), (64, 96, 64)]), (192, 224, [(0, 32, 96)])]
-        lst, x = [(R(misc, 256, 384), whole("BOb"), whole("DG"), True, False)], 0
+        lst, x = [(R(misc, 256, 384), R("GQ", 0, 128), whole("DG"), True, False)], 0
         for c, (a, b, parts) in enumerate(seg):
             lg = R("LG", 128 * c, 128 * c + 128)
-            affine(lg, whole("BOb"), R("sm", 12 + c, 13 + c), 0.0, "go")
             lst.append((R(misc, 256 + 32 * c, 288 + 32 * c), lg, whole("ND"), False, False))
             for u in range(2):
                 ts(R("X", x, x + b - a), R("Z", a, b), R("nm", 4 * u + c, 4 * u + c + 1), ALU.is_equal, tag="cmp")
@@ -447,10 +483,10 @@ def build(cfg):
         tt(R("sm", 48, 64), R("sm", 32, 48), whole("Dm"), ALU.min, "post")
         copy(whole("sU"), R("sm", 48, 64), "post")
         ra, rb, jj, kk = R("kF0", ch[0], ch[0] + NS), R("V", 320, 384), R("jU", 0, 4), R("jU", 4, 8)
-        tt(R("V", 128, 192), IND(whole("GT"), jj), ra, ALU.mult, "v4")
-        tt(R("V", 192, 256), IND(whole("GT"), kk), rb, ALU.mult, "v4")
-        tt(R("V", 0, 64), IND(R("OH", 0, 16), jj), R("NO", 128 * t, 128 * t + 64), ALU.mult, "v4")
-        tt(whole("E2"), IND(whole("E1"), jj), R("NO", 128 * t + 64, 128 * t + 128), ALU.mult, "v4")
+        tt(R("V", 128, 192), IND(whole("SP"), jj), ra, ALU.mult, "v4")
+        tt(R("V", 192, 256), IND(whole("SP"), kk), rb, ALU.mult, "v4")
+        tt(R("V", 0, 64), IND(R("OH_%d" % ch[0], HEAD, HEAD + top + 1), jj), R("NO", 128 * t, 128 * t + 64), ALU.mult, "v4")
+        tt(whole("E2"), IND(R("SP", 16, top + 17), jj), R("NO", 128 * t + 64, 128 * t + 128), ALU.mult, "v4")
         tt(R("V", 256, 320), whole("E2"), ra, ALU.add, "v4")
         if t < NT - 1:
             ts(whole("sl"), R("qsc", 31, 128, 32), col(6), ALU.is_equal)
@@ -462,7 +498,7 @@ def build(cfg):
     order = [(c, s) for s in range(3) for c in range(NC)]
     for t in range(NT):
         age[0] = t * len(order)
-        affine(R("RS%d" % (t % 2), 0, 256, 16), whole("TB"), 1.0, whole("zf") if t else 0.0)
+        affine(R("RS", 256 * (t % 2), 256 * (t % 2) + 256, 16), whole("TB"), 1.0, whole("zf") if t else 0.0)
         if t < NT - 1:
             for u in range(RB + 1):
                 gcopy(B("Q%d" % (t + 1), 0, NL, u), whole("q%d" % (t + 1)), after=sent[-NC:])
@@ -471,9 +507,10 @@ def build(cfg):
             step(t, c, s)
             if (c, s) == (0, 2):
                 slices(t)
+        if t == NT - 1:
+            copy(R("Cw", 0, 1), R("chi", 0, 1))
         tt(IND(whole("Cw"), R("sU", 8, 16)), R("V", 256, 384), R("V", 128, 256), ALU.subtract, "scat")
         tt(IND(R("Cw", NB, NW + 256), R("sU", 0, 8)), R("V", 128, 256), R("V", 0, 128), ALU.subtract, "scat")
-    copy(R("Cw", 0, 1), R("chi", 0, 1))
     dma("y", R("yc", 0, NW), R("Cw", 0, NW), "syc", 5000)
     return ops
 
@@ -499,7 +536,7 @@ def schedule(ops, cfg):
     age = [o["age"] for o in ops]
     for k in range(n - 1, -1, -1):
         age[k] = min([age[k]] + [age[x] for x in succ[k]])
-        prio[k] -= cfg["wage"] * age[k]
+        prio[k] += cfg["bias"].get(ops[k]["tag"], 0.0) - cfg["wage"] * age[k]
     ready = {e: [] for e in QUEUES}
     at = [0.0] * n
     homes = ["vs" if o["swap"] else o["eng"] for o in ops]
@@ -508,7 +545,7 @@ def schedule(ops, cfg):
             for e in homes[k]:
                 ready[e].append(k)
     free = {e: 0.0 for e in ready}
-    seq, on = [], [""] * n
+    seq, on, last = [], [""] * n, {}
     while len(seq) < n:
         t0, e = min((max(free[e], min(at[k] for k in lst)), e) for e, lst in ready.items() if lst)
 
@@ -524,6 +561,9 @@ def schedule(ops, cfg):
             ready[h].remove(k)
         on[k] = e
         free[e] = t0 + price(ops[k], e)
+        if ops[k]["part"] and last.get(e) == ops[k]["part"][0]:
+            free[e] -= ops[k]["part"][1][QUEUES.index(e)]
+        last[e] = ops[k]["part"] and ops[k]["part"][0]
         seq.append(k)
         for x in succ[k]:
             at[x] = max(at[x], free[e] + ops[k]["lat"] + lat if k in ops[x]["deps"] else free[e])
@@ -542,19 +582,29 @@ def polish(plans, seq, on, rounds, heat):
     pred = [o["deps"] | o["order"] for o in ops]
     sets = [([price(o, "v") for o in x], [price(o, "s") for o in x], [o["lat"] + lat for o in x], w) for x, lat, w in plans]
 
-    def run(sq):
+    part = [o["part"][0] if o["part"] else -1 - k for k, o in enumerate(ops)] + [None]
+    fixed = [o["part"][1] if o["part"] else None for o in ops]
+
+    def run(sq, at=0, old=None):
+        first = [-1] * 6
+        for k in sq[:at]:
+            first[eng[k]] = k
         out = []
-        for a, b, tail, w in sets:
-            free, last = [0.0] * 6, [-1] * 6
-            end, start, why = [0.0] * n, [0.0] * n, [-1] * n
-            for k in sq:
+        for x, (a, b, tail, w) in enumerate(sets):
+            start, why, end = [list(y) for y in old[x][1:]] if old else ([0.0] * n, [-1] * n, [0.0] * n)
+            last = list(first)
+            free = [end[k] - tail[k] if k >= 0 else 0.0 for k in last]
+            for k in sq[at:]:
                 e = eng[k]
-                t, y = free[e], last[e]
+                y = z = last[e]
+                t = free[e]
                 for d in deps[k]:
                     if end[d] > t:
                         t, y = end[d], n + d
                 start[k], why[k] = t, y
                 t += b[k] if e else a[k]
+                if part[k] == part[z]:
+                    t -= fixed[k][e]
                 free[e], last[e] = t, k
                 end[k] = t + tail[k]
             out.append((max(end) * w, start, why, end))
@@ -585,7 +635,7 @@ def polish(plans, seq, on, rounds, heat):
         flip = u if ops[u]["swap"] else v if ops[v]["swap"] else -1
         if flip >= 0 and rnd() < 0.3:
             eng[flip] ^= 1
-            new = seq
+            new, a = seq, seq.index(flip)
         else:
             flip = -1
             if u in pred[v]:
@@ -611,7 +661,7 @@ def polish(plans, seq, on, rounds, heat):
                     continue
                 early.reverse()
                 new = seq[:a] + early + [x for x in seq[a:b] if x not in early] + seq[b + 1:]
-        r = run(new)
+        r = run(new, a, res)
         if r[0] <= now + heat * (1.0 - it / rounds) * rnd() ** 3:
             now, res = r
             seq, arcs = new, None
@@ -620,6 +670,29 @@ def polish(plans, seq, on, rounds, heat):
         elif flip >= 0:
             eng[flip] ^= 1
     return best, keep[0], [QUEUES[e] for e in keep[1]]
+
+
+def join(ops, seq):
+    runs, last = {}, {}
+    for k in seq:
+        o = ops[k]
+        if o["part"]:
+            z = last.get(o["eng"])
+            if z is not None and ops[z]["part"] and ops[z]["part"][0] == o["part"][0]:
+                o["run"] = ops[z]["run"]
+                o["run"].append(k)
+            else:
+                o["run"] = [k]
+                runs.setdefault(o["part"][0], []).append(o["run"])
+        last[o["eng"]] = k
+    for lst in runs.values():
+        a = 0
+        for run in lst:
+            b = a + sum(ops[k]["part"][2] for k in run)
+            for k in run:
+                ops[k]["calls"] = ops[k]["part"][3](ops[k]["eng"], a, b) if k == run[0] else []
+                ops[k]["cost"] -= 0.0 if k == run[0] else ops[k]["part"][1][QUEUES.index(ops[k]["eng"])]
+            a = b
 
 
 _PLAN = {}
@@ -637,6 +710,7 @@ def plan(cfg=CFG):
             if o["swap"]:
                 o["eng"] = e
                 o["cost"], o["calls"] = o["swap"][e]
+        join(ops, seq)
         _PLAN["ops"], _PLAN["seq"] = ops, seq
     return _PLAN["ops"], _PLAN["seq"]
 

import numpy as np
from concourse.mybir import AluOpType as ALU, ActivationFunctionType as AF

NB, NL, NS, NT, TH = 1280, 256, 64, 4, 1250
NW = NB + 2 * NS * NT
MUL = 2048
RB = 4
HEAD = 96

CFG = {
    "chunks": [96, 96, 64], "ab": 4, "nd": 4, "piece": 12, "half": 64, "early": True, "mask": (),
    "wage": (700, 900, 1200), "steal": (3000, 4000), "look": 100.0, "polish": 30000, "heat": 60.0,
    "bias": dict([(x, 4000.0) for x in ("exm", "C", "vrep", "cvt")] + [(x, 2000.0) for x in ("amin", "ex", "post")]
                 + [(x, -1000.0) for x in ("gCf", "v4", "scat")] + [(x, -1800.0) for x in ("", "cmp", "min", "gp", "cnt")]),
    "ov": 20.0, "os": 30.0, "mn": 50, "oi": 45.0, "hop": 2500.0,
}
COSTS = [{"cyc": 0.84, "pe": 0.42, "lat": 185.0, "G": 1.56, "SC": 3.8, "ov": 6.0, "os": 12.0, "mn": 61, "hop": 1800.0, "weight": 0.55},
         {"cyc": 1.2, "pe": 0.6, "lat": 170.0, "G": 1.9, "SC": 5.0, "ov": 8.0, "os": 16.0, "mn": 60, "hop": 2300.0, "weight": 0.33}]


def span(L):
    return -(-(HEAD + 20 * L) // 80) * 80


def layout(cfg):
    f32, bf, f16, i32, u16 = "float32", "bfloat16", "float16", "int32", "uint16"
    flat = {
        "chi": (NB, i32), "Cw": (NW + 256, f32), "K": (NW, bf), "K0": (8, bf), "psend": (NT * NL, bf), "pin": (NL, bf),
        "hI": (64, i32), "ci": (8, i32), "cf": (16, f32), "U": (128, f32), "C5": (4, f32), "xo": (8, u16), "TB": (16, f32), "RS": (512, f32), "JJ": (5 * HEAD, bf),
        "SY": (16, bf), "SM": (16, bf), "EM": (128, f32), "I1": (128, bf), "I2": (128, bf), "LA": (128, bf),
        "G8": (256, bf), "GQ": (256, bf), "BOr": (128, bf), "BOh": (128, f16), "ones": (128, bf), "R16": (128, f32),
        "D0": (128, f32), "SP": (15 * cfg["chunks"][0] + 32, bf),
        "mk": (112, f32), "C32": (128, f32), "Dq": (128, f32), "Dt": (256, f32), "R2": (128, bf), "DG": (128, bf), "ND": (32, bf),
        "TG0": (8, f32), "TG": (16, f32), "Dm": (16, f32), "qoff": (2, u16),
        "NO": (NT * 128, f32), "Z": (224, f16), "X": (704, bf), "LG": (512, bf), "sm": (64, f32), "nm": (8, f32), "qsc": (128, f32),
        "sl": (4, bf), "zi": (2, i32), "zf": (1, f32), "V": (384, f32), "E2": (64, f32), "sU": (16, u16), "jF": (8, f32), "jU": (8, u16),
    }
    for t in range(NT):
        flat["q%d" % t] = (NL, bf)
        flat["hU%d" % t] = (64, u16)
        flat["Q%d" % t] = ((RB + 1) * NL, bf)
    NC = len(cfg["chunks"])
    for c, L in enumerate(cfg["chunks"]):
        for name, n, ty in (("key", 16 * L, bf), ("kU", L, u16), ("kF", 2 * L, f16), ("pr", L, f16), ("sc", L, f32), ("m", 256, f32),
                            ("lo", 144, f16), ("l8", 8, f32), ("nU", 8, u16), ("vU", 16, u16), ("Y", (NT + 1) * span(L), bf), ("M", 20 * L, bf)):
            flat["%s%d" % (name, c)] = (n, ty)
        for name, n, ty in (("OH", HEAD + 20 * L, bf), ("LB", 128, f16), ("RJ", 128, f32)):
            flat["%s_%d" % (name, L)] = (n, ty)
    sc = {k: ("sbuf", [128, n], ty) for k, (n, ty) in flat.items()}
    for k in ["d%d" % k for k in range(cfg["nd"])] + ["s%d" % c for c in range(NC)] + (["misc"] if cfg["nd"] + NC < 8 else []):
        sc[k] = ("psum", [128, 512], f32)
    sems = ["cv", "cs", "ct", "cg", "ls", "rq", "aq1", "aq2", "aq3", "lq", "lh", "lk", "lk0", "lc0", "lc1", "lc2", "lc3", "syc"]
    for c in range(NC):
        sems.append("syp%d" % c)
        for t in range(NT):
            sems.append("ap%d_%d" % (t, c))
    return sc, sems


SCRATCH, SEMAPHORES = layout(CFG)


def R(name, a, b, step=1):
    return (name, a, b, step)


def B(name, a, b, u, w=None):
    return ("box", name, a, b, u, w)


def IND(win, off):
    return ("ind", win, off)


def cnt(x):
    if x[0] == "ind":
        return 16 * cnt(x[2])
    if x[0] == "box":
        return (x[3] - x[2]) * (1 if x[5] is None else x[5] - x[4])
    return len(range(x[1], x[2], x[3]))


def ap(T, x):
    if not isinstance(x, tuple):
        return x
    if x[0] == "ind":
        return ap(T, x[1]).indirect(ap(T, x[2]))
    if x[0] == "box":
        w, a = RB + 1, HEAD % (RB + 1) if x[1][0] == "Y" else 0
        return T[x[1]][:, a + w * x[2] + x[4]:a + w * x[3]:w] if x[5] is None else T[x[1]][:, a + w * x[2]:a + w * x[3]]
    if len(x) > 4 and x[4] < 128:
        return T[x[0]][0:x[4], x[1]:x[2]:x[3]]
    if x[3] == 1:
        return T[x[0]][:, x[1]:x[2]]
    return T[x[0]][:, x[1]:x[2]:x[3]]


def named(x):
    return named(x[1]) if x[0] == "ind" else x[1] if x[0] == "box" else x[0]


def area(x):
    if x[0] == "box":
        return (x[1], x[2], x[3], x[4], x[4] + 1 if x[5] is None else x[5], True)
    if x[0][0] == "Y":
        return (x[0], (x[1] - HEAD % 5) // 5, -(-(x[2] - HEAD % 5) // 5), 0, 5, False)
    return (x[0], x[1], x[2], 0, 1, x[3] == 1)


def build(cfg):
    sc, _ = layout(cfg)
    G, cyc, ch = cfg["G"], cfg["cyc"], cfg["chunks"]
    NC = len(ch)
    ops, hist, banks, age = [], {}, {}, [99]

    def add(eng, cost, reads, writes, calls, sem=None, lat=0.0, after=(), tag=""):
        k = len(ops)
        deps, order = set(after), set()
        acc = []
        for xs, w in ((reads, False), (writes, True)):
            for x in xs:
                if isinstance(x, tuple):
                    if x[0] == "ind":
                        acc += [(area(x[1])[:5] + (False,), w), (area(x[2]), False)]
                    else:
                        acc.append((area(x), w))
        for (name, a, b, u, v, full), w in acc:
            if name not in sc:
                continue
            ps = sc[name][0] == "psum"
            keep = []
            for e in hist.setdefault(name, []):
                o, a2, b2, u2, v2, ow = e
                if o != k and a2 < b and a < b2 and u2 < v and u < v2 and (w or ow):
                    if ps and ops[o]["eng"] == eng and eng == "t":
                        order.add(o)
                    else:
                        deps.add(o)
                if not (w and full and a <= a2 and b2 <= b and u <= u2 and v2 <= v):
                    keep.append(e)
            keep.append((k, a, b, u, v, w))
            hist[name] = keep
            if ps:
                st = banks.setdefault(name, [None, [], []])
                if st[0] != eng:
                    st[0], st[2], st[1] = eng, st[1], []
                deps.update(st[2])
                if eng == "t":
                    order.update(o for o in st[1] if o != k)
                if k not in st[1]:
                    st[1].append(k)
        deps.discard(k)
        ops.append({"eng": eng, "cost": cost, "deps": deps, "order": order - deps, "calls": calls, "sem": sem, "lat": lat, "tag": tag,
                    "swap": None, "part": None, "age": age[0]})
        return k

    def two(*xs):
        return all(sc[named(x)][2] in ("bfloat16", "float16", "uint16") for x in xs)

    def vcost(n, rate):
        return cfg["ov"] + max(n * rate, cfg["mn"]) * cyc + (cfg["oi"] if rate in (G, cfg["SC"]) else 0)

    def scost(a):
        return cfg["os"] + (cnt(a) * cyc * G + cfg["oi"] if a[0] == "ind" else max(cnt(a), cfg["mn"]) * cyc)

    def rate(out, a, plain):
        return G if a[0] == "ind" else cfg["SC"] if out[0] == "ind" else plain

    def copy(out, a, tag=""):
        return add("v", vcost(cnt(a), rate(out, a, 0.5 if two(out, a) else 1)), [a], [out],
                   [lambda q, T: q.tensor_copy(ap(T, out), ap(T, a))], tag=tag)

    def tt(out, a, b, op, tag=""):
        ps = any(sc[named(x)][0] == "psum" for x in (a, b))
        return add("v", vcost(cnt(a), rate(out, a, 1 if ps else 2)), [a, b], [out],
                   [lambda q, T: q.tensor_tensor(ap(T, out), ap(T, a), ap(T, b), op)], tag=tag)

    def ts(out, a, s1, op0, s2=None, op1=None, tag=""):
        if op1 is None:
            f = lambda q, T: q.tensor_scalar(ap(T, out), ap(T, a), ap(T, s1), None, op0)
        else:
            f = lambda q, T: q.tensor_scalar(ap(T, out), ap(T, a), ap(T, s1), ap(T, s2), op0, op1)
        return add("v", vcost(cnt(a), rate(out, a, 0.5 if two(out, a) else 1)), [a, s1, s2], [out], [f], tag=tag)

    def mset(out, val):
        return add("v", vcost(cnt(out), 0.5 if two(out) else 1), [], [out], [lambda q, T: q.memset(ap(T, out), val)])

    def scan(out, d0, d1, op0, op1, tag=""):
        return add("v", vcost(cnt(d1), 0.5 if two(out, d0, d1) else 1), [d0, d1], [out],
                   [lambda q, T: q.tensor_tensor_scan(ap(T, out), ap(T, d0), ap(T, d1), 0.0, op0, op1)], tag=tag)

    def act(out, a, func, tag="", scale=None, bias=None):
        if scale is not None:
            f = lambda q, T: q.activation(ap(T, out), ap(T, a), func, scale=ap(T, scale))
        elif bias is not None:
            f = lambda q, T: q.activation(ap(T, out), ap(T, a), func, bias=ap(T, bias))
        else:
            f = lambda q, T: q.activation(ap(T, out), ap(T, a), func)
        return add("s", scost(a), [a, scale, bias], [out], [f], tag=tag)

    def copies(out, a):
        return {"s": [lambda q, T: q.activation(ap(T, out), ap(T, a), AF.Copy)], "v": [lambda q, T: q.tensor_copy(ap(T, out), ap(T, a))]}

    def either(eng, out, a, tag=""):
        k = act(out, a, AF.Copy, tag)
        ops[k]["swap"] = {"s": (ops[k]["cost"], ops[k]["calls"]),
                          "v": (vcost(cnt(a), rate(out, a, 0.5 if two(out, a) else 1)), copies(out, a)["v"])}
        ops[k]["eng"] = eng
        ops[k]["cost"], ops[k]["calls"] = ops[k]["swap"][eng]
        return k

    def affine(out, a, scale, bias, tag=""):
        k = ts(out, a, scale, ALU.mult, bias, ALU.add, tag)
        ops[k]["swap"] = {"v": (ops[k]["cost"], ops[k]["calls"]),
                          "s": (scost(a), [lambda q, T: q.activation(ap(T, out), ap(T, a), AF.Identity, bias=ap(T, bias), scale=ap(T, scale))])}
        return k

    def fill(out):
        a = R("JJ", 0, cnt(out))
        k = act(out, a, AF.Copy, scale=0.0)
        ops[k]["swap"] = {"s": (ops[k]["cost"], ops[k]["calls"]), "v": (vcost(cnt(out), 0.5), [lambda q, T: q.memset(ap(T, out), 0.0)])}

    def mm(lst, tag=""):
        cost, calls = 0.0, []
        for (o, l, r, st, sp) in lst:
            cost += max(64, cnt(r)) * cfg["pe"] * (4 if sc[named(l)][2] == "float32" else 1)
            calls.append(lambda q, T, o=o, l=l, r=r, st=st, sp=sp: q.matmul(ap(T, o), ap(T, l), ap(T, r), st, sp))
        return add("t", cost, [x[1] for x in lst] + [x[2] for x in lst], [x[0] for x in lst], calls, lat=60.0, tag=tag)

    def iota(out, pat, base, cm=0):
        if sc[named(out)][2] == "int32":
            f = lambda q, T: q.iota(ap(T, out), pat, base, cm)
        else:
            f = lambda q, T: q.iota(ap(T, out), pat, base, cm, allow_small_or_imprecise_dtypes=True)
        return add("g", 160 + 2 * cyc * cnt(out), [], [out], [f])

    def gcopy(out, a, after=()):
        return add("g", 210 + 2 * cyc * cnt(a), [a], [out],
                   [lambda q, T: q.affine_select(ap(T, out), ap(T, a), [[0, cnt(a)]], ALU.is_ge, 0.0, 0, 0)], after=after, tag="rep")

    def dma(eng, out, a, sem, lat):
        return add(eng, 60.0, [a], [out], [lambda q, T: q.dma_start(ap(T, out), ap(T, a))], sem=sem, lat=lat, tag="dma")

    def col(k):
        return R("cf", k, k + 1)

    def whole(n):
        return R(n, 0, sc[n][1][1])

    dma("y", whole("hI"), R("hv", 0, 64), "lh", 2000)
    for k in range(4):
        dma("y", R("chi", 320 * k, 320 * k + 320), R("ch", 320 * k, 320 * k + 320), "lc%d" % k, 2300 + 500 * k)
    dma("s", whole("q0"), R("qs", 0, NL), "lq", 2000)
    dma("s", whole("K0"), R("kb", 0, 8), "lk0", 2000)
    dma("s", R("K", 8, NB), R("kb", 8, NB), "lk", 4400)

    iota(R("ci", 0, 1), [[0, 1]], 0, 1)
    iota(col(3), [[0, 1]], 0, 1)
    iota(whole("U"), [[1, 128]], 0)
    iota(whole("R16"), [[0, 8], [1, 16]], 0)
    iota(whole("JJ"), [[0, HEAD], [1, 5]], 0)
    ts(R("ci", 1, 2), R("ci", 0, 1), 15, ALU.bitwise_and)
    ts(R("ci", 2, 3), R("ci", 0, 1), 4, ALU.arith_shift_right)
    ts(R("ci", 3, 4), R("ci", 0, 1), 14, ALU.bitwise_and)
    ts(R("ci", 4, 5), R("ci", 0, 1), 3, ALU.bitwise_and)
    copy(R("cf", 0, 3), R("ci", 1, 4))
    affine(col(4), col(0), -2048.0, 15 * 2048.0)
    affine(col(5), col(2), 2.0, 0.0)
    affine(col(6), col(2), -2.0 ** 20, 28 * 2.0 ** 19)
    affine(col(10), col(2), 2.0 ** 20, -28 * 2.0 ** 19)
    affine(col(7), col(2), 2.0, 3.0)
    affine(col(8), col(0), 2.0, 0.0)
    affine(col(9), col(0), -1.0, 0.0)
    affine(col(11), col(0), 1.0, -1.0)
    affine(col(15), col(0), 5.0, float(HEAD))
    ts(R("cf", 12, 14), R("U", 0, 2), col(3), ALU.is_equal)
    affine(col(14), col(12), 5.0, 0.0)
    ts(R("qoff", 0, 1), R("ci", 4, 5), 32, ALU.mult, 31, ALU.add)
    ts(whole("I1"), whole("U"), col(3), ALU.is_equal)
    affine(whole("I2"), whole("I1"), -1.0, 0.0)
    affine(whole("LA"), whole("U"), col(12), col(13))
    for L in sorted(set(ch), reverse=True):
        iota(whole("RJ_%d" % L), [[0, 8], [5 * L, 4], [1, 4]], HEAD)
        ts(whole("LB_%d" % L), whole("RJ_%d" % L), col(13), ALU.mult, col(14), ALU.add)
        fill(R("OH_%d" % L, 0, HEAD))
        for b in range(4):
            ts(R("OH_%d" % L, HEAD + 5 * L * b, HEAD + 5 * L * (b + 1)), R("JJ", 0, 5 * L), float(4 * b), ALU.add, col(0), ALU.is_equal)
    for u in range(2):
        iota(R("RS", 256 * u, 256 * u + 256), [[0, 256]], 0)
    iota(R("TB", 0, 8), [[0, 8]], MUL * TH + HEAD + 20 * max(ch))
    iota(R("TB", 8, 16), [[0, 8]], MUL * TH + HEAD + 20 * max(ch), 1)
    iota(whole("G8"), [[0, 2], [1, 8], [0, 16]], 0)
    ts(whole("GQ"), whole("G8"), col(1), ALU.is_equal, float(MUL), ALU.mult)
    ts(whole("BOh"), R("G8", 0, 128), col(1), ALU.is_equal)
    affine(whole("BOr"), R("GQ", 0, 128), HEAD / MUL - 1.0, float(MUL))
    iota(whole("ones"), [[0, 128]], 1)
    ts(whole("EM"), whole("R16"), col(0), ALU.is_equal)
    for c, L in enumerate(ch):
        for w in range(NT + 1):
            a = (w * span(L) + HEAD) // 5
            zero = fill if w in (0, NT) else lambda x: iota(x, [[0, cnt(x)]], 0)
            zero(B("Y%d" % c, a, a + 4 * L, RB))
            if w == 0 or L < HEAD:
                zero(R("Y%d" % c, w * span(L) + (L if w else 0), w * span(L) + HEAD))
        mset(whole(("l8%d" if c in cfg["mask"] else "lo%d") % c), 0.0)
    if cfg["mask"]:
        copy(whole("xo"), R("U", 0, 8))
    either("v", whole("SY"), R("GQ", 0, 256, 16))
    affine(whole("SM"), R("GQ", 0, 256, 16), -2.0, 0.0)
    affine(whole("D0"), whole("EM"), 65536.0 + 2048.0, -2048.0)
    affine(whole("C5"), R("U", 0, 4), 80.0, col(15))
    iota(whole("SP"), [[0, 15 * ch[0] + 32]], 0)
    for b in range(4):
        ts(R("SP", 5 * ch[0] * b, 5 * ch[0] * b + 4), R("U", 4 * b, 4 * b + 4), col(0), ALU.is_lt)
        ts(R("SP", 5 * ch[0] * b + 16, 5 * ch[0] * b + 20), R("U", 4 * b, 4 * b + 4), col(11), ALU.is_equal)
    act(whole("mk"), R("R16", 0, 112), AF.Sign, bias=col(9))
    iota(R("mk", 16, 64), [[0, 48]], 1)
    iota(whole("C32"), [[0, 4], [1, 32]], 0)
    iota(whole("R2"), [[0, 4], [1, 16], [0, 2]], 0)
    ts(whole("DG"), whole("R2"), col(0), ALU.is_equal)
    ts(whole("ND"), R("R2", 0, 32), col(0), ALU.is_equal, -1.0, ALU.mult)
    ts(whole("Dq"), whole("C32"), col(5), ALU.is_equal, -float(2 ** 25), ALU.mult)
    ts(R("Dt", 0, 128), whole("C32"), col(5), ALU.is_lt, float(2 ** 19), ALU.mult)
    ts(R("Dt", 128, 256), whole("C32"), col(7), ALU.is_gt, float(2 ** 19), ALU.mult)
    tt(R("Dt", 0, 128), R("Dt", 0, 128), R("Dt", 128, 256), ALU.add)
    tt(whole("Dq"), whole("Dq"), R("Dt", 0, 128), ALU.add)
    iota(whole("TG0"), [[1, 2], [32, 4]], 0)
    affine(whole("TG0"), whole("TG0"), 1.0, col(8))
    iota(whole("Dm"), [[128 + NB, 2], [16, 8]], NW - NB)
    affine(whole("Dm"), whole("Dm"), 1.0, col(0))
    for t in range(NT):
        iota(R("NO", 128 * t, 128 * t + 64), [[-2, 64]], -(NB + 128 * t + 1))
        iota(R("NO", 128 * t + 64, 128 * t + 128), [[4, 32], [-2, 2]], NB + 128 * t + 2)

    iota(R("Cw", NB, NW + 256), [[0, NW + 256 - NB]], 0)
    iota(R("V", 64, 128), [[0, 64]], 0)
    mset(R("Cw", 0, 1), 0.0)
    for k in range(4):
        a = max(1, 320 * k)
        copy(R("Cw", a, 320 * k + 320), R("chi", a, 320 * k + 320))
    mset(R("K", 0, 1), -2048.0)
    copy(R("K", 1, 8), R("K0", 1, 8))
    for u in range(RB + 1):
        gcopy(B("Q0", 0, NL, u), whole("q0"))

    misc = "misc" if "misc" in sc else "s0"
    copy(whole("hU0"), whole("hI"))
    k = add("g", 3000.0, [whole("q0"), whole("hU0")], [], [("sendq",)], sem="ls")
    for t in range(1, NT):
        add("n", 0.0, [], [whole("q%d" % t), whole("hU%d" % t)], [], sem="aq%d" % t, lat=3 * cfg["hop"], after=[k])

    turn, sent = [0], []

    def step(t, c, s):
        L, f0 = ch[c], sum(ch[:c])
        NH = L // 16
        key, Y, M, S = "key%d" % c, "Y%d" % c, "M%d" % c, "s%d" % c
        kU = "kU%d" % c
        w0 = span(L) * (NT if s == 1 else t)
        r0 = (w0 + HEAD) // 5

        def p_of(w):
            return R(Y, span(L) * w, span(L) * w + L)

        p = p_of(NT if s == 1 else t)
        plain = t + s == 0
        base = NB + 128 * t
        voff = R("hU%d" % t, 16 * t + f0 // 16, 16 * t + f0 // 16 + NH) if s == 0 else R("vU%d" % c, (s - 1) * 8, (s - 1) * 8 + NH)
        copy(whole(kU), IND(whole("chi") if plain else R("Cw", 0, NB if s == 0 else NW), voff), "gC")
        kF = R("kF%d" % c, s * L, s * L + L)
        if s < 2:
            copy(kF, whole(kU), "gCf")
        elif c == 0:
            copy(R("V", 320, 384), R(kU, 0, NS), "gCf")
        m = -(-L // cfg["piece"])
        for u in range(m):
            a, b = 2 * (L // 2 * u // m), 2 * (L // 2 * (u + 1) // m)
            k = either("s", R(key, 16 * a, 16 * b), IND(R("K", 0, base), R(kU, a, b)), "gK")
            ops[k]["part"] = ((t, c, s), (cfg["ov"] + cfg["oi"], cfg["os"] + cfg["oi"]), b - a,
                              lambda e, a, b: copies(R(key, 16 * a, 16 * b), IND(R("K", 0, base), R(kU, a, b)))[e])
        mm([(R(S, 0, 256) + (L,), R("q%d" % t, f0, f0 + L), whole("GQ"), True, False),
            (R(S, 128, 256) + (L,), R("LA", 0, L), whole("LB_%d" % L), False, False)], "low")

        def sums(src, weight, blocks, slots, last):
            a = r0 if src == Y else 0
            lst = [(R(S, RB * b + u, 256, 16) + (L,), B(src, a + L * b, a + L * b + L, u), whole(weight), False, False)
                   for b in blocks for u in slots]
            mm(lst[:-1] + [lst[-1][:4] + (last,)], "sum")

        ab = cfg["ab"]
        fit = 512 // (ab * L)
        halves = [(0, L)] if L < 2 * cfg["half"] else [(0, L // 2), (L // 2, L)]
        for b0 in range(0, 16 // RB, ab):
            blocks = range(b0, b0 + ab)
            for u0 in range(0, RB, fit):
                slots = range(u0, min(u0 + fit, RB))
                if plain:
                    for u in slots:
                        for b in blocks:
                            either("v", B(Y, r0 + L * b, r0 + L * b + L, u), R(key, RB * b + u, 16 * L, 16), "abs")
                else:
                    d = "d%d" % (turn[0] % cfg["nd"])
                    turn[0] += 1
                    rows = [RB * b + u for u in slots for b in blocks]
                    parts = [[(R(d, L * n + i0, L * n + i1), whole("I1"), R(key, 16 * i0 + j, 16 * i1, 16)) for n, j in enumerate(rows)]
                             for i0, i1 in halves]
                    minus = [(R(d, L * n, L * n + L), whole("I2"), p) for n in range(len(rows))]
                    parts = [minus] + parts if s > 0 and cfg["early"] else parts + [minus]
                    for n, part in enumerate(parts):
                        mm([x + (n + u == 0, n == len(parts) - 1 and u == len(part) - 1) for u, x in enumerate(part)], "d")
                    for n, u in enumerate(slots):
                        act(B(Y, r0 + L * b0, r0 + L * (b0 + ab), u), R(d, ab * L * n, ab * L * (n + 1)), AF.Abs, "abs")
                sums(Y, "SY", blocks, slots, False)
            for b in blocks:
                scan(B(M, L * b, L * b + L, 0, RB + 1), B("Q%d" % t, f0, f0 + L, 0, RB + 1),
                     B(Y, r0 + L * b, r0 + L * b + L, 0, RB + 1), ALU.max, ALU.min, "min")
                sums(M, "SM", [b], range(RB), b == 16 // RB - 1)
        m, lo = "m%d" % c, "lo%d" % c
        scan(whole(m) + (L,), R("RS", 256 * (t % 2), 256 * (t % 2) + 256) + (L,), R(S, 0, 256) + (L,), ALU.max, ALU.min, "amin")
        if c in cfg["mask"]:
            tt(whole("l8%d" % c) + (L,), R(m, 143, 256, 16) + (L,), R(m, 15, 128, 16) + (L,), ALU.subtract, "ex")
            tt(R(lo, 0, 128), IND(whole("l8%d" % c), whole("xo")), whole("EM"), ALU.mult, "ex")
            mm([(R(S, 256, 256 + NH), R(lo, 0, 128), R("BOh", 0, L, 16), True, True)], "exm")
        else:
            tt(R(lo, 15, 143, 16) + (L,), R(m, 143, 256, 16) + (L,), R(m, 15, 128, 16) + (L,), ALU.subtract, "ex")
            mm([(R(S, 256, 256 + NH), R(lo, 15 - r, 143 - r), R("I1", r, L, 16), r == 0, r == 15) for r in range(16)], "exm")
        nU = R("nU%d" % c, 0, NH)
        copy(nU, R(S, 256, 256 + NH), "C")
        if c == 0 and s == 2:
            for u in range(4):
                ts(R("LG", 128 * u, 128 * u + 128), whole("BOr"), R(S, 256 + u, 257 + u), ALU.is_le, 2048.0, ALU.mult, "go")
        if c == 0 and s > 0:
            tt(R("jF", 4 * s - 4, 4 * s), R(S, 256, 260), whole("C5"), ALU.subtract, "pre")
        new = p_of(t if s else NT) if s < 2 else R("psend", NL * t + f0, NL * t + f0 + L)
        either("s", new, IND(R(Y, w0, w0 + HEAD + 20 * L), nU), "gp")
        if s < 2:
            pr, vU = "pr%d" % c, R("vU%d" % c, s * 8, s * 8 + NH)
            tt(whole(pr), IND(whole("OH_%d" % L), nU), kF, ALU.mult, "oh")
            lst = [(R(S, 272, 272 + L), whole("BOh"), whole(pr), True, True)]
            if c == 0:
                lst.append((R(S, 400, 464), whole("BOh"), R(pr, 0, 64), True, True))
                lst.append((R(S, 464, 512), whole("BOh"), R(pr, 16, 64), True, True))
            mm(lst, "vrep")
            scan(whole("sc%d" % c), R("D0", 0, L), R(S, 272, 272 + L), ALU.add, ALU.min, "scan")
            ts(vU, R("sc%d" % c, 15, L, 16), col(4), ALU.add, tag="cvt")
            if c == 0:
                tt(R("Z", s, 224, 2), R(S, 400, 512), whole("mk"), ALU.mult)
                affine(R("TG", 8 + 4 * s, 12 + 4 * s), R("sc0", 15, 64, 16), 1.0, col(4))
                if t < NT - 1:
                    either("s", R("K", base + s, base + 128, 2), IND(R("K", 0, base), R("vU0", 8 * s, 8 * s + 4)))
        else:
            dst = p_of(t + 1) if t < NT - 1 else R("pin", f0, f0 + L)
            k = add("g", 300.0, [new], [], [("sendp", new, dst, "ap%d_%d" % (t, c))], sem="ls")
            sent.append(k)
            add("n", 0.0, [], [dst], [], sem="ap%d_%d" % (t, c), lat=2 * cfg["hop"], after=[k])
            if t == NT - 1:
                dma("y", R("yp", f0, f0 + L), dst, "syp%d" % c, 2200)

    def slices(t):
        top = 15 * ch[0] + 3
        affine(R("TG", 0, 8), whole("TG0"), 1.0, float(128 * t))
        tt(R("sm", 0, 4), R("TG", 8, 12), R("TG", 12, 16), ALU.not_equal)
        for u in range(2):
            copy(R("jU", 4 * u, 4 * u + 4), R("jF", 4 * u, 4 * u + 4), "pre")
        ts(R("sm", 4, 8), R("jF", 0, 4), float(top), ALU.is_lt, tag="pre")
        tt(R("sm", 8, 12), R("sm", 0, 4), R("sm", 4, 8), ALU.mult, "pre")
        for u in range(2):
            tt(R("nm", 4 * u, 4 * u + 4), R("TG", 8 + 4 * u, 12 + 4 * u), R("sm", 8, 12), ALU.mult, "pre")
        affine(R("sm", 16, 32), whole("TG"), 1.0, col(10), "pre")
        seg = [(0, 128, [(0, 128, 0)]), (64, 160, [(0, 64, 64), (64, 96, 32)]), (96, 192, [(0, 32, 96), (64, 96, 64)]), (192, 224, [(0, 32, 96)])]
        lst, x = [(R(misc, 256, 384), R("GQ", 0, 128), whole("DG"), True, False)], 0
        for c, (a, b, parts) in enumerate(seg):
            lg = R("LG", 128 * c, 128 * c + 128)
            lst.append((R(misc, 256 + 32 * c, 288 + 32 * c), lg, whole("ND"), False, False))
            for u in range(2):
                ts(R("X", x, x + b - a), R("Z", a, b), R("nm", 4 * u + c, 4 * u + c + 1), ALU.is_equal, tag="cmp")
                for (i0, i1, to) in parts:
                    lst.append((R(misc, 256 + to, 256 + to + i1 - i0), lg, R("X", x + i0, x + i1), False, c == 3 and u == 1))
                x += b - a
        mm(lst, "cnt")
        scan(whole("qsc"), whole("Dq"), R(misc, 256, 384), ALU.add, ALU.max, "post")
        tt(R("sm", 32, 48), IND(whole("qsc"), R("qoff", 0, 1)), R("sm", 16, 32), ALU.add, "post")
        tt(R("sm", 48, 64), R("sm", 32, 48), whole("Dm"), ALU.min, "post")
        copy(whole("sU"), R("sm", 48, 64), "post")
        ra, rb, jj, kk = R("kF0", ch[0], ch[0] + NS), R("V", 320, 384), R("jU", 0, 4), R("jU", 4, 8)
        tt(R("V", 128, 192), IND(whole("SP"), jj), ra, ALU.mult, "v4")
        tt(R("V", 192, 256), IND(whole("SP"), kk), rb, ALU.mult, "v4")
        tt(R("V", 0, 64), IND(R("OH_%d" % ch[0], HEAD, HEAD + top + 1), jj), R("NO", 128 * t, 128 * t + 64), ALU.mult, "v4")
        tt(whole("E2"), IND(R("SP", 16, top + 17), jj), R("NO", 128 * t + 64, 128 * t + 128), ALU.mult, "v4")
        tt(R("V", 256, 320), whole("E2"), ra, ALU.add, "v4")
        if t < NT - 1:
            ts(whole("sl"), R("qsc", 31, 128, 32), col(6), ALU.is_equal)
            mm([(R(misc, 384, 385), whole("ones"), R("sl", u, u + 1), u == 0, u == 3) for u in range(4)])
            copy(R("zi", 0, 1), R(misc, 384, 385))
            ts(R("zi", 1, 2), R("zi", 0, 1), 63, ALU.bitwise_and)
            ts(whole("zf"), R("zi", 1, 2), MUL, ALU.mult)

    order = [(c, s) for s in range(3) for c in range(NC)]
    for t in range(NT):
        age[0] = t * len(order)
        affine(R("RS", 256 * (t % 2), 256 * (t % 2) + 256, 16), whole("TB"), 1.0, whole("zf") if t else 0.0)
        if t < NT - 1:
            for u in range(RB + 1):
                gcopy(B("Q%d" % (t + 1), 0, NL, u), whole("q%d" % (t + 1)), after=sent[-NC:])
        for u, (c, s) in enumerate(order):
            age[0] = t * len(order) + u
            step(t, c, s)
            if (c, s) == (0, 2):
                slices(t)
        if t == NT - 1:
            copy(R("Cw", 0, 1), R("chi", 0, 1))
        tt(IND(whole("Cw"), R("sU", 8, 16)), R("V", 256, 384), R("V", 128, 256), ALU.subtract, "scat")
        tt(IND(R("Cw", NB, NW + 256), R("sU", 0, 8)), R("V", 128, 256), R("V", 0, 128), ALU.subtract, "scat")
    dma("y", R("yc", 0, NW), R("Cw", 0, NW), "syc", 5000)
    return ops


QUEUES = "vstgyn"


def price(o, e):
    return o["swap"][e][0] if o["swap"] else o["cost"]


def schedule(ops, cfg):
    n, lat = len(ops), cfg["lat"]
    succ = [[] for _ in range(n)]
    left = [0] * n
    for k, o in enumerate(ops):
        for d in o["deps"] | o["order"]:
            succ[d].append(k)
            left[k] += 1
    prio = [0.0] * n
    for k in range(n - 1, -1, -1):
        prio[k] = ops[k]["cost"] + ops[k]["lat"] + max([prio[x] + lat for x in succ[k]], default=0.0)
    age = [o["age"] for o in ops]
    for k in range(n - 1, -1, -1):
        age[k] = min([age[k]] + [age[x] for x in succ[k]])
        prio[k] += cfg["bias"].get(ops[k]["tag"], 0.0) - cfg["wage"] * age[k]
    ready = {e: [] for e in QUEUES}
    at = [0.0] * n
    homes = ["vs" if o["swap"] else o["eng"] for o in ops]
    for k in range(n):
        if left[k] == 0:
            for e in homes[k]:
                ready[e].append(k)
    free = {e: 0.0 for e in ready}
    seq, on, last = [], [""] * n, {}
    while len(seq) < n:
        t0, e = min((max(free[e], min(at[k] for k in lst)), e) for e, lst in ready.items() if lst)

        def worth(x):
            return prio[x] - (cfg["steal"] if e == "v" and ops[x]["swap"] else 0.0)

        k = max((x for x in ready[e] if at[x] <= t0 + 1e-6), key=lambda x: (worth(x), -x))
        soon = [x for x in ready[e] if t0 + 1e-6 < at[x] <= t0 + min(cfg["look"], 0.5 * price(ops[k], e)) and worth(x) > worth(k)]
        if soon:
            k = min(soon, key=lambda x: at[x])
            t0 = at[k]
        for h in homes[k]:
            ready[h].remove(k)
        on[k] = e
        free[e] = t0 + price(ops[k], e)
        if ops[k]["part"] and last.get(e) == ops[k]["part"][0]:
            free[e] -= ops[k]["part"][1][QUEUES.index(e)]
        last[e] = ops[k]["part"] and ops[k]["part"][0]
        seq.append(k)
        for x in succ[k]:
            at[x] = max(at[x], free[e] + ops[k]["lat"] + lat if k in ops[x]["deps"] else free[e])
            left[x] -= 1
            if left[x] == 0:
                for h in homes[x]:
                    ready[h].append(x)
    return seq, on


def polish(plans, seq, on, rounds, heat):
    ops = plans[0][0]
    n = len(ops)
    eng = [QUEUES.index(e) for e in on]
    deps = [tuple(o["deps"]) for o in ops]
    pred = [o["deps"] | o["order"] for o in ops]
    sets = [([price(o, "v") for o in x], [price(o, "s") for o in x], [o["lat"] + lat for o in x], w) for x, lat, w in plans]

    part = [o["part"][0] if o["part"] else -1 - k for k, o in enumerate(ops)] + [None]
    fixed = [o["part"][1] if o["part"] else None for o in ops]

    def run(sq, at=0, old=None):
        first = [-1] * 6
        for k in sq[:at]:
            first[eng[k]] = k
        out = []
        for x, (a, b, tail, w) in enumerate(sets):
            start, why, end = [list(y) for y in old[x][1:]] if old else ([0.0] * n, [-1] * n, [0.0] * n)
            last = list(first)
            free = [end[k] - tail[k] if k >= 0 else 0.0 for k in last]
            for k in sq[at:]:
                e = eng[k]
                y = z = last[e]
                t = free[e]
                for d in deps[k]:
                    if end[d] > t:
                        t, y = end[d], n + d
                start[k], why[k] = t, y
                t += b[k] if e else a[k]
                if part[k] == part[z]:
                    t -= fixed[k][e]
                free[e], last[e] = t, k
                end[k] = t + tail[k]
            out.append((max(end) * w, start, why, end))
        return sum(r[0] for r in out), out

    state = [1]

    def rnd():
        state[0] = (state[0] * 6364136223846793005 + 1442695040888963407) % 2 ** 64
        return (state[0] >> 11) / 2.0 ** 53

    now, res = run(seq)
    best, keep = now, (list(seq), list(eng))
    arcs = None
    for it in range(rounds):
        if arcs is None:
            start = res[0][1]
            seq = [k for _, _, k in sorted((start[k], u, k) for u, k in enumerate(seq))]
            arcs = []
            for _, _, why, end in res:
                k = max(range(n), key=lambda x: end[x])
                while k >= 0:
                    w = why[k]
                    if 0 <= w < n:
                        arcs.append((w, k))
                    k = w - n if w >= n else w
        u, v = arcs[int(rnd() * len(arcs))]
        flip = u if ops[u]["swap"] else v if ops[v]["swap"] else -1
        if flip >= 0 and rnd() < 0.3:
            eng[flip] ^= 1
            new, a = seq, seq.index(flip)
        else:
            flip = -1
            if u in pred[v]:
                continue
            a, b = seq.index(u), seq.index(v)
            far = int(rnd() ** 2 * 4)
            if rnd() < 0.5:
                while far and b + 1 < n:
                    b += 1
                    far -= eng[seq[b]] == eng[u]
                if any(u in pred[x] for x in seq[a + 1:b + 1]):
                    continue
                new = seq[:a] + seq[a + 1:b + 1] + [u] + seq[b + 1:]
            else:
                while far and a > 0:
                    a -= 1
                    far -= eng[seq[a]] == eng[v]
                early = [v]
                for x in seq[b - 1:a - 1 if a else None:-1]:
                    if any(x in pred[y] for y in early):
                        early.append(x)
                if any(eng[x] == eng[v] for x in early[1:]):
                    continue
                early.reverse()
                new = seq[:a] + early + [x for x in seq[a:b] if x not in early] + seq[b + 1:]
        r = run(new, a, res)
        if r[0] <= now + heat * (1.0 - it / rounds) * rnd() ** 3:
            now, res = r
            seq, arcs = new, None
            if now < best:
                best, keep = now, (list(seq), list(eng))
        elif flip >= 0:
            eng[flip] ^= 1
    return best, keep[0], [QUEUES[e] for e in keep[1]]


def join(ops, seq):
    runs, last = {}, {}
    for k in seq:
        o = ops[k]
        if o["part"]:
            z = last.get(o["eng"])
            if z is not None and ops[z]["part"] and ops[z]["part"][0] == o["part"][0]:
                o["run"] = ops[z]["run"]
                o["run"].append(k)
            else:
                o["run"] = [k]
                runs.setdefault(o["part"][0], []).append(o["run"])
        last[o["eng"]] = k
    for lst in runs.values():
        a = 0
        for run in lst:
            b = a + sum(ops[k]["part"][2] for k in run)
            for k in run:
                ops[k]["calls"] = ops[k]["part"][3](ops[k]["eng"], a, b) if k == run[0] else []
                ops[k]["cost"] -= 0.0 if k == run[0] else ops[k]["part"][1][QUEUES.index(ops[k]["eng"])]
            a = b


_PLAN = {}


def plan(cfg=CFG):
    if not _PLAN:
        sets = [dict(cfg, **c) for c in COSTS]
        plans = [(build(c), c["lat"], c["weight"]) for c in sets]
        tries = [polish(plans, *schedule(x[0], dict(c, wage=w, steal=s)), 0, 0.0) for x, c in zip(plans, sets)
                 for w in cfg["wage"] for s in cfg["steal"]]
        _PLAN["score"], seq, on = polish(plans, *min(tries)[1:], cfg["polish"], cfg["heat"])
        ops = plans[0][0]
        for o, e in zip(ops, on):
            if o["swap"]:
                o["eng"] = e
                o["cost"], o["calls"] = o["swap"][e]
        join(ops, seq)
        _PLAN["ops"], _PLAN["seq"] = ops, seq
    return _PLAN["ops"], _PLAN["seq"]


def relay_of(core, T, topo):
    ok = [c for c in topo.cores_of(core) if T.rank_of(c) is None and all(topo.may_write(c, d) for d in T.cores)]
    same = [c for c in ok if topo.die(c) == topo.die(core)]
    return (same or ok)[0]


def put(g, T, topo, core, dst_core, out, src, sem):
    rid, pid = topo.addr(dst_core, core)
    g.remote_dma(ap(T, out), ap(T, src), T.sem[sem], T.sem.ls, pid, rid, topo.mask(core, dst_core))
    return len(topo.engines(core, dst_core))


def bundle(t):
    return [R("q%d" % t, 0, NL), R("hU%d" % t, 0, 64)]


def last_hop(T, topo, src_rank, dst_rank):
    a, b = T.cores[src_rank], T.cores[dst_rank]
    return a if topo.may_write(a, b) else relay_of(a, T, topo)


def relay_program(g, core, rank, T, topo):
    ops, seq = plan()
    N = len(T.cores)
    own = T.cores[rank]
    e = len(topo.engines(own, core))
    sent = 0
    for k in seq:
        for call in ops[k]["calls"]:
            if isinstance(call, tuple) and call[0] == "sendq":
                far = [t for t in range(1, NT) if last_hop(T, topo, rank, (rank + t) % N) == core]
                if far:
                    g.wait_ge(T.sem.rq, 2 * e)
                for t in far:
                    for o, s in zip(bundle(t), bundle(0)):
                        sent += put(g, T, topo, core, T.cores[(rank + t) % N], o, s, "aq%d" % t)
            elif isinstance(call, tuple) and last_hop(T, topo, rank, (rank + 1) % N) == core:
                g.wait_ge(T.sem[call[3]], e)
                sent += put(g, T, topo, core, T.cores[(rank + 1) % N], call[2], call[1], call[3])
    if sent:
        g.wait_ge(T.sem.ls, sent)


def rank_program(g, core, T, topo):
    rank = T.rank_of(core)
    N = len(T.cores)
    if rank is None:
        for r in range(N):
            if relay_of(T.cores[r], T, topo) == core:
                relay_program(g, core, r, T, topo)
        return
    ops, seq = plan()
    queue = {"v": g.vector, "s": g.scalar, "t": g.tensor, "g": g, "y": g.sync}
    own = {"v": "cv", "s": "cs", "t": "ct", "g": "cg"}
    relay = relay_of(core, T, topo)
    count = {}
    known = {e: {} for e in queue}
    done = {}
    for k in seq:
        o = ops[k]
        e = o["eng"]
        if e == "n":
            if o["sem"][1] == "q":
                frm, times = (rank - int(o["sem"][2])) % N, 2
            else:
                frm, times = (rank - 1) % N, 1
            count[o["sem"]] = times * len(topo.engines(last_hop(T, topo, frm, rank), core))
            done[k] = (o["sem"], count[o["sem"]], {})
            continue
        q, kn = queue[e], known[e]
        need = {}
        for d in o["deps"]:
            if done[d][0] != "ls" and done[d][1] > need.get(done[d][0], (0, None))[0]:
                need[done[d][0]] = (done[d][1], d)
        for s, (v, d) in sorted(need.items(), key=lambda x: -x[1][1]):
            if kn.get(s, 0) < v:
                q.wait_ge(T.sem[s], v)
                kn[s] = v
                for s2, v2 in done[d][2].items():
                    if kn.get(s2, 0) < v2:
                        kn[s2] = v2
        s = o["sem"] or own[e]
        for call in o["calls"]:
            if not isinstance(call, tuple):
                inc = 16 if o["sem"] else 1
                call(q, T).then_inc(T.sem[s], inc)
                count[s] = count.get(s, 0) + inc
            elif call[0] == "sendq":
                via = False
                for t in range(1, NT):
                    to = (rank + t) % N
                    if last_hop(T, topo, rank, to) != core:
                        via = True
                if via:
                    for x in bundle(0):
                        count[s] = count.get(s, 0) + put(g, T, topo, core, relay, x, x, "rq")
                for t in range(1, NT):
                    to = (rank + t) % N
                    if last_hop(T, topo, rank, to) == core:
                        for x, y in zip(bundle(t), bundle(0)):
                            count[s] = count.get(s, 0) + put(g, T, topo, core, T.cores[to], x, y, "aq%d" % t)
            else:
                to = (rank + 1) % N
                if last_hop(T, topo, rank, to) == core:
                    count[s] = count.get(s, 0) + put(g, T, topo, core, T.cores[to], call[2], call[1], call[3])
                else:
                    count[s] = count.get(s, 0) + put(g, T, topo, core, relay, call[1], call[1], call[3])
        done[k] = (s, count[s], dict(kn))
    for s, v in sorted(count.items()):
        e = "y" if s[0] == "s" else "g"
        queue[e].wait_ge(T.sem[s], v)
